import numpy as np
import ml_dtypes


def mxq(x, axis, fmt="e4m3"):
    dtype, down = {"e4m3": (ml_dtypes.float8_e4m3fn, 7), "e5m2": (ml_dtypes.float8_e5m2, 14)}[fmt]
    v = np.moveaxis(np.asarray(x, np.float32).astype(ml_dtypes.bfloat16).astype(np.float64), axis, -1)
    blocks = v.reshape(v.shape[:-1] + (-1, 32))
    amax = np.abs(blocks).max(-1, keepdims=True)
    byte = np.maximum(np.where(amax > 0, np.frexp(amax)[1] - 1 + 127, 0) - down, 1)
    scale = np.exp2(byte - 127.0)
    codes = (blocks / scale).astype(np.float32).astype(dtype).astype(np.float64)
    return np.moveaxis((codes * scale).reshape(v.shape), -1, axis)


WIDE = False


def mx_kscale(k):
    if not WIDE:
        return np.ones(k)
    levels = np.array([10, -10, 5, -5, 0])
    if k % 512:
        return np.exp2(np.random.permutation(np.resize(levels, k // 32))).repeat(32)
    a = np.empty((k // 512, 16))
    for p in range(k // 512):
        a[p, :8] = np.random.permutation(np.resize(levels, 8))
        for g in range(8):
            far = levels[np.abs(levels - a[p, g]) >= 10]
            a[p, g + 8] = far[np.random.randint(len(far))]
    return np.exp2(a.ravel()).repeat(32)


def f64(x):
    return np.asarray(x).astype(np.float64)


def striped(idx):
    return np.tile(idx.reshape(-1, 16).T, (8, 1)).astype(np.uint16)


def unstriped(offs):
    return offs[:16].T.reshape(-1).astype(np.int64)


E2M1 = np.array([0.0, 0.5, 1.0, 1.5, 2.0, 3.0, 4.0, 6.0, -0.0, -0.5, -1.0, -1.5, -2.0, -3.0, -4.0, -6.0])


def pack_weight(w, fmt):
    k, n = w.shape
    w = f64(np.asarray(w, np.float32).astype(ml_dtypes.bfloat16)).reshape(k // 32, 32, n)
    amax = np.abs(w).max(1)
    if fmt == "e4m3":
        byte = np.frexp(amax)[1] - 1 + 127 - 7
    else:
        mant, ex = np.frexp(amax / 6.0)
        byte = np.where(mant > 0.5, ex, ex - 1) + 127
    byte = np.clip(np.where(amax > 0, byte, 1), 1, 254)
    scaled = (w * np.exp2(127.0 - byte)[:, None, :]).reshape(k, n).astype(np.float32)
    by_word = np.ascontiguousarray(scaled.reshape(k // 512, 128, 4, n).transpose(0, 1, 3, 2))
    if fmt == "e4m3":
        words = by_word.astype(ml_dtypes.float8_e4m3fn).view(np.uint8)
    else:
        c = by_word.astype(ml_dtypes.float4_e2m1fn).view(np.uint8) & 0xF
        words = (c[..., 0::2] | (c[..., 1::2] << 4)).reshape(k // 512, 128, 2 * n)
    return np.ascontiguousarray(words), np.ascontiguousarray(byte.astype(np.uint8).reshape(k // 512, 16, n))


def unpack_weight(words, scales, fmt):
    g, _, n = scales.shape
    words = np.ascontiguousarray(words).reshape(g, 128, n, -1)
    if fmt == "e4m3":
        vals = words.view(ml_dtypes.float8_e4m3fn).astype(np.float64)
    else:
        nib = np.empty((g, 128, n, 4), np.uint8)
        nib[..., 0::2] = words & 0xF
        nib[..., 1::2] = words >> 4
        vals = E2M1[nib]
    vals = vals * np.repeat(np.exp2(scales.astype(np.float64) - 127.0), 8, axis=1)[..., None]
    return vals.transpose(0, 1, 3, 2).reshape(g * 512, n)


def gelu(v):
    return 0.5 * v * (1.0 + np.tanh(np.sqrt(2.0 / np.pi) * (v + 0.044715 * v**3)))


def bf(x):
    return np.asarray(x, np.float32).astype(ml_dtypes.bfloat16)


def planes(Y):
    n, m = Y.shape
    b = f64(bf(Y)).reshape(n // 32, 32, m)
    amax = np.abs(b).max(1)
    byte = np.clip(np.where(amax > 0, np.frexp(amax)[1] - 1 + 127 - 7, 1), 1, 254)
    codes = (b * np.exp2(127.0 - byte)[:, None, :]).reshape(n, m).astype(np.float32).astype(ml_dtypes.float8_e4m3fn).view(np.uint8)
    words = codes.reshape(n // 512, 128, 4, m).transpose(0, 1, 3, 2)
    return np.ascontiguousarray(words), np.ascontiguousarray(byte.astype(np.uint8).reshape(n // 512, 16, m))


K, H, N, T, S = 1024, 512, 384, 4096, 1024

def setup_inputs():
    n = np.random.standard_normal
    s = mx_kscale(K)[:, None]
    u = mx_kscale(H)[:, None]
    tab_words, tab_scales = pack_weight(n((K, T)) * s, "e4m3")
    wa_words, wa_scales = pack_weight(n((K, H)) / np.sqrt(K) / s, "e2m1")
    wx_words, wx_scales = pack_weight(n((K, N)) / np.sqrt(K) / s, "e4m3")
    return {
        "tab_words": tab_words, "tab_scales": tab_scales,
        "offs": striped(np.random.permutation(T)[:S]),
        "wa_words": wa_words, "wa_scales": wa_scales,
        "wb": (0.35 * n((K, H)) / np.sqrt(K) / s).astype(np.float32),
        "gain": (np.exp(0.3 * n(H)) * u[:, 0]).astype(np.float32),
        "wh": (1.5 * n((H, N)) / np.sqrt(H) / u).astype(np.float32),
        "wx_words": wx_words, "wx_scales": wx_scales,
        "conf": np.random.uniform(0.1, 0.9, (N, S)).astype(np.float32),
    }

def reference(tab_words, tab_scales, offs, wa_words, wa_scales, wb, gain, wh,
              wx_words, wx_scales, conf):
    v = unpack_weight(tab_words, tab_scales, "e4m3")[:, unstriped(offs)]
    wa = unpack_weight(wa_words, wa_scales, "e2m1")
    wx = unpack_weight(wx_words, wx_scales, "e4m3")
    qb = mxq(f64(wb), 0, "e4m3")
    qh = mxq(f64(wh), 0, "e4m3")
    a = np.tanh(wa.T @ v)
    b = np.exp(qb.T @ v)
    h = a * b * f64(gain)[:, None]
    words, scales = planes(h)
    hq = mxq(h, 0, "e4m3")
    e = wx.T @ v
    both = qh.T @ hq + wx.T @ v
    y = f64(conf) * both - e
    return y, h, words, scales

@@ -1,0 +1,280 @@
+from contextlib import ExitStack
+
+import concourse.mybir as mybir
+
+K, H, N, T, S = 1024, 512, 384, 4096, 1024
+FLOPS = 2 * S * (2 * K * H + 2 * K * N + H * N)
+
+F32 = mybir.dt.float32
+BF16 = mybir.dt.bfloat16
+I32 = mybir.dt.int32
+U32 = mybir.dt.uint32
+U16 = mybir.dt.uint16
+U8 = mybir.dt.uint8
+FP8X4 = mybir.dt.float8_e4m3fn_x4
+FP4X4 = mybir.dt.float4_e2m1fn_x4
+ACT = mybir.ActivationFunctionType
+ALU = mybir.AluOpType
+
+P = 128
+PACK = 4
+PASSES = K // (P * PACK)
+COLS = 512
+HALVES = S // COLS
+N_TILES = N // P
+QUADS = 4
+
+
+def tile_list_uwb_range_correction_kernel(
+    tc, tab_words, tab_scales, offs, wa_words, wa_scales, wb, gain, wh, wx_words, wx_scales, conf,
+    out_0, out_1, out_2, out_3,
+):
+    nc = tc.nc
+    with ExitStack() as ctx:
+        keep = ctx.enter_context(tc.tile_pool(name="keep", bufs=1))
+        psum = ctx.enter_context(tc.psum_pool(name="psum", bufs=1))
+
+        def sbuf(name, shape, dtype):
+            return keep.tile(shape, dtype, name=name, align_bytes=64)
+
+        def bank(i):
+            return psum.tile([P, COLS], F32, name="bank%d" % i)
+
+        offsets = keep.tile([P, S // 16], U16, name="offsets")
+        nc.sync.dma_start(offsets[:], offs)
+
+        tab_s = sbuf("tab_s", [P, T], U8)
+        wa_s_raw = sbuf("wa_s_raw", [P, PASSES, H], U8)
+        v_s1 = sbuf("v_s1", [P, S], U8)
+        wx_s = sbuf("wx_s", [P, PASSES, N], U8)
+        warm = sbuf("warm", [P, 8], F32)
+        nc.vector.memset(tab_s[:].bitcast(I32), 0)
+        nc.vector.memset(wa_s_raw[:].bitcast(I32), 0)
+        nc.vector.memset(warm[:], 0.0)
+        nc.vector.memset(v_s1[:].bitcast(I32), 0)
+        nc.vector.memset(wx_s[:].bitcast(I32), 0)
+
+        for q in range(QUADS):
+            nc.gpsimd.dma_start(
+                out=tab_s[32 * q : 32 * q + 8, :].bitcast(I32),
+                in_=tab_scales[:, 4 * q : 4 * q + 4, :].bitcast(I32),
+            )
+        wa_raw = sbuf("wa_raw", [P, PASSES, 2 * H], U8)
+        nc.sync.dma_start(out=wa_raw[:].bitcast(I32), in_=wa_words.rearrange("a p c -> p a c").bitcast(I32))
+        tab_w = []
+        for a in range(PASSES):
+            words = sbuf("tab_w%d" % a, [P, T], I32)
+            nc.sync.dma_start(out=words[:], in_=tab_words[a].rearrange("p t i -> p (t i)").bitcast(I32))
+            tab_w.append(words)
+        for q in range(QUADS):
+            nc.scalar.dma_start(
+                out=wa_s_raw[32 * q : 32 * q + 4, :, :].bitcast(I32),
+                in_=wa_scales[:, 4 * q : 4 * q + 4, :].rearrange("a r c -> r a c").bitcast(I32),
+            )
+        warm_out = sbuf("warm_out", [P, 8], F32)
+        nc.scalar.activation(out=warm_out[:], in_=warm[:], func=ACT.Exp)
+        wb_raw = []
+        for a in range(PASSES):
+            rows = sbuf("wb_raw%d" % a, [P, PACK, H], F32)
+            nc.sync.dma_start(out=rows[:], in_=wb[512 * a : 512 * (a + 1), :].rearrange("(p j) c -> p j c", j=PACK))
+            wb_raw.append(rows)
+        wh_raw = sbuf("wh_raw", [P, PACK, N], F32)
+        nc.sync.dma_start(out=wh_raw[:], in_=wh.rearrange("(p j) c -> p j c", j=PACK))
+        wx_w = sbuf("wx_w", [P, PASSES, N], I32)
+        nc.sync.dma_start(out=wx_w[:], in_=wx_words.rearrange("a p c i -> p a (c i)").bitcast(I32))
+        conf_sb = []
+        for h in range(HALVES):
+            rows = sbuf("conf%d" % h, [P, N_TILES, COLS], F32)
+            nc.sync.dma_start(
+                out=rows[:], in_=conf[:, h * COLS : (h + 1) * COLS].rearrange("(n p) j -> p n j", p=P)
+            )
+            conf_sb.append(rows)
+        gain_sb = sbuf("gain_sb", [P, PACK], F32)
+        nc.gpsimd.dma_start(out=gain_sb[:], in_=gain.rearrange("(p t) -> p t", t=PACK))
+
+        wa_w = sbuf("wa_w", [P, PASSES, 2 * H], U8)
+        wa_s = sbuf("wa_s", [P, PASSES, H], U8)
+        nc.vector.tensor_copy(
+            out=wa_w[:].rearrange("p a (t m b) -> p a t m b", t=PACK, b=2),
+            in_=wa_raw[:].rearrange("p a (m t b) -> p a t m b", t=PACK, b=2),
+        )
+
+        v_s0 = sbuf("v_s0", [P, S], U8)
+        nc.vector.tensor_copy(out=v_s0[:], in_=tab_s[:].indirect(offsets[:]))
+        nc.gpsimd.dma_start(out=v_s1[0:112, :].bitcast(I32), in_=v_s0[4:116, :].bitcast(I32))
+        v_s = [v_s0, v_s1]
+        for q in range(QUADS):
+            nc.gpsimd.dma_start(
+                out=wx_s[32 * q : 32 * q + 4, :, :].bitcast(I32),
+                in_=wx_scales[:, 4 * q : 4 * q + 4, :].rearrange("a r c -> r a c").bitcast(I32),
+            )
+        nc.vector.tensor_copy(
+            out=wa_s[:].rearrange("p a (t m) -> p a t m", t=PACK),
+            in_=wa_s_raw[:].rearrange("p a (m t) -> p a t m", t=PACK),
+        )
+        v_w = {}
+        for a in range(PASSES):
+            for h in range(HALVES):
+                picked = sbuf("v_w%d%d" % (a, h), [P, COLS], U32)
+                nc.vector.tensor_copy(
+                    out=picked[:],
+                    in_=tab_w[a][:].bitcast(U32).indirect(offsets[:, h * COLS // 16 : (h + 1) * COLS // 16]),
+                )
+                v_w[a, h] = picked
+
+        def times_v(acc, words, scales, a, h, start, stop):
+            nc.tensor.matmul_mx(
+                out=acc[:], lhsT=words, lhsT_scale=scales,
+                rhs=v_w[a, h][:].bitcast(FP8X4), rhs_scale=v_s[a][:, h * COLS : (h + 1) * COLS],
+                start=start, stop=stop,
+            )
+
+        def wa_pass(acc, t, a, h):
+            times_v(acc, wa_w[:, a, 2 * P * t : 2 * P * (t + 1)].bitcast(FP4X4), wa_s[:, a, P * t : P * (t + 1)],
+                    a, h, a == 0, a == PASSES - 1)
+
+        def wx_passes(acc, n, h, stop):
+            for a in range(PASSES):
+                times_v(acc, wx_w[:, a, P * n : P * (n + 1)].bitcast(FP8X4), wx_s[:, a, P * n : P * (n + 1)],
+                        a, h, a == 0, stop and a == PASSES - 1)
+
+        a_acc = {}
+        for h in range(HALVES):
+            for t in range(PACK):
+                a_acc[h, t] = bank(PACK * h + t)
+                wa_pass(a_acc[h, t], t, 0, h)
+        tanh_a = [sbuf("tanh_a%d" % h, [P, PACK, COLS], F32) for h in range(HALVES)]
+        for h in range(HALVES):
+            for t in range(PACK):
+                wa_pass(a_acc[h, t], t, 1, h)
+                nc.scalar.activation(out=tanh_a[h][:, t, :], in_=a_acc[h, t][:], func=ACT.Tanh)
+
+        wb_w, wb_s = [], []
+        for a in range(PASSES):
+            grouped = sbuf("wb_g%d" % a, [P, PACK * H], BF16)
+            nc.vector.tensor_copy(
+                out=grouped[:].rearrange("p (t m j) -> p m j t", t=PACK, j=PACK),
+                in_=wb_raw[a][:].rearrange("p j (m t) -> p m j t", t=PACK),
+            )
+            codes = sbuf("wb_w%d" % a, [P, H], U32)
+            scales = sbuf("wb_s%d" % a, [P, H], U8)
+            nc.vector.quantize_mx(out=codes[:].bitcast(FP8X4), scales=scales[:], in_=grouped[:])
+            wb_w.append(codes)
+            wb_s.append(scales)
+
+        e_banks = [[0, 1, 2], [4, 5, 0]]
+        both_banks = [[6, 7, 3], [6, 1, 7]]
+        b_banks = [[3, 4, 5, 6], [7, 3, 4, 5]]
+        e_acc, both_acc = {}, {}
+        for n in range(N_TILES):
+            e_acc[0, n] = bank(e_banks[0][n])
+            wx_passes(e_acc[0, n], n, 0, True)
+
+        exp_b = [sbuf("exp_b%d" % h, [P, PACK, COLS], F32) for h in range(HALVES)]
+        h_sb = [sbuf("h_sb%d" % h, [P, PACK, COLS], F32) for h in range(HALVES)]
+        h_g = [sbuf("h_g%d" % h, [P, PACK * COLS], BF16) for h in range(HALVES)]
+        h_w = [sbuf("h_w%d" % h, [P, COLS], U32) for h in range(HALVES)]
+        h_s = sbuf("h_s", [P, S], U8)
+        h_rows = out_1.rearrange("(p t) j -> p t j", t=PACK)
+
+        def exp_stage(h):
+            for t in range(PACK):
+                acc = bank(b_banks[h][t])
+                for a in range(PASSES):
+                    times_v(acc, wb_w[a][:, P * t : P * (t + 1)].bitcast(FP8X4), wb_s[a][:, P * t : P * (t + 1)],
+                            a, h, a == 0, a == PASSES - 1)
+                nc.scalar.activation(out=exp_b[h][:, t, :], in_=acc[:], func=ACT.Exp)
+
+        def code_stage(h):
+            for t in range(PACK):
+                nc.vector.scalar_tensor_tensor(
+                    out=h_sb[h][:, t, :], in0=tanh_a[h][:, t, :], scalar=gain_sb[:, t : t + 1],
+                    in1=exp_b[h][:, t, :], op0=ALU.mult, op1=ALU.mult,
+                )
+            nc.sync.dma_start(out=h_rows[:, :, h * COLS : (h + 1) * COLS], in_=h_sb[h][:])
+
+        def interleave(copy, dst, src):
+            copy(
+                out=dst.rearrange("p (c i t) -> p c t i", i=4, t=PACK),
+                in_=src.rearrange("p t (c i) -> p c t i", i=4),
+            )
+
+        def quantize_h(h):
+            nc.vector.quantize_mx(
+                out=h_w[h][:].bitcast(FP8X4), scales=h_s[:, h * COLS : (h + 1) * COLS], in_=h_g[h][:]
+            )
+            nc.sync.dma_start(
+                out=out_2[0, :, h * COLS : (h + 1) * COLS, :].rearrange("p m t -> p (m t)").bitcast(I32),
+                in_=h_w[h][:].bitcast(I32),
+            )
+
+        wh_g = sbuf("wh_g", [P, PACK * N], BF16)
+        wh_w = sbuf("wh_w", [P, N], U32)
+        wh_s = sbuf("wh_s", [P, N], U8)
+
+        def open_both(h, n):
+            both_acc[h, n] = bank(both_banks[h][n])
+            wx_passes(both_acc[h, n], n, h, False)
+
+        def close_both(h, n):
+            nc.tensor.matmul_mx(
+                out=both_acc[h, n][:], lhsT=wh_w[:, P * n : P * (n + 1)].bitcast(FP8X4),
+                lhsT_scale=wh_s[:, P * n : P * (n + 1)],
+                rhs=h_w[h][:].bitcast(FP8X4), rhs_scale=h_s[:, h * COLS : (h + 1) * COLS],
+                start=False, stop=True,
+            )
+
+        weighted = {}
+
+        def weigh(h, n):
+            weighted[h, n] = sbuf("weighted%d%d" % (h, n), [P, COLS], F32)
+            nc.vector.tensor_tensor(out=weighted[h, n][:], in0=both_acc[h, n][:], in1=conf_sb[h][:, n, :], op=ALU.mult)
+
+        def finish(h, n):
+            y = sbuf("y%d%d" % (h, n), [P, COLS], F32)
+            nc.vector.tensor_tensor(out=y[:], in0=weighted[h, n][:], in1=e_acc[h, n][:], op=ALU.subtract)
+            nc.sync.dma_start(out=out_0[P * n : P * (n + 1), h * COLS : (h + 1) * COLS], in_=y[:])
+
+        def open_e(h, n):
+            e_acc[h, n] = bank(e_banks[h][n])
+            wx_passes(e_acc[h, n], n, h, True)
+
+        exp_stage(0)
+        code_stage(0)
+        interleave(nc.scalar.copy, wh_g[:], wh_raw[:])
+        interleave(nc.vector.tensor_copy, h_g[0][:], h_sb[0][:])
+        exp_stage(1)
+        nc.vector.quantize_mx(out=wh_w[:, 0:256].bitcast(FP8X4), scales=wh_s[:, 0:256], in_=wh_g[:, 0:1024])
+        quantize_h(0)
+        nc.vector.quantize_mx(out=wh_w[:, 256:N].bitcast(FP8X4), scales=wh_s[:, 256:N], in_=wh_g[:, 1024 : PACK * N])
+        for n in range(N_TILES):
+            open_both(0, n)
+        for n in range(N_TILES):
+            close_both(0, n)
+        open_e(1, 0)
+        open_e(1, 1)
+        code_stage(1)
+        interleave(nc.scalar.copy, h_g[1][:], h_sb[1][:])
+        weigh(0, 0)
+        weigh(0, 1)
+        finish(0, 0)
+        open_both(1, 0)
+        open_e(1, 2)
+        weigh(0, 2)
+        finish(0, 1)
+        open_both(1, 1)
+        open_both(1, 2)
+        quantize_h(1)
+        for n in range(N_TILES):
+            close_both(1, n)
+        finish(0, 2)
+        for q in range(QUADS):
+            nc.scalar.dma_start(
+                out=out_3[0, 4 * q : 4 * q + 4, :].bitcast(I32), in_=h_s[32 * q : 32 * q + 4, :].bitcast(I32)
+            )
+        weigh(1, 0)
+        weigh(1, 1)
+        finish(1, 0)
+        weigh(1, 2)
+        finish(1, 1)
+        finish(1, 2)

@@ -34,8 +34,8 @@ def tile_list_uwb_range_correction_kernel(
         keep = ctx.enter_context(tc.tile_pool(name="keep", bufs=1))
         psum = ctx.enter_context(tc.psum_pool(name="psum", bufs=1))
 
-        def sbuf(name, shape, dtype):
-            return keep.tile(shape, dtype, name=name, align_bytes=64)
+        def sbuf(name, shape, dtype, slot=None):
+            return keep.tile(shape, dtype, name=name, tag=slot or name, align_bytes=64)
 
         def bank(i):
             return psum.tile([P, COLS], F32, name="bank%d" % i)
@@ -45,27 +45,31 @@ def tile_list_uwb_range_correction_kernel(
 
         tab_s = sbuf("tab_s", [P, T], U8)
         wa_s_raw = sbuf("wa_s_raw", [P, PASSES, H], U8)
-        v_s1 = sbuf("v_s1", [P, S], U8)
+        v_s = sbuf("v_s", [P, PASSES, S], U8)
         wx_s = sbuf("wx_s", [P, PASSES, N], U8)
         warm = sbuf("warm", [P, 8], F32)
-        nc.vector.memset(tab_s[:].bitcast(I32), 0)
         nc.vector.memset(wa_s_raw[:].bitcast(I32), 0)
-        nc.vector.memset(warm[:], 0.0)
-        nc.vector.memset(v_s1[:].bitcast(I32), 0)
-        nc.vector.memset(wx_s[:].bitcast(I32), 0)
+        for q in range(QUADS):
+            engine = nc.vector if q % 2 == 0 else nc.gpsimd
+            engine.memset(tab_s[32 * q : 32 * q + 24, :].bitcast(I32), 0)
+        nc.gpsimd.memset(v_s[96:128, :, :].bitcast(I32), 0)
+        nc.gpsimd.memset(warm[:], 0.0)
+        nc.gpsimd.memset(wx_s[:].bitcast(I32), 0)
 
         for q in range(QUADS):
-            nc.gpsimd.dma_start(
-                out=tab_s[32 * q : 32 * q + 8, :].bitcast(I32),
+            nc.sync.dma_start(
+                out=tab_s[32 * q + 24 : 32 * q + 32, :].bitcast(I32),
                 in_=tab_scales[:, 4 * q : 4 * q + 4, :].bitcast(I32),
             )
         wa_raw = sbuf("wa_raw", [P, PASSES, 2 * H], U8)
         nc.sync.dma_start(out=wa_raw[:].bitcast(I32), in_=wa_words.rearrange("a p c -> p a c").bitcast(I32))
-        tab_w = []
-        for a in range(PASSES):
+
+        def load_table(a):
             words = sbuf("tab_w%d" % a, [P, T], I32)
             nc.sync.dma_start(out=words[:], in_=tab_words[a].rearrange("p t i -> p (t i)").bitcast(I32))
-            tab_w.append(words)
+            return words
+
+        tab_w = [load_table(a) for a in range(PASSES)]
         for q in range(QUADS):
             nc.scalar.dma_start(
                 out=wa_s_raw[32 * q : 32 * q + 4, :, :].bitcast(I32),
@@ -73,47 +77,30 @@ def tile_list_uwb_range_correction_kernel(
             )
         warm_out = sbuf("warm_out", [P, 8], F32)
         nc.scalar.activation(out=warm_out[:], in_=warm[:], func=ACT.Exp)
-        wb_raw = []
-        for a in range(PASSES):
-            rows = sbuf("wb_raw%d" % a, [P, PACK, H], F32)
-            nc.sync.dma_start(out=rows[:], in_=wb[512 * a : 512 * (a + 1), :].rearrange("(p j) c -> p j c", j=PACK))
-            wb_raw.append(rows)
-        wh_raw = sbuf("wh_raw", [P, PACK, N], F32)
-        nc.sync.dma_start(out=wh_raw[:], in_=wh.rearrange("(p j) c -> p j c", j=PACK))
-        wx_w = sbuf("wx_w", [P, PASSES, N], I32)
-        nc.sync.dma_start(out=wx_w[:], in_=wx_words.rearrange("a p c i -> p a (c i)").bitcast(I32))
-        conf_sb = []
-        for h in range(HALVES):
-            rows = sbuf("conf%d" % h, [P, N_TILES, COLS], F32)
-            nc.sync.dma_start(
-                out=rows[:], in_=conf[:, h * COLS : (h + 1) * COLS].rearrange("(n p) j -> p n j", p=P)
-            )
-            conf_sb.append(rows)
         gain_sb = sbuf("gain_sb", [P, PACK], F32)
         nc.gpsimd.dma_start(out=gain_sb[:], in_=gain.rearrange("(p t) -> p t", t=PACK))
-
-        wa_w = sbuf("wa_w", [P, PASSES, 2 * H], U8)
-        wa_s = sbuf("wa_s", [P, PASSES, H], U8)
-        nc.vector.tensor_copy(
-            out=wa_w[:].rearrange("p a (t m b) -> p a t m b", t=PACK, b=2),
-            in_=wa_raw[:].rearrange("p a (m t b) -> p a t m b", t=PACK, b=2),
-        )
-
-        v_s0 = sbuf("v_s0", [P, S], U8)
-        nc.vector.tensor_copy(out=v_s0[:], in_=tab_s[:].indirect(offsets[:]))
-        nc.gpsimd.dma_start(out=v_s1[0:112, :].bitcast(I32), in_=v_s0[4:116, :].bitcast(I32))
-        v_s = [v_s0, v_s1]
         for q in range(QUADS):
             nc.gpsimd.dma_start(
                 out=wx_s[32 * q : 32 * q + 4, :, :].bitcast(I32),
                 in_=wx_scales[:, 4 * q : 4 * q + 4, :].rearrange("a r c -> r a c").bitcast(I32),
             )
+
+        picked_s = sbuf("picked_s", [P, S], U8)
+        nc.vector.tensor_copy(out=picked_s[:], in_=tab_s[:].indirect(offsets[:]))
+        for a in range(PASSES):
+            nc.scalar.dma_start(
+                out=v_s[0:100, a, :].bitcast(I32), in_=picked_s[24 + 4 * a : 124 + 4 * a, :].bitcast(I32)
+            )
+
+        wa_w = sbuf("wa_w", [P, PASSES, 2 * H], U8)
+        wa_s = sbuf("wa_s", [P, PASSES, H], U8)
         nc.vector.tensor_copy(
-            out=wa_s[:].rearrange("p a (t m) -> p a t m", t=PACK),
-            in_=wa_s_raw[:].rearrange("p a (m t) -> p a t m", t=PACK),
+            out=wa_w[:].bitcast(U16).rearrange("p a (t m) -> p a t m", t=PACK),
+            in_=wa_raw[:].bitcast(U16).rearrange("p a (m t) -> p a t m", t=PACK),
         )
         v_w = {}
-        for a in range(PASSES):
+
+        def gather_words(a):
             for h in range(HALVES):
                 picked = sbuf("v_w%d%d" % (a, h), [P, COLS], U32)
                 nc.vector.tensor_copy(
@@ -122,10 +109,26 @@ def tile_list_uwb_range_correction_kernel(
                 )
                 v_w[a, h] = picked
 
+        def load_wb(a, slot):
+            rows = sbuf("wb_raw%d" % a, [P, PACK, H], F32, slot=slot)
+            nc.sync.dma_start(out=rows[:], in_=wb[512 * a : 512 * (a + 1), :].rearrange("(p j) c -> p j c", j=PACK))
+            return rows
+
+        wb_raw = [load_wb(0, "picked_s")]
+        gather_words(0)
+        wb_raw.append(load_wb(1, "tab_w0"))
+        nc.vector.tensor_copy(
+            out=wa_s[:].rearrange("p a (t m) -> p a t m", t=PACK),
+            in_=wa_s_raw[:].rearrange("p a (m t) -> p a t m", t=PACK),
+        )
+        gather_words(1)
+        wh_raw = sbuf("wh_raw", [P, PACK, N], F32, slot="tab_w1")
+        nc.sync.dma_start(out=wh_raw[:], in_=wh.rearrange("(p j) c -> p j c", j=PACK))
+
         def times_v(acc, words, scales, a, h, start, stop):
             nc.tensor.matmul_mx(
                 out=acc[:], lhsT=words, lhsT_scale=scales,
-                rhs=v_w[a, h][:].bitcast(FP8X4), rhs_scale=v_s[a][:, h * COLS : (h + 1) * COLS],
+                rhs=v_w[a, h][:].bitcast(FP8X4), rhs_scale=v_s[:, a, h * COLS : (h + 1) * COLS],
                 start=start, stop=stop,
             )
 
@@ -149,12 +152,12 @@ def tile_list_uwb_range_correction_kernel(
                 wa_pass(a_acc[h, t], t, 1, h)
                 nc.scalar.activation(out=tanh_a[h][:, t, :], in_=a_acc[h, t][:], func=ACT.Tanh)
 
-        wb_w, wb_s = [], []
+        wb_w, wb_s, conf_sb = [], [], []
         for a in range(PASSES):
             grouped = sbuf("wb_g%d" % a, [P, PACK * H], BF16)
             nc.vector.tensor_copy(
-                out=grouped[:].rearrange("p (t m j) -> p m j t", t=PACK, j=PACK),
-                in_=wb_raw[a][:].rearrange("p j (m t) -> p m j t", t=PACK),
+                out=grouped[:].rearrange("p (t m j) -> p m t j", t=PACK, j=PACK),
+                in_=wb_raw[a][:].rearrange("p j (m t) -> p m t j", t=PACK),
             )
             codes = sbuf("wb_w%d" % a, [P, H], U32)
             scales = sbuf("wb_s%d" % a, [P, H], U8)
@@ -162,6 +165,17 @@ def tile_list_uwb_range_correction_kernel(
             wb_w.append(codes)
             wb_s.append(scales)
 
+        wx_w = sbuf("wx_w", [P, PASSES, N], I32, slot="picked_s")
+        nc.sync.dma_start(out=wx_w[:], in_=wx_words.rearrange("a p c i -> p a (c i)").bitcast(I32))
+
+        def load_conf(h, slot):
+            rows = sbuf("conf%d" % h, [P, N_TILES, COLS], F32, slot=slot)
+            nc.sync.dma_start(
+                out=rows[:], in_=conf[:, h * COLS : (h + 1) * COLS].rearrange("(n p) j -> p n j", p=P)
+            )
+            conf_sb.append(rows)
+
+        load_conf(0, "tab_w0")
         e_banks = [[0, 1, 2], [4, 5, 0]]
         both_banks = [[6, 7, 3], [6, 1, 7]]
         b_banks = [[3, 4, 5, 6], [7, 3, 4, 5]]
@@ -242,6 +256,7 @@ def tile_list_uwb_range_correction_kernel(
         exp_stage(0)
         code_stage(0)
         interleave(nc.scalar.copy, wh_g[:], wh_raw[:])
+        load_conf(1, "tab_w1")
         interleave(nc.vector.tensor_copy, h_g[0][:], h_sb[0][:])
         exp_stage(1)
         nc.vector.quantize_mx(out=wh_w[:, 0:256].bitcast(FP8X4), scales=wh_s[:, 0:256], in_=wh_g[:, 0:1024])

@@ -23,6 +23,7 @@ COLS = 512
 HALVES = S // COLS
 N_TILES = N // P
 QUADS = 4
+WB_SPLIT = 384
 
 
 def tile_list_uwb_range_correction_kernel(
@@ -50,8 +51,7 @@ def tile_list_uwb_range_correction_kernel(
         warm = sbuf("warm", [P, 8], F32)
         nc.vector.memset(wa_s_raw[:].bitcast(I32), 0)
         for q in range(QUADS):
-            engine = nc.vector if q % 2 == 0 else nc.gpsimd
-            engine.memset(tab_s[32 * q : 32 * q + 24, :].bitcast(I32), 0)
+            nc.vector.memset(tab_s[32 * q : 32 * q + 24, :].bitcast(I32), 0)
         nc.gpsimd.memset(v_s[96:128, :, :].bitcast(I32), 0)
         nc.gpsimd.memset(warm[:], 0.0)
         nc.gpsimd.memset(wx_s[:].bitcast(I32), 0)
@@ -109,18 +109,20 @@ def tile_list_uwb_range_correction_kernel(
                 )
                 v_w[a, h] = picked
 
-        def load_wb(a, slot):
-            rows = sbuf("wb_raw%d" % a, [P, PACK, H], F32, slot=slot)
-            nc.sync.dma_start(out=rows[:], in_=wb[512 * a : 512 * (a + 1), :].rearrange("(p j) c -> p j c", j=PACK))
-            return rows
+        def load_wb(a, c0, c1, slot):
+            rows = sbuf("wb_raw%d_%d" % (a, c0), [P, PACK, c1 - c0], F32, slot=slot)
+            nc.sync.dma_start(
+                out=rows[:], in_=wb[512 * a : 512 * (a + 1), c0:c1].rearrange("(p j) c -> p j c", j=PACK)
+            )
+            return rows, c0, c1
 
-        wb_raw = [load_wb(0, "picked_s")]
+        wb_raw = [[load_wb(0, 0, H, "picked_s")]]
         gather_words(0)
-        wb_raw.append(load_wb(1, "tab_w0"))
         nc.vector.tensor_copy(
             out=wa_s[:].rearrange("p a (t m) -> p a t m", t=PACK),
             in_=wa_s_raw[:].rearrange("p a (m t) -> p a t m", t=PACK),
         )
+        wb_raw.append([load_wb(1, 0, WB_SPLIT, "tab_w0"), load_wb(1, WB_SPLIT, H, "wa_s_raw")])
         gather_words(1)
         wh_raw = sbuf("wh_raw", [P, PACK, N], F32, slot="tab_w1")
         nc.sync.dma_start(out=wh_raw[:], in_=wh.rearrange("(p j) c -> p j c", j=PACK))
@@ -155,13 +157,19 @@ def tile_list_uwb_range_correction_kernel(
         wb_w, wb_s, conf_sb = [], [], []
         for a in range(PASSES):
             grouped = sbuf("wb_g%d" % a, [P, PACK * H], BF16)
-            nc.vector.tensor_copy(
-                out=grouped[:].rearrange("p (t m j) -> p m t j", t=PACK, j=PACK),
-                in_=wb_raw[a][:].rearrange("p j (m t) -> p m t j", t=PACK),
-            )
+            for rows, c0, c1 in wb_raw[a]:
+                nc.vector.tensor_copy(
+                    out=grouped[:].rearrange("p (t m j) -> p m t j", t=PACK, j=PACK)[:, c0 // PACK : c1 // PACK, :, :],
+                    in_=rows[:].rearrange("p j (m t) -> p m t j", t=PACK),
+                )
             codes = sbuf("wb_w%d" % a, [P, H], U32)
             scales = sbuf("wb_s%d" % a, [P, H], U8)
-            nc.vector.quantize_mx(out=codes[:].bitcast(FP8X4), scales=scales[:], in_=grouped[:])
+            width = H if a == 0 else H // 2
+            for c0 in range(0, H, width):
+                nc.vector.quantize_mx(
+                    out=codes[:, c0 : c0 + width].bitcast(FP8X4), scales=scales[:, c0 : c0 + width],
+                    in_=grouped[:, PACK * c0 : PACK * (c0 + width)],
+                )
             wb_w.append(codes)
             wb_s.append(scales)
 
@@ -176,13 +184,21 @@ def tile_list_uwb_range_correction_kernel(
             conf_sb.append(rows)
 
         load_conf(0, "tab_w0")
-        e_banks = [[0, 1, 2], [4, 5, 0]]
-        both_banks = [[6, 7, 3], [6, 1, 7]]
+        load_conf(1, "wb_g1")
+        e_banks = [[0, 1, 2], [4, 0, 1]]
+        both_banks = [[6, 7, 3], [5, 6, 7]]
         b_banks = [[3, 4, 5, 6], [7, 3, 4, 5]]
-        e_acc, both_acc = {}, {}
-        for n in range(N_TILES):
-            e_acc[0, n] = bank(e_banks[0][n])
-            wx_passes(e_acc[0, n], n, 0, True)
+        e_acc, both_acc, b_acc = {}, {}, {}
+
+        def wb_pass(h, t, a):
+            if a == 0:
+                b_acc[h, t] = bank(b_banks[h][t])
+            times_v(b_acc[h, t], wb_w[a][:, P * t : P * (t + 1)].bitcast(FP8X4), wb_s[a][:, P * t : P * (t + 1)],
+                    a, h, a == 0, a == PASSES - 1)
+
+        early = [(0, 0), (0, 1), (0, 2), (0, 3), (1, 0)]
+        for h, t in early:
+            wb_pass(h, t, 0)
 
         exp_b = [sbuf("exp_b%d" % h, [P, PACK, COLS], F32) for h in range(HALVES)]
         h_sb = [sbuf("h_sb%d" % h, [P, PACK, COLS], F32) for h in range(HALVES)]
@@ -193,11 +209,10 @@ def tile_list_uwb_range_correction_kernel(
 
         def exp_stage(h):
             for t in range(PACK):
-                acc = bank(b_banks[h][t])
-                for a in range(PASSES):
-                    times_v(acc, wb_w[a][:, P * t : P * (t + 1)].bitcast(FP8X4), wb_s[a][:, P * t : P * (t + 1)],
-                            a, h, a == 0, a == PASSES - 1)
-                nc.scalar.activation(out=exp_b[h][:, t, :], in_=acc[:], func=ACT.Exp)
+                if (h, t) not in early:
+                    wb_pass(h, t, 0)
+                wb_pass(h, t, 1)
+                nc.scalar.activation(out=exp_b[h][:, t, :], in_=b_acc[h, t][:], func=ACT.Exp)
 
         def code_stage(h):
             for t in range(PACK):
@@ -222,7 +237,6 @@ def tile_list_uwb_range_correction_kernel(
                 in_=h_w[h][:].bitcast(I32),
             )
 
-        wh_g = sbuf("wh_g", [P, PACK * N], BF16)
         wh_w = sbuf("wh_w", [P, N], U32)
         wh_s = sbuf("wh_s", [P, N], U8)
 
@@ -244,52 +258,60 @@ def tile_list_uwb_range_correction_kernel(
             weighted[h, n] = sbuf("weighted%d%d" % (h, n), [P, COLS], F32)
             nc.vector.tensor_tensor(out=weighted[h, n][:], in0=both_acc[h, n][:], in1=conf_sb[h][:, n, :], op=ALU.mult)
 
-        def finish(h, n):
+        def finish(h, n, engine, e_values):
             y = sbuf("y%d%d" % (h, n), [P, COLS], F32)
-            nc.vector.tensor_tensor(out=y[:], in0=weighted[h, n][:], in1=e_acc[h, n][:], op=ALU.subtract)
+            engine.tensor_tensor(out=y[:], in0=weighted[h, n][:], in1=e_values, op=ALU.subtract)
             nc.sync.dma_start(out=out_0[P * n : P * (n + 1), h * COLS : (h + 1) * COLS], in_=y[:])
 
         def open_e(h, n):
             e_acc[h, n] = bank(e_banks[h][n])
             wx_passes(e_acc[h, n], n, h, True)
 
-        exp_stage(0)
-        code_stage(0)
-        interleave(nc.scalar.copy, wh_g[:], wh_raw[:])
-        load_conf(1, "tab_w1")
-        interleave(nc.vector.tensor_copy, h_g[0][:], h_sb[0][:])
-        exp_stage(1)
+        wh_g = sbuf("wh_g", [P, PACK * N], BF16)
+        interleave(nc.vector.tensor_copy, wh_g[:], wh_raw[:])
         nc.vector.quantize_mx(out=wh_w[:, 0:256].bitcast(FP8X4), scales=wh_s[:, 0:256], in_=wh_g[:, 0:1024])
-        quantize_h(0)
         nc.vector.quantize_mx(out=wh_w[:, 256:N].bitcast(FP8X4), scales=wh_s[:, 256:N], in_=wh_g[:, 1024 : PACK * N])
+        exp_stage(0)
+        exp_stage(1)
+        code_stage(0)
+        code_stage(1)
+        for n in range(N_TILES):
+            open_e(0, n)
+        interleave(nc.vector.tensor_copy, h_g[0][:], h_sb[0][:])
+        interleave(nc.scalar.copy, h_g[1][:], h_sb[1][:])
+        quantize_h(0)
         for n in range(N_TILES):
             open_both(0, n)
         for n in range(N_TILES):
             close_both(0, n)
-        open_e(1, 0)
-        open_e(1, 1)
-        code_stage(1)
-        interleave(nc.scalar.copy, h_g[1][:], h_sb[1][:])
-        weigh(0, 0)
-        weigh(0, 1)
-        finish(0, 0)
-        open_both(1, 0)
-        open_e(1, 2)
-        weigh(0, 2)
-        finish(0, 1)
-        open_both(1, 1)
-        open_both(1, 2)
-        quantize_h(1)
+        e_sb = {}
+
+        def copy_e(h, n, slot):
+            e_sb[h, n] = sbuf("e_sb%d%d" % (h, n), [P, COLS], F32, slot=slot)
+            nc.scalar.copy(out=e_sb[h, n][:], in_=e_acc[h, n][:])
+
         for n in range(N_TILES):
-            close_both(1, n)
-        finish(0, 2)
+            copy_e(0, n, ["wb_w1", "wb_s1", "wb_w0"][n])
+        open_e(1, 0)
+        open_both(1, 0)
+        copy_e(1, 0, None)
+        for n in range(N_TILES):
+            weigh(0, n)
+            finish(0, n, nc.gpsimd, e_sb[0, n][:])
+            if n == 1:
+                quantize_h(1)
         for q in range(QUADS):
-            nc.scalar.dma_start(
+            nc.sync.dma_start(
                 out=out_3[0, 4 * q : 4 * q + 4, :].bitcast(I32), in_=h_s[32 * q : 32 * q + 4, :].bitcast(I32)
             )
-        weigh(1, 0)
-        weigh(1, 1)
-        finish(1, 0)
-        weigh(1, 2)
-        finish(1, 1)
-        finish(1, 2)
+        close_both(1, 0)
+        for n in range(1, N_TILES):
+            open_both(1, n)
+            close_both(1, n)
+        for n in range(1, N_TILES):
+            open_e(1, n)
+        for n in range(N_TILES):
+            weigh(1, n)
+        finish(1, 0, nc.gpsimd, e_sb[1, 0][:])
+        for n in range(1, N_TILES):
+            finish(1, n, nc.vector, e_acc[1, n][:])

@@ -33,10 +33,14 @@ def tile_list_uwb_range_correction_kernel(
     nc = tc.nc
     with ExitStack() as ctx:
         keep = ctx.enter_context(tc.tile_pool(name="keep", bufs=1))
+        reuse = ctx.enter_context(tc.tile_pool(name="reuse", bufs=1))
         psum = ctx.enter_context(tc.psum_pool(name="psum", bufs=1))
 
         def sbuf(name, shape, dtype, slot=None):
             return keep.tile(shape, dtype, name=name, tag=slot or name, align_bytes=64)
+
+        def placed(name, shape, dtype, offset):
+            return reuse.tile(shape, dtype, name=name, offset=offset, align_bytes=64)
 
         def bank(i):
             return psum.tile([P, COLS], F32, name="bank%d" % i)
@@ -46,51 +50,46 @@ def tile_list_uwb_range_correction_kernel(
 
         tab_s = sbuf("tab_s", [P, T], U8)
         wa_s_raw = sbuf("wa_s_raw", [P, PASSES, H], U8)
-        v_s = sbuf("v_s", [P, PASSES, S], U8)
-        wx_s = sbuf("wx_s", [P, PASSES, N], U8)
+        v_s1 = sbuf("v_s1", [P, S], U8)
         warm = sbuf("warm", [P, 8], F32)
+        nc.vector.memset(tab_s[:].bitcast(I32), 0)
         nc.vector.memset(wa_s_raw[:].bitcast(I32), 0)
-        for q in range(QUADS):
-            nc.vector.memset(tab_s[32 * q : 32 * q + 24, :].bitcast(I32), 0)
-        nc.gpsimd.memset(v_s[96:128, :, :].bitcast(I32), 0)
-        nc.gpsimd.memset(warm[:], 0.0)
-        nc.gpsimd.memset(wx_s[:].bitcast(I32), 0)
+        nc.vector.memset(warm[:], 0.0)
+        nc.vector.memset(v_s1[96:128, :].bitcast(I32), 0)
 
-        for q in range(QUADS):
-            nc.sync.dma_start(
-                out=tab_s[32 * q + 24 : 32 * q + 32, :].bitcast(I32),
-                in_=tab_scales[:, 4 * q : 4 * q + 4, :].bitcast(I32),
-            )
         wa_raw = sbuf("wa_raw", [P, PASSES, 2 * H], U8)
         nc.sync.dma_start(out=wa_raw[:].bitcast(I32), in_=wa_words.rearrange("a p c -> p a c").bitcast(I32))
-
-        def load_table(a):
-            words = sbuf("tab_w%d" % a, [P, T], I32)
+        tab_w = []
+        for a in range(PASSES):
+            words = placed("tab_w%d" % a, [P, T], I32, 4 * T * a)
             nc.sync.dma_start(out=words[:], in_=tab_words[a].rearrange("p t i -> p (t i)").bitcast(I32))
-            return words
+            tab_w.append(words)
 
-        tab_w = [load_table(a) for a in range(PASSES)]
+        def load_wb(rows, a, c0, c1):
+            nc.sync.dma_start(
+                out=rows[:], in_=wb[512 * a : 512 * (a + 1), c0:c1].rearrange("(p j) c -> p j c", j=PACK)
+            )
+            return rows, c0, c1
+
+        wb_raw = [
+            [load_wb(sbuf("wb_raw0", [P, PACK, H], F32), 0, 0, H)],
+            [load_wb(sbuf("wb_raw1", [P, PACK, WB_SPLIT], F32), 1, 0, WB_SPLIT)],
+        ]
+
+        for q in range(QUADS):
+            nc.gpsimd.dma_start(
+                out=tab_s[32 * q : 32 * q + 8, :].bitcast(I32),
+                in_=tab_scales[:, 4 * q : 4 * q + 4, :].bitcast(I32),
+            )
         for q in range(QUADS):
             nc.scalar.dma_start(
                 out=wa_s_raw[32 * q : 32 * q + 4, :, :].bitcast(I32),
                 in_=wa_scales[:, 4 * q : 4 * q + 4, :].rearrange("a r c -> r a c").bitcast(I32),
             )
-        warm_out = sbuf("warm_out", [P, 8], F32)
-        nc.scalar.activation(out=warm_out[:], in_=warm[:], func=ACT.Exp)
         gain_sb = sbuf("gain_sb", [P, PACK], F32)
         nc.gpsimd.dma_start(out=gain_sb[:], in_=gain.rearrange("(p t) -> p t", t=PACK))
-        for q in range(QUADS):
-            nc.gpsimd.dma_start(
-                out=wx_s[32 * q : 32 * q + 4, :, :].bitcast(I32),
-                in_=wx_scales[:, 4 * q : 4 * q + 4, :].rearrange("a r c -> r a c").bitcast(I32),
-            )
-
-        picked_s = sbuf("picked_s", [P, S], U8)
-        nc.vector.tensor_copy(out=picked_s[:], in_=tab_s[:].indirect(offsets[:]))
-        for a in range(PASSES):
-            nc.scalar.dma_start(
-                out=v_s[0:100, a, :].bitcast(I32), in_=picked_s[24 + 4 * a : 124 + 4 * a, :].bitcast(I32)
-            )
+        warm_out = sbuf("warm_out", [P, 8], F32)
+        nc.scalar.activation(out=warm_out[:], in_=warm[:], func=ACT.Exp)
 
         wa_w = sbuf("wa_w", [P, PASSES, 2 * H], U8)
         wa_s = sbuf("wa_s", [P, PASSES, H], U8)
@@ -98,39 +97,48 @@ def tile_list_uwb_range_correction_kernel(
             out=wa_w[:].bitcast(U16).rearrange("p a (t m) -> p a t m", t=PACK),
             in_=wa_raw[:].bitcast(U16).rearrange("p a (m t) -> p a t m", t=PACK),
         )
+
+        picked_s = sbuf("picked_s", [P, S], U8)
+        nc.vector.tensor_copy(out=picked_s[:], in_=tab_s[:].indirect(offsets[:]))
+        nc.scalar.dma_start(out=v_s1[0:112, :].bitcast(I32), in_=picked_s[4:116, :].bitcast(I32))
+        v_s = [picked_s, v_s1]
         v_w = {}
 
-        def gather_words(a):
-            for h in range(HALVES):
-                picked = sbuf("v_w%d%d" % (a, h), [P, COLS], U32)
-                nc.vector.tensor_copy(
-                    out=picked[:],
-                    in_=tab_w[a][:].bitcast(U32).indirect(offsets[:, h * COLS // 16 : (h + 1) * COLS // 16]),
-                )
-                v_w[a, h] = picked
+        picked = sbuf("v_w0", [P, S], U32, slot="tab_s")
+        nc.vector.tensor_copy(out=picked[:], in_=tab_w[0][:].bitcast(U32).indirect(offsets[:]))
+        for h in range(HALVES):
+            v_w[0, h] = picked[:, h * COLS : (h + 1) * COLS]
 
-        def load_wb(a, c0, c1, slot):
-            rows = sbuf("wb_raw%d_%d" % (a, c0), [P, PACK, c1 - c0], F32, slot=slot)
-            nc.sync.dma_start(
-                out=rows[:], in_=wb[512 * a : 512 * (a + 1), c0:c1].rearrange("(p j) c -> p j c", j=PACK)
+        wb_raw[1].append(load_wb(placed("wb_last", [P, PACK, H - WB_SPLIT], F32, 0), 1, WB_SPLIT, H))
+        wx_w = placed("wx_w", [P, PASSES, N], I32, 2048)
+        nc.sync.dma_start(out=wx_w[:], in_=wx_words.rearrange("a p c i -> p a (c i)").bitcast(I32))
+        wh_raw = placed("wh_raw", [P, PACK, N], F32, 5120)
+        nc.sync.dma_start(out=wh_raw[:], in_=wh.rearrange("(p j) c -> p j c", j=PACK))
+        wx_s = placed("wx_s", [P, PASSES, N], U8, 11264)
+        nc.vector.memset(wx_s[:].bitcast(I32), 0)
+        for q in range(QUADS):
+            nc.scalar.dma_start(
+                out=wx_s[32 * q : 32 * q + 4, :, :].bitcast(I32),
+                in_=wx_scales[:, 4 * q : 4 * q + 4, :].rearrange("a r c -> r a c").bitcast(I32),
             )
-            return rows, c0, c1
-
-        wb_raw = [[load_wb(0, 0, H, "picked_s")]]
-        gather_words(0)
         nc.vector.tensor_copy(
             out=wa_s[:].rearrange("p a (t m) -> p a t m", t=PACK),
             in_=wa_s_raw[:].rearrange("p a (m t) -> p a t m", t=PACK),
         )
-        wb_raw.append([load_wb(1, 0, WB_SPLIT, "tab_w0"), load_wb(1, WB_SPLIT, H, "wa_s_raw")])
-        gather_words(1)
-        wh_raw = sbuf("wh_raw", [P, PACK, N], F32, slot="tab_w1")
-        nc.sync.dma_start(out=wh_raw[:], in_=wh.rearrange("(p j) c -> p j c", j=PACK))
+        for h in range(HALVES):
+            picked = sbuf("v_w1%d" % h, [P, COLS], U32, slot="wa_s_raw" if h == 0 else None)
+            nc.vector.tensor_copy(
+                out=picked[:],
+                in_=tab_w[1][:].bitcast(U32).indirect(offsets[:, h * COLS // 16 : (h + 1) * COLS // 16]),
+            )
+            v_w[1, h] = picked[:]
+        conf_sb = placed("conf_sb", [P, N_TILES, S], F32, 4 * T)
+        nc.sync.dma_start(out=conf_sb[:], in_=conf.rearrange("(n p) j -> p n j", p=P))
 
         def times_v(acc, words, scales, a, h, start, stop):
             nc.tensor.matmul_mx(
                 out=acc[:], lhsT=words, lhsT_scale=scales,
-                rhs=v_w[a, h][:].bitcast(FP8X4), rhs_scale=v_s[:, a, h * COLS : (h + 1) * COLS],
+                rhs=v_w[a, h].bitcast(FP8X4), rhs_scale=v_s[a][:, h * COLS : (h + 1) * COLS],
                 start=start, stop=stop,
             )
 
@@ -144,19 +152,21 @@ def tile_list_uwb_range_correction_kernel(
                         a, h, a == 0, stop and a == PASSES - 1)
 
         a_acc = {}
+        tanh_a = [sbuf("tanh_a%d" % h, [P, PACK, COLS], F32) for h in range(HALVES)]
         for h in range(HALVES):
             for t in range(PACK):
                 a_acc[h, t] = bank(PACK * h + t)
                 wa_pass(a_acc[h, t], t, 0, h)
-        tanh_a = [sbuf("tanh_a%d" % h, [P, PACK, COLS], F32) for h in range(HALVES)]
-        for h in range(HALVES):
             for t in range(PACK):
                 wa_pass(a_acc[h, t], t, 1, h)
                 nc.scalar.activation(out=tanh_a[h][:, t, :], in_=a_acc[h, t][:], func=ACT.Tanh)
 
-        wb_w, wb_s, conf_sb = [], [], []
+        wb_w, wb_s = [], []
         for a in range(PASSES):
-            grouped = sbuf("wb_g%d" % a, [P, PACK * H], BF16)
+            if a == 0:
+                grouped = placed("wb_g0", [P, PACK * H], BF16, 4 * T + 4 * N_TILES * S)
+            else:
+                grouped = sbuf("wb_g1", [P, PACK * H], BF16, slot="wb_raw0")
             for rows, c0, c1 in wb_raw[a]:
                 nc.vector.tensor_copy(
                     out=grouped[:].rearrange("p (t m j) -> p m t j", t=PACK, j=PACK)[:, c0 // PACK : c1 // PACK, :, :],
@@ -173,18 +183,6 @@ def tile_list_uwb_range_correction_kernel(
             wb_w.append(codes)
             wb_s.append(scales)
 
-        wx_w = sbuf("wx_w", [P, PASSES, N], I32, slot="picked_s")
-        nc.sync.dma_start(out=wx_w[:], in_=wx_words.rearrange("a p c i -> p a (c i)").bitcast(I32))
-
-        def load_conf(h, slot):
-            rows = sbuf("conf%d" % h, [P, N_TILES, COLS], F32, slot=slot)
-            nc.sync.dma_start(
-                out=rows[:], in_=conf[:, h * COLS : (h + 1) * COLS].rearrange("(n p) j -> p n j", p=P)
-            )
-            conf_sb.append(rows)
-
-        load_conf(0, "tab_w0")
-        load_conf(1, "wb_g1")
         e_banks = [[0, 1, 2], [4, 0, 1]]
         both_banks = [[6, 7, 3], [5, 6, 7]]
         b_banks = [[3, 4, 5, 6], [7, 3, 4, 5]]
@@ -256,7 +254,7 @@ def tile_list_uwb_range_correction_kernel(
 
         def weigh(h, n):
             weighted[h, n] = sbuf("weighted%d%d" % (h, n), [P, COLS], F32)
-            nc.vector.tensor_tensor(out=weighted[h, n][:], in0=both_acc[h, n][:], in1=conf_sb[h][:, n, :], op=ALU.mult)
+            nc.vector.tensor_tensor(out=weighted[h, n][:], in0=both_acc[h, n][:], in1=conf_sb[:, n, h * COLS : (h + 1) * COLS], op=ALU.mult)
 
         def finish(h, n, engine, e_values):
             y = sbuf("y%d%d" % (h, n), [P, COLS], F32)
@@ -267,7 +265,7 @@ def tile_list_uwb_range_correction_kernel(
             e_acc[h, n] = bank(e_banks[h][n])
             wx_passes(e_acc[h, n], n, h, True)
 
-        wh_g = sbuf("wh_g", [P, PACK * N], BF16)
+        wh_g = sbuf("wh_g", [P, PACK * N], BF16, slot="wb_raw1")
         interleave(nc.vector.tensor_copy, wh_g[:], wh_raw[:])
         nc.vector.quantize_mx(out=wh_w[:, 0:256].bitcast(FP8X4), scales=wh_s[:, 0:256], in_=wh_g[:, 0:1024])
         nc.vector.quantize_mx(out=wh_w[:, 256:N].bitcast(FP8X4), scales=wh_s[:, 256:N], in_=wh_g[:, 1024 : PACK * N])
@@ -294,24 +292,22 @@ def tile_list_uwb_range_correction_kernel(
             copy_e(0, n, ["wb_w1", "wb_s1", "wb_w0"][n])
         open_e(1, 0)
         open_both(1, 0)
-        copy_e(1, 0, None)
         for n in range(N_TILES):
             weigh(0, n)
             finish(0, n, nc.gpsimd, e_sb[0, n][:])
             if n == 1:
                 quantize_h(1)
         for q in range(QUADS):
-            nc.sync.dma_start(
+            nc.scalar.dma_start(
                 out=out_3[0, 4 * q : 4 * q + 4, :].bitcast(I32), in_=h_s[32 * q : 32 * q + 4, :].bitcast(I32)
             )
         close_both(1, 0)
         for n in range(1, N_TILES):
             open_both(1, n)
             close_both(1, n)
-        for n in range(1, N_TILES):
             open_e(1, n)
+        weigh(1, 0)
         for n in range(N_TILES):
-            weigh(1, n)
-        finish(1, 0, nc.gpsimd, e_sb[1, 0][:])
-        for n in range(1, N_TILES):
+            if n + 1 < N_TILES:
+                weigh(1, n + 1)
             finish(1, n, nc.vector, e_acc[1, n][:])

@@ -18,12 +18,36 @@ ALU = mybir.AluOpType
 
 P = 128
 PACK = 4
-PASSES = K // (P * PACK)
+K_PASS = P * PACK
+PASSES = K // K_PASS
 COLS = 512
 HALVES = S // COLS
 N_TILES = N // P
 QUADS = 4
+SCALE_ROWS = 16
+LIST_ROWS = 16
+
+TAB_S_ROW = P - PASSES * SCALE_ROWS
 WB_SPLIT = 384
+WH_SPLIT = 256
+H_SPLIT = 256
+
+TAB_W_BYTES = 4 * T
+WB_COL_BYTES = 4 * PACK
+WB0_AT = TAB_W_BYTES
+TAB_W_AT = [0, WB0_AT + WB_COL_BYTES * H]
+TAB_S_AT = TAB_W_AT[1] - T // 2
+WB1_AT = TAB_W_AT[0]
+WH_AT = WB1_AT + WB_COL_BYTES * H
+GAIN_AT = WH_AT + WB_COL_BYTES * N
+CONF_AT = TAB_S_AT
+WX_W_AT = CONF_AT + 4 * N_TILES * S
+WX_S_AT = WX_W_AT + 4 * PASSES * N
+
+B_BANKS = [[3, 4, 5, 6], [7, 3, 4, 5]]
+E_BANKS = [[0, 1, 2], [4, 0, 1]]
+BOTH_BANKS = [[6, 7, 3], [5, 6, 7]]
+B_EARLY = [(0, 0), (0, 1), (0, 2), (0, 3), (1, 0)]
 
 
 def tile_list_uwb_range_correction_kernel(
@@ -36,8 +60,8 @@ def tile_list_uwb_range_correction_kernel(
         reuse = ctx.enter_context(tc.tile_pool(name="reuse", bufs=1))
         psum = ctx.enter_context(tc.psum_pool(name="psum", bufs=1))
 
-        def sbuf(name, shape, dtype, slot=None):
-            return keep.tile(shape, dtype, name=name, tag=slot or name, align_bytes=64)
+        def sbuf(name, shape, dtype, tag=None):
+            return keep.tile(shape, dtype, name=name, tag=tag or name, align_bytes=64)
 
         def placed(name, shape, dtype, offset):
             return reuse.tile(shape, dtype, name=name, offset=offset, align_bytes=64)
@@ -45,51 +69,59 @@ def tile_list_uwb_range_correction_kernel(
         def bank(i):
             return psum.tile([P, COLS], F32, name="bank%d" % i)
 
-        offsets = keep.tile([P, S // 16], U16, name="offsets")
+        def half_cols(half):
+            return slice(half * COLS, (half + 1) * COLS)
+
+        def tile_cols(i):
+            return slice(P * i, P * (i + 1))
+
+        def scale_rows(q):
+            return slice(32 * q, 32 * q + 4)
+
+        def load_weight_scales(dst, src):
+            for q in range(QUADS):
+                nc.sync.dma_start(
+                    out=dst[scale_rows(q), :, :].bitcast(I32),
+                    in_=src[:, 4 * q : 4 * q + 4, :].rearrange("a r c -> r a c").bitcast(I32),
+                )
+
+        offsets = keep.tile([P, S // LIST_ROWS], U16, name="offsets")
         nc.sync.dma_start(offsets[:], offs)
 
-        tab_s = sbuf("tab_s", [P, T], U8)
+        tab_s = placed("tab_s", [P, T], U8, TAB_S_AT)
         wa_s_raw = sbuf("wa_s_raw", [P, PASSES, H], U8)
-        v_s1 = sbuf("v_s1", [P, S], U8)
-        warm = sbuf("warm", [P, 8], F32)
-        nc.vector.memset(tab_s[:].bitcast(I32), 0)
+        v_s = sbuf("v_s", [P, PASSES, S], U8)
         nc.vector.memset(wa_s_raw[:].bitcast(I32), 0)
-        nc.vector.memset(warm[:], 0.0)
-        nc.vector.memset(v_s1[96:128, :].bitcast(I32), 0)
+        nc.vector.memset(tab_s[0:TAB_S_ROW, :].bitcast(I32), 0)
+        nc.vector.memset(v_s[:].bitcast(I32), 0)
 
+        nc.sync.dma_start(
+            out=tab_s[TAB_S_ROW:P, :].bitcast(I32), in_=tab_scales.rearrange("a q t -> (a q) t").bitcast(I32)
+        )
         wa_raw = sbuf("wa_raw", [P, PASSES, 2 * H], U8)
         nc.sync.dma_start(out=wa_raw[:].bitcast(I32), in_=wa_words.rearrange("a p c -> p a c").bitcast(I32))
-        tab_w = []
-        for a in range(PASSES):
-            words = placed("tab_w%d" % a, [P, T], I32, 4 * T * a)
+        load_weight_scales(wa_s_raw, wa_scales)
+
+        def load_table(a):
+            words = placed("tab_w%d" % a, [P, T], I32, TAB_W_AT[a])
             nc.sync.dma_start(out=words[:], in_=tab_words[a].rearrange("p t i -> p (t i)").bitcast(I32))
-            tab_w.append(words)
+            return words
 
-        def load_wb(rows, a, c0, c1):
-            nc.sync.dma_start(
-                out=rows[:], in_=wb[512 * a : 512 * (a + 1), c0:c1].rearrange("(p j) c -> p j c", j=PACK)
-            )
-            return rows, c0, c1
+        tab_w = [load_table(0)]
 
-        wb_raw = [
-            [load_wb(sbuf("wb_raw0", [P, PACK, H], F32), 0, 0, H)],
-            [load_wb(sbuf("wb_raw1", [P, PACK, WB_SPLIT], F32), 1, 0, WB_SPLIT)],
-        ]
+        picked_s = sbuf("picked_s", [P, S], U8)
+        nc.vector.tensor_copy(out=picked_s[:], in_=tab_s[:].indirect(offsets[:]))
 
-        for q in range(QUADS):
-            nc.gpsimd.dma_start(
-                out=tab_s[32 * q : 32 * q + 8, :].bitcast(I32),
-                in_=tab_scales[:, 4 * q : 4 * q + 4, :].bitcast(I32),
-            )
-        for q in range(QUADS):
-            nc.scalar.dma_start(
-                out=wa_s_raw[32 * q : 32 * q + 4, :, :].bitcast(I32),
-                in_=wa_scales[:, 4 * q : 4 * q + 4, :].rearrange("a r c -> r a c").bitcast(I32),
-            )
-        gain_sb = sbuf("gain_sb", [P, PACK], F32)
-        nc.gpsimd.dma_start(out=gain_sb[:], in_=gain.rearrange("(p t) -> p t", t=PACK))
-        warm_out = sbuf("warm_out", [P, 8], F32)
-        nc.scalar.activation(out=warm_out[:], in_=warm[:], func=ACT.Exp)
+        def place_scales(a):
+            for q in range(QUADS):
+                row = TAB_S_ROW + SCALE_ROWS * a + 4 * q
+                nc.sync.dma_start(
+                    out=v_s[scale_rows(q), a, :].bitcast(I32), in_=picked_s[row : row + 4, :].bitcast(I32)
+                )
+
+        place_scales(0)
+        tab_w.append(load_table(1))
+        place_scales(1)
 
         wa_w = sbuf("wa_w", [P, PASSES, 2 * H], U8)
         wa_s = sbuf("wa_s", [P, PASSES, H], U8)
@@ -97,84 +129,77 @@ def tile_list_uwb_range_correction_kernel(
             out=wa_w[:].bitcast(U16).rearrange("p a (t m) -> p a t m", t=PACK),
             in_=wa_raw[:].bitcast(U16).rearrange("p a (m t) -> p a t m", t=PACK),
         )
-
-        picked_s = sbuf("picked_s", [P, S], U8)
-        nc.vector.tensor_copy(out=picked_s[:], in_=tab_s[:].indirect(offsets[:]))
-        nc.scalar.dma_start(out=v_s1[0:112, :].bitcast(I32), in_=picked_s[4:116, :].bitcast(I32))
-        v_s = [picked_s, v_s1]
         v_w = {}
 
-        picked = sbuf("v_w0", [P, S], U32, slot="tab_s")
-        nc.vector.tensor_copy(out=picked[:], in_=tab_w[0][:].bitcast(U32).indirect(offsets[:]))
-        for h in range(HALVES):
-            v_w[0, h] = picked[:, h * COLS : (h + 1) * COLS]
+        def gather_words(a):
+            for half in range(HALVES):
+                picked = sbuf("v_w%d%d" % (a, half), [P, COLS], U32)
+                entries = offsets[:, half * COLS // LIST_ROWS : (half + 1) * COLS // LIST_ROWS]
+                nc.vector.tensor_copy(out=picked[:], in_=tab_w[a][:].bitcast(U32).indirect(entries))
+                v_w[a, half] = picked
 
-        wb_raw[1].append(load_wb(placed("wb_last", [P, PACK, H - WB_SPLIT], F32, 0), 1, WB_SPLIT, H))
-        wx_w = placed("wx_w", [P, PASSES, N], I32, 2048)
-        nc.sync.dma_start(out=wx_w[:], in_=wx_words.rearrange("a p c i -> p a (c i)").bitcast(I32))
-        wh_raw = placed("wh_raw", [P, PACK, N], F32, 5120)
-        nc.sync.dma_start(out=wh_raw[:], in_=wh.rearrange("(p j) c -> p j c", j=PACK))
-        wx_s = placed("wx_s", [P, PASSES, N], U8, 11264)
-        nc.vector.memset(wx_s[:].bitcast(I32), 0)
-        for q in range(QUADS):
-            nc.scalar.dma_start(
-                out=wx_s[32 * q : 32 * q + 4, :, :].bitcast(I32),
-                in_=wx_scales[:, 4 * q : 4 * q + 4, :].rearrange("a r c -> r a c").bitcast(I32),
+        def load_wb(name, a, c0, c1, offset):
+            rows = placed(name, [P, PACK, c1 - c0], F32, offset + WB_COL_BYTES * c0)
+            nc.sync.dma_start(
+                out=rows[:], in_=wb[K_PASS * a : K_PASS * (a + 1), c0:c1].rearrange("(p j) c -> p j c", j=PACK)
             )
+            return rows, c0, c1
+
+        wb_raw = [[load_wb("wb_raw0", 0, 0, H, WB0_AT)]]
         nc.vector.tensor_copy(
             out=wa_s[:].rearrange("p a (t m) -> p a t m", t=PACK),
             in_=wa_s_raw[:].rearrange("p a (m t) -> p a t m", t=PACK),
         )
-        for h in range(HALVES):
-            picked = sbuf("v_w1%d" % h, [P, COLS], U32, slot="wa_s_raw" if h == 0 else None)
-            nc.vector.tensor_copy(
-                out=picked[:],
-                in_=tab_w[1][:].bitcast(U32).indirect(offsets[:, h * COLS // 16 : (h + 1) * COLS // 16]),
-            )
-            v_w[1, h] = picked[:]
-        conf_sb = placed("conf_sb", [P, N_TILES, S], F32, 4 * T)
-        nc.sync.dma_start(out=conf_sb[:], in_=conf.rearrange("(n p) j -> p n j", p=P))
+        gather_words(0)
+        wb_raw.append([load_wb("wb_raw1", 1, 0, WB_SPLIT, WB1_AT), load_wb("wb_last", 1, WB_SPLIT, H, WB1_AT)])
+        gain_sb = placed("gain_sb", [P, PACK], F32, GAIN_AT)
+        nc.sync.dma_start(out=gain_sb[:], in_=gain.rearrange("(p t) -> p t", t=PACK))
+        wh_raw = placed("wh_raw", [P, PACK, N], F32, WH_AT)
+        nc.sync.dma_start(out=wh_raw[:], in_=wh.rearrange("(p j) c -> p j c", j=PACK))
+        gather_words(1)
+        wx_w = placed("wx_w", [P, PASSES, N], I32, WX_W_AT)
+        nc.sync.dma_start(out=wx_w[:], in_=wx_words.rearrange("a p c i -> p a (c i)").bitcast(I32))
+        wx_s = placed("wx_s", [P, PASSES, N], U8, WX_S_AT)
+        nc.vector.memset(wx_s[:].bitcast(I32), 0)
+        load_weight_scales(wx_s, wx_scales)
 
-        def times_v(acc, words, scales, a, h, start, stop):
+        def times_v(acc, words, scales, a, half, start, stop):
             nc.tensor.matmul_mx(
                 out=acc[:], lhsT=words, lhsT_scale=scales,
-                rhs=v_w[a, h].bitcast(FP8X4), rhs_scale=v_s[a][:, h * COLS : (h + 1) * COLS],
+                rhs=v_w[a, half][:].bitcast(FP8X4), rhs_scale=v_s[:, a, half_cols(half)],
                 start=start, stop=stop,
             )
 
-        def wa_pass(acc, t, a, h):
-            times_v(acc, wa_w[:, a, 2 * P * t : 2 * P * (t + 1)].bitcast(FP4X4), wa_s[:, a, P * t : P * (t + 1)],
-                    a, h, a == 0, a == PASSES - 1)
+        def wa_pass(acc, t, a, half):
+            words = wa_w[:, a, 2 * P * t : 2 * P * (t + 1)].bitcast(FP4X4)
+            times_v(acc, words, wa_s[:, a, tile_cols(t)], a, half, a == 0, a == PASSES - 1)
 
-        def wx_passes(acc, n, h, stop):
+        def wx_passes(acc, n, half, closes):
             for a in range(PASSES):
-                times_v(acc, wx_w[:, a, P * n : P * (n + 1)].bitcast(FP8X4), wx_s[:, a, P * n : P * (n + 1)],
-                        a, h, a == 0, stop and a == PASSES - 1)
+                words = wx_w[:, a, tile_cols(n)].bitcast(FP8X4)
+                times_v(acc, words, wx_s[:, a, tile_cols(n)], a, half, a == 0, closes and a == PASSES - 1)
 
         a_acc = {}
-        tanh_a = [sbuf("tanh_a%d" % h, [P, PACK, COLS], F32) for h in range(HALVES)]
-        for h in range(HALVES):
+        tanh_a = [sbuf("tanh_a%d" % half, [P, PACK, COLS], F32) for half in range(HALVES)]
+        for half in range(HALVES):
             for t in range(PACK):
-                a_acc[h, t] = bank(PACK * h + t)
-                wa_pass(a_acc[h, t], t, 0, h)
+                a_acc[half, t] = bank(PACK * half + t)
+                wa_pass(a_acc[half, t], t, 0, half)
             for t in range(PACK):
-                wa_pass(a_acc[h, t], t, 1, h)
-                nc.scalar.activation(out=tanh_a[h][:, t, :], in_=a_acc[h, t][:], func=ACT.Tanh)
+                wa_pass(a_acc[half, t], t, 1, half)
+                nc.scalar.activation(out=tanh_a[half][:, t, :], in_=a_acc[half, t][:], func=ACT.Tanh)
 
         wb_w, wb_s = [], []
         for a in range(PASSES):
-            if a == 0:
-                grouped = placed("wb_g0", [P, PACK * H], BF16, 4 * T + 4 * N_TILES * S)
-            else:
-                grouped = sbuf("wb_g1", [P, PACK * H], BF16, slot="wb_raw0")
+            grouped = sbuf("wb_g%d" % a, [P, PACK * H], BF16)
+            dealt = grouped[:].rearrange("p (t m j) -> p m t j", t=PACK, j=PACK)
             for rows, c0, c1 in wb_raw[a]:
                 nc.vector.tensor_copy(
-                    out=grouped[:].rearrange("p (t m j) -> p m t j", t=PACK, j=PACK)[:, c0 // PACK : c1 // PACK, :, :],
-                    in_=rows[:].rearrange("p j (m t) -> p m t j", t=PACK),
+                    out=dealt[:, c0 // PACK : c1 // PACK, :, :], in_=rows[:].rearrange("p j (m t) -> p m t j", t=PACK)
                 )
             codes = sbuf("wb_w%d" % a, [P, H], U32)
             scales = sbuf("wb_s%d" % a, [P, H], U8)
-            width = H if a == 0 else H // 2
+            width = H // 2 if a == PASSES - 1 else H
             for c0 in range(0, H, width):
                 nc.vector.quantize_mx(
                     out=codes[:, c0 : c0 + width].bitcast(FP8X4), scales=scales[:, c0 : c0 + width],
@@ -183,42 +208,44 @@ def tile_list_uwb_range_correction_kernel(
             wb_w.append(codes)
             wb_s.append(scales)
 
-        e_banks = [[0, 1, 2], [4, 0, 1]]
-        both_banks = [[6, 7, 3], [5, 6, 7]]
-        b_banks = [[3, 4, 5, 6], [7, 3, 4, 5]]
-        e_acc, both_acc, b_acc = {}, {}, {}
+        conf_sb = placed("conf_sb", [P, N_TILES, S], F32, CONF_AT)
+        nc.sync.dma_start(out=conf_sb[:], in_=conf.rearrange("(n p) j -> p n j", p=P))
 
-        def wb_pass(h, t, a):
+        b_acc, e_acc, both_acc = {}, {}, {}
+
+        def wb_pass(half, t, a):
             if a == 0:
-                b_acc[h, t] = bank(b_banks[h][t])
-            times_v(b_acc[h, t], wb_w[a][:, P * t : P * (t + 1)].bitcast(FP8X4), wb_s[a][:, P * t : P * (t + 1)],
-                    a, h, a == 0, a == PASSES - 1)
+                b_acc[half, t] = bank(B_BANKS[half][t])
+            words = wb_w[a][:, tile_cols(t)].bitcast(FP8X4)
+            times_v(b_acc[half, t], words, wb_s[a][:, tile_cols(t)], a, half, a == 0, a == PASSES - 1)
 
-        early = [(0, 0), (0, 1), (0, 2), (0, 3), (1, 0)]
-        for h, t in early:
-            wb_pass(h, t, 0)
+        for half, t in B_EARLY:
+            wb_pass(half, t, 0)
 
-        exp_b = [sbuf("exp_b%d" % h, [P, PACK, COLS], F32) for h in range(HALVES)]
-        h_sb = [sbuf("h_sb%d" % h, [P, PACK, COLS], F32) for h in range(HALVES)]
-        h_g = [sbuf("h_g%d" % h, [P, PACK * COLS], BF16) for h in range(HALVES)]
-        h_w = [sbuf("h_w%d" % h, [P, COLS], U32) for h in range(HALVES)]
+        exp_b = [sbuf("exp_b%d" % half, [P, PACK, COLS], F32) for half in range(HALVES)]
+        h_sb = [sbuf("h_sb%d" % half, [P, PACK, COLS], F32) for half in range(HALVES)]
+        h_g = [sbuf("h_g%d" % half, [P, PACK * COLS], BF16) for half in range(HALVES)]
+        h_w = [sbuf("h_w%d" % half, [P, COLS], U32) for half in range(HALVES)]
         h_s = sbuf("h_s", [P, S], U8)
         h_rows = out_1.rearrange("(p t) j -> p t j", t=PACK)
 
-        def exp_stage(h):
+        def exp_stage(half):
             for t in range(PACK):
-                if (h, t) not in early:
-                    wb_pass(h, t, 0)
-                wb_pass(h, t, 1)
-                nc.scalar.activation(out=exp_b[h][:, t, :], in_=b_acc[h, t][:], func=ACT.Exp)
+                if (half, t) not in B_EARLY:
+                    wb_pass(half, t, 0)
+                wb_pass(half, t, 1)
+                nc.scalar.activation(out=exp_b[half][:, t, :], in_=b_acc[half, t][:], func=ACT.Exp)
 
-        def code_stage(h):
+        def code_stage(half):
             for t in range(PACK):
                 nc.vector.scalar_tensor_tensor(
-                    out=h_sb[h][:, t, :], in0=tanh_a[h][:, t, :], scalar=gain_sb[:, t : t + 1],
-                    in1=exp_b[h][:, t, :], op0=ALU.mult, op1=ALU.mult,
+                    out=h_sb[half][:, t, :], in0=tanh_a[half][:, t, :], scalar=gain_sb[:, t : t + 1],
+                    in1=exp_b[half][:, t, :], op0=ALU.mult, op1=ALU.mult,
                 )
-            nc.sync.dma_start(out=h_rows[:, :, h * COLS : (h + 1) * COLS], in_=h_sb[h][:])
+                if t % 2 == 1:
+                    nc.sync.dma_start(
+                        out=h_rows[:, t - 1 : t + 1, half_cols(half)], in_=h_sb[half][:, t - 1 : t + 1, :]
+                    )
 
         def interleave(copy, dst, src):
             copy(
@@ -226,86 +253,86 @@ def tile_list_uwb_range_correction_kernel(
                 in_=src.rearrange("p t (c i) -> p c t i", i=4),
             )
 
-        def quantize_h(h):
-            nc.vector.quantize_mx(
-                out=h_w[h][:].bitcast(FP8X4), scales=h_s[:, h * COLS : (h + 1) * COLS], in_=h_g[h][:]
-            )
+        def quantize_h(half):
+            nc.vector.quantize_mx(out=h_w[half][:].bitcast(FP8X4), scales=h_s[:, half_cols(half)], in_=h_g[half][:])
             nc.sync.dma_start(
-                out=out_2[0, :, h * COLS : (h + 1) * COLS, :].rearrange("p m t -> p (m t)").bitcast(I32),
-                in_=h_w[h][:].bitcast(I32),
+                out=out_2[0, :, half_cols(half), :].rearrange("p m t -> p (m t)").bitcast(I32),
+                in_=h_w[half][:].bitcast(I32),
             )
 
         wh_w = sbuf("wh_w", [P, N], U32)
         wh_s = sbuf("wh_s", [P, N], U8)
 
-        def open_both(h, n):
-            both_acc[h, n] = bank(both_banks[h][n])
-            wx_passes(both_acc[h, n], n, h, False)
+        def open_both(half, n):
+            both_acc[half, n] = bank(BOTH_BANKS[half][n])
+            wx_passes(both_acc[half, n], n, half, False)
 
-        def close_both(h, n):
+        def close_both(half, n):
             nc.tensor.matmul_mx(
-                out=both_acc[h, n][:], lhsT=wh_w[:, P * n : P * (n + 1)].bitcast(FP8X4),
-                lhsT_scale=wh_s[:, P * n : P * (n + 1)],
-                rhs=h_w[h][:].bitcast(FP8X4), rhs_scale=h_s[:, h * COLS : (h + 1) * COLS],
+                out=both_acc[half, n][:], lhsT=wh_w[:, tile_cols(n)].bitcast(FP8X4), lhsT_scale=wh_s[:, tile_cols(n)],
+                rhs=h_w[half][:].bitcast(FP8X4), rhs_scale=h_s[:, half_cols(half)],
                 start=False, stop=True,
             )
 
         weighted = {}
 
-        def weigh(h, n):
-            weighted[h, n] = sbuf("weighted%d%d" % (h, n), [P, COLS], F32)
-            nc.vector.tensor_tensor(out=weighted[h, n][:], in0=both_acc[h, n][:], in1=conf_sb[:, n, h * COLS : (h + 1) * COLS], op=ALU.mult)
+        def weigh(half, n):
+            weighted[half, n] = sbuf("weighted%d%d" % (half, n), [P, COLS], F32)
+            nc.vector.tensor_tensor(
+                out=weighted[half, n][:], in0=both_acc[half, n][:], in1=conf_sb[:, n, half_cols(half)], op=ALU.mult
+            )
 
-        def finish(h, n, engine, e_values):
-            y = sbuf("y%d%d" % (h, n), [P, COLS], F32)
-            engine.tensor_tensor(out=y[:], in0=weighted[h, n][:], in1=e_values, op=ALU.subtract)
-            nc.sync.dma_start(out=out_0[P * n : P * (n + 1), h * COLS : (h + 1) * COLS], in_=y[:])
+        def finish(half, n, engine, e_values):
+            y = sbuf("y%d%d" % (half, n), [P, COLS], F32)
+            engine.tensor_tensor(out=y[:], in0=weighted[half, n][:], in1=e_values, op=ALU.subtract)
+            nc.sync.dma_start(out=out_0[tile_cols(n), half_cols(half)], in_=y[:])
 
-        def open_e(h, n):
-            e_acc[h, n] = bank(e_banks[h][n])
-            wx_passes(e_acc[h, n], n, h, True)
+        def e_passes(half, n):
+            e_acc[half, n] = bank(E_BANKS[half][n])
+            wx_passes(e_acc[half, n], n, half, True)
 
-        wh_g = sbuf("wh_g", [P, PACK * N], BF16, slot="wb_raw1")
+        wh_g = sbuf("wh_g", [P, PACK * N], BF16)
         interleave(nc.vector.tensor_copy, wh_g[:], wh_raw[:])
-        nc.vector.quantize_mx(out=wh_w[:, 0:256].bitcast(FP8X4), scales=wh_s[:, 0:256], in_=wh_g[:, 0:1024])
-        nc.vector.quantize_mx(out=wh_w[:, 256:N].bitcast(FP8X4), scales=wh_s[:, 256:N], in_=wh_g[:, 1024 : PACK * N])
-        exp_stage(0)
-        exp_stage(1)
-        code_stage(0)
-        code_stage(1)
+        for c0, c1 in ((0, WH_SPLIT), (WH_SPLIT, N)):
+            nc.vector.quantize_mx(
+                out=wh_w[:, c0:c1].bitcast(FP8X4), scales=wh_s[:, c0:c1], in_=wh_g[:, PACK * c0 : PACK * c1]
+            )
+        for half in range(HALVES):
+            exp_stage(half)
+        for half in range(HALVES):
+            code_stage(half)
         for n in range(N_TILES):
-            open_e(0, n)
-        interleave(nc.vector.tensor_copy, h_g[0][:], h_sb[0][:])
-        interleave(nc.scalar.copy, h_g[1][:], h_sb[1][:])
+            e_passes(0, n)
+        interleave(nc.scalar.copy, h_g[0][:], h_sb[0][:])
+        interleave(nc.vector.tensor_copy, h_g[1][:, 0 : PACK * H_SPLIT], h_sb[1][:, :, 0:H_SPLIT])
+        interleave(nc.scalar.copy, h_g[1][:, PACK * H_SPLIT : PACK * COLS], h_sb[1][:, :, H_SPLIT:COLS])
         quantize_h(0)
         for n in range(N_TILES):
             open_both(0, n)
         for n in range(N_TILES):
             close_both(0, n)
-        e_sb = {}
 
-        def copy_e(h, n, slot):
-            e_sb[h, n] = sbuf("e_sb%d%d" % (h, n), [P, COLS], F32, slot=slot)
-            nc.scalar.copy(out=e_sb[h, n][:], in_=e_acc[h, n][:])
-
-        for n in range(N_TILES):
-            copy_e(0, n, ["wb_w1", "wb_s1", "wb_w0"][n])
-        open_e(1, 0)
+        e_sb = []
+        for n, tag in enumerate(("wb_w1", "wb_s1", "wb_w0")):
+            e_sb.append(sbuf("e_sb%d" % n, [P, COLS], F32, tag=tag))
+            nc.scalar.copy(out=e_sb[n][:], in_=e_acc[0, n][:])
+        e_passes(1, 0)
         open_both(1, 0)
         for n in range(N_TILES):
-            weigh(0, n)
-            finish(0, n, nc.gpsimd, e_sb[0, n][:])
-            if n == 1:
+            if n == N_TILES - 1:
                 quantize_h(1)
+            weigh(0, n)
+            finish(0, n, nc.gpsimd, e_sb[n][:])
         for q in range(QUADS):
             nc.scalar.dma_start(
-                out=out_3[0, 4 * q : 4 * q + 4, :].bitcast(I32), in_=h_s[32 * q : 32 * q + 4, :].bitcast(I32)
+                out=out_3[0, 4 * q : 4 * q + 4, :].bitcast(I32), in_=h_s[scale_rows(q), :].bitcast(I32)
             )
+
         close_both(1, 0)
         for n in range(1, N_TILES):
             open_both(1, n)
             close_both(1, n)
-            open_e(1, n)
+            e_passes(1, n)
         weigh(1, 0)
         for n in range(N_TILES):
             if n + 1 < N_TILES:

@@ -29,8 +29,9 @@ LIST_ROWS = 16
 
 TAB_S_ROW = P - PASSES * SCALE_ROWS
 WB_SPLIT = 384
-WH_SPLIT = 256
-H_SPLIT = 256
+QCOLS = 256
+QUARTERS = S // QCOLS
+BANKS = 8
 
 TAB_W_BYTES = 4 * T
 WB_COL_BYTES = 4 * PACK
@@ -43,11 +44,6 @@ GAIN_AT = WH_AT + WB_COL_BYTES * N
 CONF_AT = TAB_S_AT
 WX_W_AT = CONF_AT + 4 * N_TILES * S
 WX_S_AT = WX_W_AT + 4 * PASSES * N
-
-B_BANKS = [[3, 4, 5, 6], [7, 3, 4, 5]]
-E_BANKS = [[0, 1, 2], [4, 0, 1]]
-BOTH_BANKS = [[6, 7, 3], [5, 6, 7]]
-B_EARLY = [(0, 0), (0, 1), (0, 2), (0, 3), (1, 0)]
 
 
 def tile_list_uwb_range_correction_kernel(
@@ -174,20 +170,21 @@ def tile_list_uwb_range_correction_kernel(
             words = wa_w[:, a, 2 * P * t : 2 * P * (t + 1)].bitcast(FP4X4)
             times_v(acc, words, wa_s[:, a, tile_cols(t)], a, half, a == 0, a == PASSES - 1)
 
-        def wx_passes(acc, n, half, closes):
-            for a in range(PASSES):
-                words = wx_w[:, a, tile_cols(n)].bitcast(FP8X4)
-                times_v(acc, words, wx_s[:, a, tile_cols(n)], a, half, a == 0, closes and a == PASSES - 1)
-
         a_acc = {}
         tanh_a = [sbuf("tanh_a%d" % half, [P, PACK, COLS], F32) for half in range(HALVES)]
+
+        def tanh_stage(half):
+            for t in range(PACK):
+                nc.scalar.activation(out=tanh_a[half][:, t, :], in_=a_acc[half, t][:], func=ACT.Tanh)
+
         for half in range(HALVES):
             for t in range(PACK):
                 a_acc[half, t] = bank(PACK * half + t)
                 wa_pass(a_acc[half, t], t, 0, half)
+        for half in range(HALVES):
             for t in range(PACK):
                 wa_pass(a_acc[half, t], t, 1, half)
-                nc.scalar.activation(out=tanh_a[half][:, t, :], in_=a_acc[half, t][:], func=ACT.Tanh)
+        tanh_stage(0)
 
         wb_w, wb_s = [], []
         for a in range(PASSES):
@@ -211,30 +208,22 @@ def tile_list_uwb_range_correction_kernel(
         conf_sb = placed("conf_sb", [P, N_TILES, S], F32, CONF_AT)
         nc.sync.dma_start(out=conf_sb[:], in_=conf.rearrange("(n p) j -> p n j", p=P))
 
-        b_acc, e_acc, both_acc = {}, {}, {}
-
-        def wb_pass(half, t, a):
-            if a == 0:
-                b_acc[half, t] = bank(B_BANKS[half][t])
+        def wb_pass(acc, half, t, a):
             words = wb_w[a][:, tile_cols(t)].bitcast(FP8X4)
-            times_v(b_acc[half, t], words, wb_s[a][:, tile_cols(t)], a, half, a == 0, a == PASSES - 1)
-
-        for half, t in B_EARLY:
-            wb_pass(half, t, 0)
+            times_v(acc, words, wb_s[a][:, tile_cols(t)], a, half, a == 0, a == PASSES - 1)
 
         exp_b = [sbuf("exp_b%d" % half, [P, PACK, COLS], F32) for half in range(HALVES)]
         h_sb = [sbuf("h_sb%d" % half, [P, PACK, COLS], F32) for half in range(HALVES)]
-        h_g = [sbuf("h_g%d" % half, [P, PACK * COLS], BF16) for half in range(HALVES)]
-        h_w = [sbuf("h_w%d" % half, [P, COLS], U32) for half in range(HALVES)]
+        h_w = sbuf("h_w", [P, S], U32)
         h_s = sbuf("h_s", [P, S], U8)
         h_rows = out_1.rearrange("(p t) j -> p t j", t=PACK)
 
         def exp_stage(half):
             for t in range(PACK):
-                if (half, t) not in B_EARLY:
-                    wb_pass(half, t, 0)
-                wb_pass(half, t, 1)
-                nc.scalar.activation(out=exp_b[half][:, t, :], in_=b_acc[half, t][:], func=ACT.Exp)
+                acc = bank(PACK * half + t)
+                for a in range(PASSES):
+                    wb_pass(acc, half, t, a)
+                nc.scalar.activation(out=exp_b[half][:, t, :], in_=acc[:], func=ACT.Exp)
 
         def code_stage(half):
             for t in range(PACK):
@@ -253,88 +242,93 @@ def tile_list_uwb_range_correction_kernel(
                 in_=src.rearrange("p t (c i) -> p c t i", i=4),
             )
 
-        def quantize_h(half):
-            nc.vector.quantize_mx(out=h_w[half][:].bitcast(FP8X4), scales=h_s[:, half_cols(half)], in_=h_g[half][:])
-            nc.sync.dma_start(
-                out=out_2[0, :, half_cols(half), :].rearrange("p m t -> p (m t)").bitcast(I32),
-                in_=h_w[half][:].bitcast(I32),
-            )
-
-        wh_w = sbuf("wh_w", [P, N], U32)
-        wh_s = sbuf("wh_s", [P, N], U8)
-
-        def open_both(half, n):
-            both_acc[half, n] = bank(BOTH_BANKS[half][n])
-            wx_passes(both_acc[half, n], n, half, False)
-
-        def close_both(half, n):
-            nc.tensor.matmul_mx(
-                out=both_acc[half, n][:], lhsT=wh_w[:, tile_cols(n)].bitcast(FP8X4), lhsT_scale=wh_s[:, tile_cols(n)],
-                rhs=h_w[half][:].bitcast(FP8X4), rhs_scale=h_s[:, half_cols(half)],
-                start=False, stop=True,
-            )
-
-        weighted = {}
-
-        def weigh(half, n):
-            weighted[half, n] = sbuf("weighted%d%d" % (half, n), [P, COLS], F32)
-            nc.vector.tensor_tensor(
-                out=weighted[half, n][:], in0=both_acc[half, n][:], in1=conf_sb[:, n, half_cols(half)], op=ALU.mult
-            )
-
-        def finish(half, n, engine, e_values):
-            y = sbuf("y%d%d" % (half, n), [P, COLS], F32)
-            engine.tensor_tensor(out=y[:], in0=weighted[half, n][:], in1=e_values, op=ALU.subtract)
-            nc.sync.dma_start(out=out_0[tile_cols(n), half_cols(half)], in_=y[:])
-
-        def e_passes(half, n):
-            e_acc[half, n] = bank(E_BANKS[half][n])
-            wx_passes(e_acc[half, n], n, half, True)
-
-        wh_g = sbuf("wh_g", [P, PACK * N], BF16)
-        interleave(nc.vector.tensor_copy, wh_g[:], wh_raw[:])
-        for c0, c1 in ((0, WH_SPLIT), (WH_SPLIT, N)):
-            nc.vector.quantize_mx(
-                out=wh_w[:, c0:c1].bitcast(FP8X4), scales=wh_s[:, c0:c1], in_=wh_g[:, PACK * c0 : PACK * c1]
-            )
-        for half in range(HALVES):
-            exp_stage(half)
+        exp_stage(0)
+        tanh_stage(1)
+        exp_stage(1)
         for half in range(HALVES):
             code_stage(half)
-        for n in range(N_TILES):
-            e_passes(0, n)
-        interleave(nc.scalar.copy, h_g[0][:], h_sb[0][:])
-        interleave(nc.vector.tensor_copy, h_g[1][:, 0 : PACK * H_SPLIT], h_sb[1][:, :, 0:H_SPLIT])
-        interleave(nc.scalar.copy, h_g[1][:, PACK * H_SPLIT : PACK * COLS], h_sb[1][:, :, H_SPLIT:COLS])
-        quantize_h(0)
-        for n in range(N_TILES):
-            open_both(0, n)
-        for n in range(N_TILES):
-            close_both(0, n)
 
-        e_sb = []
-        for n, tag in enumerate(("wb_w1", "wb_s1", "wb_w0")):
-            e_sb.append(sbuf("e_sb%d" % n, [P, COLS], F32, tag=tag))
-            nc.scalar.copy(out=e_sb[n][:], in_=e_acc[0, n][:])
-        e_passes(1, 0)
-        open_both(1, 0)
-        for n in range(N_TILES):
-            if n == N_TILES - 1:
-                quantize_h(1)
-            weigh(0, n)
-            finish(0, n, nc.gpsimd, e_sb[n][:])
+        wh_g = sbuf("wh_g", [P, PACK * N], BF16)
+        wh_w = sbuf("wh_w", [P, N], U32)
+        wh_s = sbuf("wh_s", [P, N], U8)
+        interleave(nc.vector.tensor_copy, wh_g[:], wh_raw[:])
+        nc.vector.quantize_mx(out=wh_w[:].bitcast(FP8X4), scales=wh_s[:], in_=wh_g[:])
+
+        def quarter_cols(q):
+            return slice(q * QCOLS, (q + 1) * QCOLS)
+
+        def in_half(q):
+            half, c0 = divmod(q * QCOLS, COLS)
+            return half, slice(c0, c0 + QCOLS)
+
+        def quantize_h(q):
+            half, cols = in_half(q)
+            grouped = sbuf("h_g%d" % q, [P, PACK * QCOLS], BF16)
+            interleave(nc.scalar.copy, grouped[:], h_sb[half][:, :, cols])
+            nc.vector.quantize_mx(
+                out=h_w[:, quarter_cols(q)].bitcast(FP8X4), scales=h_s[:, quarter_cols(q)], in_=grouped[:]
+            )
+            if cols.stop == COLS:
+                nc.sync.dma_start(
+                    out=out_2[0, :, half_cols(half), :].rearrange("p m t -> p (m t)").bitcast(I32),
+                    in_=h_w[:, half_cols(half)].bitcast(I32),
+                )
+
+        def wx_passes(acc, n, q, start, stop):
+            half, cols = in_half(q)
+            for a in range(PASSES):
+                nc.tensor.matmul_mx(
+                    out=acc, lhsT=wx_w[:, a, tile_cols(n)].bitcast(FP8X4), lhsT_scale=wx_s[:, a, tile_cols(n)],
+                    rhs=v_w[a, half][:, cols].bitcast(FP8X4), rhs_scale=v_s[:, a, quarter_cols(q)],
+                    start=start and a == 0, stop=stop and a == PASSES - 1,
+                )
+
+        def wh_pass(acc, n, q, stop):
+            nc.tensor.matmul_mx(
+                out=acc, lhsT=wh_w[:, tile_cols(n)].bitcast(FP8X4), lhsT_scale=wh_s[:, tile_cols(n)],
+                rhs=h_w[:, quarter_cols(q)].bitcast(FP8X4), rhs_scale=h_s[:, quarter_cols(q)],
+                start=False, stop=stop,
+            )
+
+        sums = {}
+
+        def products(q):
+            both01, e01, last = [
+                bank((N_TILES * q + i) % BANKS)[:].rearrange("p (u c) -> p u c", c=QCOLS) for i in range(N_TILES)
+            ]
+            for n in range(2):
+                wx_passes(both01[:, n, :], n, q, n == 0, False)
+            wx_passes(last[:, 1, :], 2, q, True, True)
+            wx_passes(last[:, 0, :], 2, q, True, False)
+            for n in range(2):
+                wx_passes(e01[:, n, :], n, q, True, True)
+            for n in range(2):
+                wh_pass(both01[:, n, :], n, q, n == 1)
+            wh_pass(last[:, 0, :], 2, q, True)
+            sums[q] = both01, e01, last
+
+        y_rows = out_0.rearrange("(n p) j -> p n j", p=P)
+
+        def finish(q):
+            both01, e01, last = sums[q]
+            weighted = sbuf("weighted%d" % q, [P, N_TILES, QCOLS], F32)
+            y = sbuf("y%d" % q, [P, N_TILES, QCOLS], F32)
+            parts = ((slice(0, 2), both01, e01), (slice(2, 3), last[:, 0:1, :], last[:, 1:2, :]))
+            for rows, both, e in parts:
+                nc.vector.tensor_tensor(
+                    out=weighted[:, rows, :], in0=both, in1=conf_sb[:, rows, quarter_cols(q)], op=ALU.mult
+                )
+            for rows, both, e in parts:
+                nc.vector.tensor_tensor(out=y[:, rows, :], in0=weighted[:, rows, :], in1=e, op=ALU.subtract)
+                nc.sync.dma_start(out=y_rows[:, rows, quarter_cols(q)], in_=y[:, rows, :])
+
+        for q in range(QUARTERS):
+            quantize_h(q)
+            if q > 0:
+                finish(q - 1)
+            products(q)
         for q in range(QUADS):
             nc.scalar.dma_start(
                 out=out_3[0, 4 * q : 4 * q + 4, :].bitcast(I32), in_=h_s[scale_rows(q), :].bitcast(I32)
             )
-
-        close_both(1, 0)
-        for n in range(1, N_TILES):
-            open_both(1, n)
-            close_both(1, n)
-            e_passes(1, n)
-        weigh(1, 0)
-        for n in range(N_TILES):
-            if n + 1 < N_TILES:
-                weigh(1, n + 1)
-            finish(1, n, nc.vector, e_acc[1, n][:])
+        finish(QUARTERS - 1)

@@ -41,8 +41,9 @@ TAB_S_AT = TAB_W_AT[1] - T // 2
 WB1_AT = TAB_W_AT[0]
 WH_AT = WB1_AT + WB_COL_BYTES * H
 GAIN_AT = WH_AT + WB_COL_BYTES * N
-CONF_AT = TAB_S_AT
-WX_W_AT = CONF_AT + 4 * N_TILES * S
+CONF_BYTES = 4 * N_TILES * COLS
+CONF_AT = [TAB_S_AT + CONF_BYTES, TAB_S_AT]
+WX_W_AT = TAB_S_AT + HALVES * CONF_BYTES
 WX_S_AT = WX_W_AT + 4 * PASSES * N
 
 
@@ -153,6 +154,13 @@ def tile_list_uwb_range_correction_kernel(
         wh_raw = placed("wh_raw", [P, PACK, N], F32, WH_AT)
         nc.sync.dma_start(out=wh_raw[:], in_=wh.rearrange("(p j) c -> p j c", j=PACK))
         gather_words(1)
+
+        def load_conf(half):
+            rows = placed("conf%d" % half, [P, N_TILES, COLS], F32, CONF_AT[half])
+            nc.sync.dma_start(out=rows[:], in_=conf[:, half_cols(half)].rearrange("(n p) j -> p n j", p=P))
+            return rows
+
+        conf_sb = [load_conf(0)]
         wx_w = placed("wx_w", [P, PASSES, N], I32, WX_W_AT)
         nc.sync.dma_start(out=wx_w[:], in_=wx_words.rearrange("a p c i -> p a (c i)").bitcast(I32))
         wx_s = placed("wx_s", [P, PASSES, N], U8, WX_S_AT)
@@ -205,8 +213,7 @@ def tile_list_uwb_range_correction_kernel(
             wb_w.append(codes)
             wb_s.append(scales)
 
-        conf_sb = placed("conf_sb", [P, N_TILES, S], F32, CONF_AT)
-        nc.sync.dma_start(out=conf_sb[:], in_=conf.rearrange("(n p) j -> p n j", p=P))
+        conf_sb.append(load_conf(1))
 
         def wb_pass(acc, half, t, a):
             words = wb_w[a][:, tile_cols(t)].bitcast(FP8X4)
@@ -214,7 +221,7 @@ def tile_list_uwb_range_correction_kernel(
 
         exp_b = [sbuf("exp_b%d" % half, [P, PACK, COLS], F32) for half in range(HALVES)]
         h_sb = [sbuf("h_sb%d" % half, [P, PACK, COLS], F32) for half in range(HALVES)]
-        h_w = sbuf("h_w", [P, S], U32)
+        h_w = [sbuf("h_w0", [P, COLS], U32), placed("h_w1", [P, COLS], U32, CONF_AT[0])]
         h_s = sbuf("h_s", [P, S], U8)
         h_rows = out_1.rearrange("(p t) j -> p t j", t=PACK)
 
@@ -266,69 +273,93 @@ def tile_list_uwb_range_correction_kernel(
             grouped = sbuf("h_g%d" % q, [P, PACK * QCOLS], BF16)
             interleave(nc.scalar.copy, grouped[:], h_sb[half][:, :, cols])
             nc.vector.quantize_mx(
-                out=h_w[:, quarter_cols(q)].bitcast(FP8X4), scales=h_s[:, quarter_cols(q)], in_=grouped[:]
+                out=h_w[half][:, cols].bitcast(FP8X4), scales=h_s[:, quarter_cols(q)], in_=grouped[:]
             )
             if cols.stop == COLS:
                 nc.sync.dma_start(
                     out=out_2[0, :, half_cols(half), :].rearrange("p m t -> p (m t)").bitcast(I32),
-                    in_=h_w[:, half_cols(half)].bitcast(I32),
+                    in_=h_w[half][:].bitcast(I32),
                 )
 
-        def wx_passes(acc, n, q, start, stop):
-            half, cols = in_half(q)
+        def wx_passes(acc, n, half, closes):
             for a in range(PASSES):
-                nc.tensor.matmul_mx(
-                    out=acc, lhsT=wx_w[:, a, tile_cols(n)].bitcast(FP8X4), lhsT_scale=wx_s[:, a, tile_cols(n)],
-                    rhs=v_w[a, half][:, cols].bitcast(FP8X4), rhs_scale=v_s[:, a, quarter_cols(q)],
-                    start=start and a == 0, stop=stop and a == PASSES - 1,
-                )
+                words = wx_w[:, a, tile_cols(n)].bitcast(FP8X4)
+                times_v(acc, words, wx_s[:, a, tile_cols(n)], a, half, a == 0, closes and a == PASSES - 1)
 
-        def wh_pass(acc, n, q, stop):
+        def wh_pass(acc, n, q):
+            half, cols = in_half(q)
             nc.tensor.matmul_mx(
-                out=acc, lhsT=wh_w[:, tile_cols(n)].bitcast(FP8X4), lhsT_scale=wh_s[:, tile_cols(n)],
-                rhs=h_w[:, quarter_cols(q)].bitcast(FP8X4), rhs_scale=h_s[:, quarter_cols(q)],
-                start=False, stop=stop,
+                out=acc[:, cols], lhsT=wh_w[:, tile_cols(n)].bitcast(FP8X4), lhsT_scale=wh_s[:, tile_cols(n)],
+                rhs=h_w[half][:, cols].bitcast(FP8X4), rhs_scale=h_s[:, quarter_cols(q)],
+                start=False, stop=cols.stop == COLS,
             )
 
-        sums = {}
+        both_acc, e_acc, weighted = {}, {}, {}
 
-        def products(q):
-            both01, e01, last = [
-                bank((N_TILES * q + i) % BANKS)[:].rearrange("p (u c) -> p u c", c=QCOLS) for i in range(N_TILES)
-            ]
-            for n in range(2):
-                wx_passes(both01[:, n, :], n, q, n == 0, False)
-            wx_passes(last[:, 1, :], 2, q, True, True)
-            wx_passes(last[:, 0, :], 2, q, True, False)
-            for n in range(2):
-                wx_passes(e01[:, n, :], n, q, True, True)
-            for n in range(2):
-                wh_pass(both01[:, n, :], n, q, n == 1)
-            wh_pass(last[:, 0, :], 2, q, True)
-            sums[q] = both01, e01, last
+        def open_both(half, n):
+            both_acc[half, n] = bank((2 * N_TILES * half + n) % BANKS)
+            wx_passes(both_acc[half, n], n, half, False)
 
-        y_rows = out_0.rearrange("(n p) j -> p n j", p=P)
+        def e_passes(half, n):
+            e_acc[half, n] = bank((2 * N_TILES * half + N_TILES + n) % BANKS)
+            wx_passes(e_acc[half, n], n, half, True)
 
-        def finish(q):
-            both01, e01, last = sums[q]
-            weighted = sbuf("weighted%d" % q, [P, N_TILES, QCOLS], F32)
-            y = sbuf("y%d" % q, [P, N_TILES, QCOLS], F32)
-            parts = ((slice(0, 2), both01, e01), (slice(2, 3), last[:, 0:1, :], last[:, 1:2, :]))
-            for rows, both, e in parts:
-                nc.vector.tensor_tensor(
-                    out=weighted[:, rows, :], in0=both, in1=conf_sb[:, rows, quarter_cols(q)], op=ALU.mult
-                )
-            for rows, both, e in parts:
-                nc.vector.tensor_tensor(out=y[:, rows, :], in0=weighted[:, rows, :], in1=e, op=ALU.subtract)
-                nc.sync.dma_start(out=y_rows[:, rows, quarter_cols(q)], in_=y[:, rows, :])
+        def weigh(half, n):
+            weighted[half, n] = sbuf("weighted%d%d" % (half, n), [P, COLS], F32)
+            nc.vector.tensor_tensor(
+                out=weighted[half, n][:], in0=both_acc[half, n][:], in1=conf_sb[half][:, n, :], op=ALU.mult
+            )
 
-        for q in range(QUARTERS):
-            quantize_h(q)
-            if q > 0:
-                finish(q - 1)
-            products(q)
+        def finish(half, n, engine, e_values):
+            y = sbuf("y%d%d" % (half, n), [P, COLS], F32)
+            engine.tensor_tensor(out=y[:], in0=weighted[half, n][:], in1=e_values, op=ALU.subtract)
+            nc.sync.dma_start(out=out_0[tile_cols(n), half_cols(half)], in_=y[:])
+
+        for n in range(N_TILES):
+            open_both(0, n)
+        for n in range(N_TILES):
+            e_passes(0, n)
+        for n in range(N_TILES - 1):
+            open_both(1, n)
+
+        def finish_on_gpsimd(half, n):
+            finish(half, n, nc.gpsimd, e_sb[half, n][:])
+
+        def copy_e(half, n):
+            e_sb[half, n] = sbuf("e_sb%d%d" % (half, n), [P, COLS], F32)
+            nc.scalar.copy(out=e_sb[half, n][:], in_=e_acc[half, n][:])
+
+        def close_both(half):
+            first, second = HALVES * half, HALVES * half + 1
+            for n in range(N_TILES):
+                wh_pass(both_acc[half, n], n, first)
+            for n in range(N_TILES):
+                wh_pass(both_acc[half, n], n, second)
+
+        e_sb = {}
+        quantize_h(0)
+        quantize_h(1)
+        copy_e(0, 1)
+        close_both(0)
+        for n in range(N_TILES):
+            weigh(0, n)
+        quantize_h(2)
+        quantize_h(3)
+        copy_e(0, 2)
+        finish(0, 0, nc.vector, e_acc[0, 0][:])
+        open_both(1, N_TILES - 1)
+        close_both(1)
+        for n in range(N_TILES):
+            e_passes(1, n)
+        copy_e(1, 0)
         for q in range(QUADS):
             nc.scalar.dma_start(
                 out=out_3[0, 4 * q : 4 * q + 4, :].bitcast(I32), in_=h_s[scale_rows(q), :].bitcast(I32)
             )
-        finish(QUARTERS - 1)
+        finish_on_gpsimd(0, 1)
+        finish_on_gpsimd(0, 2)
+        weigh(1, 0)
+        finish_on_gpsimd(1, 0)
+        for n in range(1, N_TILES):
+            weigh(1, n)
+            finish(1, n, nc.vector, e_acc[1, n][:])

@@ -27,10 +27,8 @@ QUADS = 4
 SCALE_ROWS = 16
 LIST_ROWS = 16
 
-TAB_S_ROW = P - PASSES * SCALE_ROWS
-WB_SPLIT = 384
-QCOLS = 256
-QUARTERS = S // QCOLS
+TAB_S_ROW = [96, 112]
+H_SPLIT = 256
 BANKS = 8
 
 TAB_W_BYTES = 4 * T
@@ -41,10 +39,10 @@ TAB_S_AT = TAB_W_AT[1] - T // 2
 WB1_AT = TAB_W_AT[0]
 WH_AT = WB1_AT + WB_COL_BYTES * H
 GAIN_AT = WH_AT + WB_COL_BYTES * N
-CONF_BYTES = 4 * N_TILES * COLS
-CONF_AT = [TAB_S_AT + CONF_BYTES, TAB_S_AT]
-WX_W_AT = TAB_S_AT + HALVES * CONF_BYTES
-WX_S_AT = WX_W_AT + 4 * PASSES * N
+WX_S_AT = GAIN_AT + 64
+CONF_BYTES = 4 * S
+CONF_AT = [TAB_S_AT + CONF_BYTES, TAB_S_AT + 2 * CONF_BYTES, TAB_S_AT]
+WX_W_AT = TAB_S_AT + N_TILES * CONF_BYTES
 
 
 def tile_list_uwb_range_correction_kernel(
@@ -75,9 +73,9 @@ def tile_list_uwb_range_correction_kernel(
         def scale_rows(q):
             return slice(32 * q, 32 * q + 4)
 
-        def load_weight_scales(dst, src):
+        def load_weight_scales(queue, dst, src):
             for q in range(QUADS):
-                nc.sync.dma_start(
+                queue.dma_start(
                     out=dst[scale_rows(q), :, :].bitcast(I32),
                     in_=src[:, 4 * q : 4 * q + 4, :].rearrange("a r c -> r a c").bitcast(I32),
                 )
@@ -89,15 +87,14 @@ def tile_list_uwb_range_correction_kernel(
         wa_s_raw = sbuf("wa_s_raw", [P, PASSES, H], U8)
         v_s = sbuf("v_s", [P, PASSES, S], U8)
         nc.vector.memset(wa_s_raw[:].bitcast(I32), 0)
-        nc.vector.memset(tab_s[0:TAB_S_ROW, :].bitcast(I32), 0)
-        nc.vector.memset(v_s[:].bitcast(I32), 0)
+        nc.vector.memset(tab_s[0 : TAB_S_ROW[0], :].bitcast(I32), 0)
 
         nc.sync.dma_start(
-            out=tab_s[TAB_S_ROW:P, :].bitcast(I32), in_=tab_scales.rearrange("a q t -> (a q) t").bitcast(I32)
+            out=tab_s[TAB_S_ROW[0] : P, :].bitcast(I32), in_=tab_scales.rearrange("a q t -> (a q) t").bitcast(I32)
         )
         wa_raw = sbuf("wa_raw", [P, PASSES, 2 * H], U8)
         nc.sync.dma_start(out=wa_raw[:].bitcast(I32), in_=wa_words.rearrange("a p c -> p a c").bitcast(I32))
-        load_weight_scales(wa_s_raw, wa_scales)
+        load_weight_scales(nc.sync, wa_s_raw, wa_scales)
 
         def load_table(a):
             words = placed("tab_w%d" % a, [P, T], I32, TAB_W_AT[a])
@@ -111,7 +108,7 @@ def tile_list_uwb_range_correction_kernel(
 
         def place_scales(a):
             for q in range(QUADS):
-                row = TAB_S_ROW + SCALE_ROWS * a + 4 * q
+                row = TAB_S_ROW[a] + 4 * q
                 nc.sync.dma_start(
                     out=v_s[scale_rows(q), a, :].bitcast(I32), in_=picked_s[row : row + 4, :].bitcast(I32)
                 )
@@ -135,37 +132,36 @@ def tile_list_uwb_range_correction_kernel(
                 nc.vector.tensor_copy(out=picked[:], in_=tab_w[a][:].bitcast(U32).indirect(entries))
                 v_w[a, half] = picked
 
-        def load_wb(name, a, c0, c1, offset):
-            rows = placed(name, [P, PACK, c1 - c0], F32, offset + WB_COL_BYTES * c0)
+        def load_wb(a, offset):
+            rows = placed("wb_raw%d" % a, [P, PACK, H], F32, offset)
             nc.sync.dma_start(
-                out=rows[:], in_=wb[K_PASS * a : K_PASS * (a + 1), c0:c1].rearrange("(p j) c -> p j c", j=PACK)
+                out=rows[:], in_=wb[K_PASS * a : K_PASS * (a + 1), :].rearrange("(p j) c -> p j c", j=PACK)
             )
-            return rows, c0, c1
+            return rows
 
-        wb_raw = [[load_wb("wb_raw0", 0, 0, H, WB0_AT)]]
+        wb_raw = [load_wb(0, WB0_AT)]
         nc.vector.tensor_copy(
             out=wa_s[:].rearrange("p a (t m) -> p a t m", t=PACK),
             in_=wa_s_raw[:].rearrange("p a (m t) -> p a t m", t=PACK),
         )
         gather_words(0)
-        wb_raw.append([load_wb("wb_raw1", 1, 0, WB_SPLIT, WB1_AT), load_wb("wb_last", 1, WB_SPLIT, H, WB1_AT)])
+        wb_raw.append(load_wb(1, WB1_AT))
         gain_sb = placed("gain_sb", [P, PACK], F32, GAIN_AT)
-        nc.sync.dma_start(out=gain_sb[:], in_=gain.rearrange("(p t) -> p t", t=PACK))
+        nc.gpsimd.dma_start(out=gain_sb[:], in_=gain.rearrange("(p t) -> p t", t=PACK))
         wh_raw = placed("wh_raw", [P, PACK, N], F32, WH_AT)
         nc.sync.dma_start(out=wh_raw[:], in_=wh.rearrange("(p j) c -> p j c", j=PACK))
+        wx_s = placed("wx_s", [P, PASSES, N], U8, WX_S_AT)
+        load_weight_scales(nc.gpsimd, wx_s, wx_scales)
         gather_words(1)
-
-        def load_conf(half):
-            rows = placed("conf%d" % half, [P, N_TILES, COLS], F32, CONF_AT[half])
-            nc.sync.dma_start(out=rows[:], in_=conf[:, half_cols(half)].rearrange("(n p) j -> p n j", p=P))
-            return rows
-
-        conf_sb = [load_conf(0)]
         wx_w = placed("wx_w", [P, PASSES, N], I32, WX_W_AT)
         nc.sync.dma_start(out=wx_w[:], in_=wx_words.rearrange("a p c i -> p a (c i)").bitcast(I32))
-        wx_s = placed("wx_s", [P, PASSES, N], U8, WX_S_AT)
-        nc.vector.memset(wx_s[:].bitcast(I32), 0)
-        load_weight_scales(wx_s, wx_scales)
+
+        conf_rows = conf.rearrange("(n p) j -> p n j", p=P)
+        conf_of = {}
+        for half in range(HALVES):
+            pair = placed("conf_pair%d" % half, [P, 2, COLS], F32, CONF_AT[half])
+            nc.sync.dma_start(out=pair[:], in_=conf_rows[:, 0:2, half_cols(half)])
+            conf_of[half, 0], conf_of[half, 1] = pair[:, 0, :], pair[:, 1, :]
 
         def times_v(acc, words, scales, a, half, start, stop):
             nc.tensor.matmul_mx(
@@ -198,10 +194,7 @@ def tile_list_uwb_range_correction_kernel(
         for a in range(PASSES):
             grouped = sbuf("wb_g%d" % a, [P, PACK * H], BF16)
             dealt = grouped[:].rearrange("p (t m j) -> p m t j", t=PACK, j=PACK)
-            for rows, c0, c1 in wb_raw[a]:
-                nc.vector.tensor_copy(
-                    out=dealt[:, c0 // PACK : c1 // PACK, :, :], in_=rows[:].rearrange("p j (m t) -> p m t j", t=PACK)
-                )
+            nc.vector.tensor_copy(out=dealt, in_=wb_raw[a][:].rearrange("p j (m t) -> p m t j", t=PACK))
             codes = sbuf("wb_w%d" % a, [P, H], U32)
             scales = sbuf("wb_s%d" % a, [P, H], U8)
             width = H // 2 if a == PASSES - 1 else H
@@ -213,7 +206,10 @@ def tile_list_uwb_range_correction_kernel(
             wb_w.append(codes)
             wb_s.append(scales)
 
-        conf_sb.append(load_conf(1))
+        conf_last = placed("conf_last", [P, S], F32, CONF_AT[2])
+        nc.sync.dma_start(out=conf_last[:], in_=conf_rows[:, 2, :])
+        for half in range(HALVES):
+            conf_of[half, 2] = conf_last[:, half_cols(half)]
 
         def wb_pass(acc, half, t, a):
             words = wb_w[a][:, tile_cols(t)].bitcast(FP8X4)
@@ -261,37 +257,25 @@ def tile_list_uwb_range_correction_kernel(
         interleave(nc.vector.tensor_copy, wh_g[:], wh_raw[:])
         nc.vector.quantize_mx(out=wh_w[:].bitcast(FP8X4), scales=wh_s[:], in_=wh_g[:])
 
-        def quarter_cols(q):
-            return slice(q * QCOLS, (q + 1) * QCOLS)
+        h_g = [sbuf("h_g%d" % half, [P, PACK * COLS], BF16) for half in range(HALVES)]
 
-        def in_half(q):
-            half, c0 = divmod(q * QCOLS, COLS)
-            return half, slice(c0, c0 + QCOLS)
-
-        def quantize_h(q):
-            half, cols = in_half(q)
-            grouped = sbuf("h_g%d" % q, [P, PACK * QCOLS], BF16)
-            interleave(nc.scalar.copy, grouped[:], h_sb[half][:, :, cols])
-            nc.vector.quantize_mx(
-                out=h_w[half][:, cols].bitcast(FP8X4), scales=h_s[:, quarter_cols(q)], in_=grouped[:]
+        def quantize_h(half):
+            nc.vector.quantize_mx(out=h_w[half][:].bitcast(FP8X4), scales=h_s[:, half_cols(half)], in_=h_g[half][:])
+            nc.sync.dma_start(
+                out=out_2[0, :, half_cols(half), :].rearrange("p m t -> p (m t)").bitcast(I32),
+                in_=h_w[half][:].bitcast(I32),
             )
-            if cols.stop == COLS:
-                nc.sync.dma_start(
-                    out=out_2[0, :, half_cols(half), :].rearrange("p m t -> p (m t)").bitcast(I32),
-                    in_=h_w[half][:].bitcast(I32),
-                )
 
         def wx_passes(acc, n, half, closes):
             for a in range(PASSES):
                 words = wx_w[:, a, tile_cols(n)].bitcast(FP8X4)
                 times_v(acc, words, wx_s[:, a, tile_cols(n)], a, half, a == 0, closes and a == PASSES - 1)
 
-        def wh_pass(acc, n, q):
-            half, cols = in_half(q)
+        def close_both(half, n):
             nc.tensor.matmul_mx(
-                out=acc[:, cols], lhsT=wh_w[:, tile_cols(n)].bitcast(FP8X4), lhsT_scale=wh_s[:, tile_cols(n)],
-                rhs=h_w[half][:, cols].bitcast(FP8X4), rhs_scale=h_s[:, quarter_cols(q)],
-                start=False, stop=cols.stop == COLS,
+                out=both_acc[half, n][:], lhsT=wh_w[:, tile_cols(n)].bitcast(FP8X4), lhsT_scale=wh_s[:, tile_cols(n)],
+                rhs=h_w[half][:].bitcast(FP8X4), rhs_scale=h_s[:, half_cols(half)],
+                start=False, stop=True,
             )
 
         both_acc, e_acc, weighted = {}, {}, {}
@@ -307,11 +291,11 @@ def tile_list_uwb_range_correction_kernel(
         def weigh(half, n):
             weighted[half, n] = sbuf("weighted%d%d" % (half, n), [P, COLS], F32)
             nc.vector.tensor_tensor(
-                out=weighted[half, n][:], in0=both_acc[half, n][:], in1=conf_sb[half][:, n, :], op=ALU.mult
+                out=weighted[half, n][:], in0=both_acc[half, n][:], in1=conf_of[half, n], op=ALU.mult
             )
 
-        def finish(half, n, engine, e_values):
-            y = sbuf("y%d%d" % (half, n), [P, COLS], F32)
+        def finish(half, n, engine, e_values, tag=None):
+            y = sbuf("y%d%d" % (half, n), [P, COLS], F32, tag=tag)
             engine.tensor_tensor(out=y[:], in0=weighted[half, n][:], in1=e_values, op=ALU.subtract)
             nc.sync.dma_start(out=out_0[tile_cols(n), half_cols(half)], in_=y[:])
 
@@ -322,44 +306,35 @@ def tile_list_uwb_range_correction_kernel(
         for n in range(N_TILES - 1):
             open_both(1, n)
 
-        def finish_on_gpsimd(half, n):
-            finish(half, n, nc.gpsimd, e_sb[half, n][:])
-
         def copy_e(half, n):
-            e_sb[half, n] = sbuf("e_sb%d%d" % (half, n), [P, COLS], F32)
-            nc.scalar.copy(out=e_sb[half, n][:], in_=e_acc[half, n][:])
+            values = sbuf("e_sb%d%d" % (half, n), [P, COLS], F32)
+            nc.scalar.copy(out=values[:], in_=e_acc[half, n][:])
+            return values[:]
 
-        def close_both(half):
-            first, second = HALVES * half, HALVES * half + 1
-            for n in range(N_TILES):
-                wh_pass(both_acc[half, n], n, first)
-            for n in range(N_TILES):
-                wh_pass(both_acc[half, n], n, second)
-
-        e_sb = {}
+        interleave(nc.scalar.copy, h_g[0][:, 0 : PACK * H_SPLIT], h_sb[0][:, :, 0:H_SPLIT])
+        interleave(nc.vector.tensor_copy, h_g[0][:, PACK * H_SPLIT : PACK * COLS], h_sb[0][:, :, H_SPLIT:COLS])
         quantize_h(0)
-        quantize_h(1)
-        copy_e(0, 1)
-        close_both(0)
+        interleave(nc.scalar.copy, h_g[1][:], h_sb[1][:])
         for n in range(N_TILES):
+            close_both(0, n)
+        for n in range(N_TILES - 1):
             weigh(0, n)
-        quantize_h(2)
-        quantize_h(3)
-        copy_e(0, 2)
+        quantize_h(1)
+        weigh(0, N_TILES - 1)
         finish(0, 0, nc.vector, e_acc[0, 0][:])
+        finish(0, 1, nc.gpsimd, copy_e(0, 1), tag="h_g1")
+        finish(0, 2, nc.gpsimd, copy_e(0, 2))
         open_both(1, N_TILES - 1)
-        close_both(1)
+        for n in range(N_TILES):
+            close_both(1, n)
         for n in range(N_TILES):
             e_passes(1, n)
-        copy_e(1, 0)
+        weigh(1, 0)
+        finish(1, 0, nc.gpsimd, copy_e(1, 0))
         for q in range(QUADS):
             nc.scalar.dma_start(
                 out=out_3[0, 4 * q : 4 * q + 4, :].bitcast(I32), in_=h_s[scale_rows(q), :].bitcast(I32)
             )
-        finish_on_gpsimd(0, 1)
-        finish_on_gpsimd(0, 2)
-        weigh(1, 0)
-        finish_on_gpsimd(1, 0)
         for n in range(1, N_TILES):
             weigh(1, n)
             finish(1, n, nc.vector, e_acc[1, n][:])

@@ -30,6 +30,7 @@ LIST_ROWS = 16
 TAB_S_ROW = [96, 112]
 H_SPLIT = 256
 BANKS = 8
+E_BANKS = [[3, 4, 5], [3, 1, 2]]
 
 TAB_W_BYTES = 4 * T
 WB_COL_BYTES = 4 * PACK
@@ -147,11 +148,11 @@ def tile_list_uwb_range_correction_kernel(
         gather_words(0)
         wb_raw.append(load_wb(1, WB1_AT))
         gain_sb = placed("gain_sb", [P, PACK], F32, GAIN_AT)
-        nc.gpsimd.dma_start(out=gain_sb[:], in_=gain.rearrange("(p t) -> p t", t=PACK))
+        nc.sync.dma_start(out=gain_sb[:], in_=gain.rearrange("(p t) -> p t", t=PACK))
         wh_raw = placed("wh_raw", [P, PACK, N], F32, WH_AT)
         nc.sync.dma_start(out=wh_raw[:], in_=wh.rearrange("(p j) c -> p j c", j=PACK))
         wx_s = placed("wx_s", [P, PASSES, N], U8, WX_S_AT)
-        load_weight_scales(nc.gpsimd, wx_s, wx_scales)
+        load_weight_scales(nc.sync, wx_s, wx_scales)
         gather_words(1)
         wx_w = placed("wx_w", [P, PASSES, N], I32, WX_W_AT)
         nc.sync.dma_start(out=wx_w[:], in_=wx_words.rearrange("a p c i -> p a (c i)").bitcast(I32))
@@ -248,9 +249,6 @@ def tile_list_uwb_range_correction_kernel(
         exp_stage(0)
         tanh_stage(1)
         exp_stage(1)
-        for half in range(HALVES):
-            code_stage(half)
-
         wh_g = sbuf("wh_g", [P, PACK * N], BF16)
         wh_w = sbuf("wh_w", [P, N], U32)
         wh_s = sbuf("wh_s", [P, N], U8)
@@ -285,7 +283,7 @@ def tile_list_uwb_range_correction_kernel(
             wx_passes(both_acc[half, n], n, half, False)
 
         def e_passes(half, n):
-            e_acc[half, n] = bank((2 * N_TILES * half + N_TILES + n) % BANKS)
+            e_acc[half, n] = bank(E_BANKS[half][n])
             wx_passes(e_acc[half, n], n, half, True)
 
         def weigh(half, n):
@@ -301,8 +299,7 @@ def tile_list_uwb_range_correction_kernel(
 
         for n in range(N_TILES):
             open_both(0, n)
-        for n in range(N_TILES):
-            e_passes(0, n)
+        e_passes(0, 0)
         for n in range(N_TILES - 1):
             open_both(1, n)
 
@@ -311,23 +308,32 @@ def tile_list_uwb_range_correction_kernel(
             nc.scalar.copy(out=values[:], in_=e_acc[half, n][:])
             return values[:]
 
+        code_stage(0)
         interleave(nc.scalar.copy, h_g[0][:, 0 : PACK * H_SPLIT], h_sb[0][:, :, 0:H_SPLIT])
         interleave(nc.vector.tensor_copy, h_g[0][:, PACK * H_SPLIT : PACK * COLS], h_sb[0][:, :, H_SPLIT:COLS])
         quantize_h(0)
-        interleave(nc.scalar.copy, h_g[1][:], h_sb[1][:])
+        code_stage(1)
+        e_first = copy_e(0, 0)
+        for t0 in range(0, PACK, 2):
+            nc.scalar.copy(
+                out=h_g[1][:].rearrange("p (c i t) -> p c t i", i=4, t=PACK)[:, :, t0 : t0 + 2, :],
+                in_=h_sb[1][:, t0 : t0 + 2, :].rearrange("p t (c i) -> p c t i", i=4),
+            )
         for n in range(N_TILES):
             close_both(0, n)
-        for n in range(N_TILES - 1):
+        for n in (2, 1):
+            e_passes(0, n)
+        for n in range(N_TILES):
             weigh(0, n)
         quantize_h(1)
-        weigh(0, N_TILES - 1)
-        finish(0, 0, nc.vector, e_acc[0, 0][:])
+        finish(0, 0, nc.gpsimd, e_first)
         finish(0, 1, nc.gpsimd, copy_e(0, 1), tag="h_g1")
-        finish(0, 2, nc.gpsimd, copy_e(0, 2))
+        finish(0, 2, nc.vector, e_acc[0, 2][:])
         open_both(1, N_TILES - 1)
+        e_passes(1, 0)
         for n in range(N_TILES):
             close_both(1, n)
-        for n in range(N_TILES):
+        for n in range(1, N_TILES):
             e_passes(1, n)
         weigh(1, 0)
         finish(1, 0, nc.gpsimd, copy_e(1, 0))
@@ -337,4 +343,5 @@ def tile_list_uwb_range_correction_kernel(
             )
         for n in range(1, N_TILES):
             weigh(1, n)
+        for n in range(1, N_TILES):
             finish(1, n, nc.vector, e_acc[1, n][:])

@@ -28,9 +28,11 @@ SCALE_ROWS = 16
 LIST_ROWS = 16
 
 TAB_S_ROW = [96, 112]
-H_SPLIT = 256
-BANKS = 8
-E_BANKS = [[3, 4, 5], [3, 1, 2]]
+WB_SPLIT = 320
+A_BANKS = [[0, 1, 2, 3], [4, 5, 6, 0]]
+B_BANKS = [[0, 1, 2, 3], [4, 1, 2, 7]]
+BOTH_BANKS = [[5, 6, 3], [4, 1, 5]]
+E_BANKS = [[0, 7, 2], [6, 0, 3]]
 
 TAB_W_BYTES = 4 * T
 WB_COL_BYTES = 4 * PACK
@@ -38,12 +40,14 @@ WB0_AT = TAB_W_BYTES
 TAB_W_AT = [0, WB0_AT + WB_COL_BYTES * H]
 TAB_S_AT = TAB_W_AT[1] - T // 2
 WB1_AT = TAB_W_AT[0]
+TANH_AT = {(1, 1): WB1_AT, (1, 2): WB1_AT + 4 * COLS}
 WH_AT = WB1_AT + WB_COL_BYTES * H
 GAIN_AT = WH_AT + WB_COL_BYTES * N
 WX_S_AT = GAIN_AT + 64
 CONF_BYTES = 4 * S
 CONF_AT = [TAB_S_AT + CONF_BYTES, TAB_S_AT + 2 * CONF_BYTES, TAB_S_AT]
 WX_W_AT = TAB_S_AT + N_TILES * CONF_BYTES
+H_G1_AT = TAB_W_AT[1] + TAB_W_BYTES
 
 
 def tile_list_uwb_range_correction_kernel(
@@ -175,27 +179,34 @@ def tile_list_uwb_range_correction_kernel(
             words = wa_w[:, a, 2 * P * t : 2 * P * (t + 1)].bitcast(FP4X4)
             times_v(acc, words, wa_s[:, a, tile_cols(t)], a, half, a == 0, a == PASSES - 1)
 
-        a_acc = {}
-        tanh_a = [sbuf("tanh_a%d" % half, [P, PACK, COLS], F32) for half in range(HALVES)]
+        a_acc, tanh_a = {}, {}
+        tiles = [(half, t) for half in range(HALVES) for t in range(PACK)]
 
-        def tanh_stage(half):
-            for t in range(PACK):
-                nc.scalar.activation(out=tanh_a[half][:, t, :], in_=a_acc[half, t][:], func=ACT.Tanh)
+        def tanh_of(half, t):
+            name = "tanh_a%d%d" % (half, t)
+            if (half, t) in TANH_AT:
+                tanh_a[half, t] = placed(name, [P, COLS], F32, TANH_AT[half, t])
+            else:
+                tanh_a[half, t] = sbuf(name, [P, COLS], F32)
+            nc.scalar.activation(out=tanh_a[half, t][:], in_=a_acc[half, t][:], func=ACT.Tanh)
 
-        for half in range(HALVES):
-            for t in range(PACK):
-                a_acc[half, t] = bank(PACK * half + t)
-                wa_pass(a_acc[half, t], t, 0, half)
-        for half in range(HALVES):
-            for t in range(PACK):
-                wa_pass(a_acc[half, t], t, 1, half)
-        tanh_stage(0)
+        for half, t in tiles[:-1]:
+            a_acc[half, t] = bank(A_BANKS[half][t])
+            wa_pass(a_acc[half, t], t, 0, half)
+        for half, t in tiles[:-1]:
+            wa_pass(a_acc[half, t], t, 1, half)
+        for half, t in tiles[:PACK]:
+            tanh_of(half, t)
 
         wb_w, wb_s = [], []
         for a in range(PASSES):
             grouped = sbuf("wb_g%d" % a, [P, PACK * H], BF16)
             dealt = grouped[:].rearrange("p (t m j) -> p m t j", t=PACK, j=PACK)
-            nc.vector.tensor_copy(out=dealt, in_=wb_raw[a][:].rearrange("p j (m t) -> p m t j", t=PACK))
+            rows = wb_raw[a][:].rearrange("p j (m t) -> p m t j", t=PACK)
+            share = (H if a == 0 else WB_SPLIT) // PACK
+            nc.vector.tensor_copy(out=dealt[:, 0:share, :, :], in_=rows[:, 0:share, :, :])
+            if share < P:
+                nc.scalar.copy(out=dealt[:, share:P, :, :], in_=rows[:, share:P, :, :])
             codes = sbuf("wb_w%d" % a, [P, H], U32)
             scales = sbuf("wb_s%d" % a, [P, H], U8)
             width = H // 2 if a == PASSES - 1 else H
@@ -224,15 +235,15 @@ def tile_list_uwb_range_correction_kernel(
 
         def exp_stage(half):
             for t in range(PACK):
-                acc = bank(PACK * half + t)
+                acc = bank(B_BANKS[half][t])
                 for a in range(PASSES):
                     wb_pass(acc, half, t, a)
                 nc.scalar.activation(out=exp_b[half][:, t, :], in_=acc[:], func=ACT.Exp)
 
-        def code_stage(half):
-            for t in range(PACK):
+        def code_stage(half, planes=range(PACK)):
+            for t in planes:
                 nc.vector.scalar_tensor_tensor(
-                    out=h_sb[half][:, t, :], in0=tanh_a[half][:, t, :], scalar=gain_sb[:, t : t + 1],
+                    out=h_sb[half][:, t, :], in0=tanh_a[half, t][:], scalar=gain_sb[:, t : t + 1],
                     in1=exp_b[half][:, t, :], op0=ALU.mult, op1=ALU.mult,
                 )
                 if t % 2 == 1:
@@ -247,7 +258,12 @@ def tile_list_uwb_range_correction_kernel(
             )
 
         exp_stage(0)
-        tanh_stage(1)
+        half, t = tiles[-1]
+        a_acc[half, t] = bank(A_BANKS[half][t])
+        for a in range(PASSES):
+            wa_pass(a_acc[half, t], t, a, half)
+        for half, t in tiles[PACK:]:
+            tanh_of(half, t)
         exp_stage(1)
         wh_g = sbuf("wh_g", [P, PACK * N], BF16)
         wh_w = sbuf("wh_w", [P, N], U32)
@@ -255,7 +271,7 @@ def tile_list_uwb_range_correction_kernel(
         interleave(nc.vector.tensor_copy, wh_g[:], wh_raw[:])
         nc.vector.quantize_mx(out=wh_w[:].bitcast(FP8X4), scales=wh_s[:], in_=wh_g[:])
 
-        h_g = [sbuf("h_g%d" % half, [P, PACK * COLS], BF16) for half in range(HALVES)]
+        h_g = [sbuf("h_g0", [P, PACK * COLS], BF16), placed("h_g1", [P, PACK * COLS], BF16, H_G1_AT)]
 
         def quantize_h(half):
             nc.vector.quantize_mx(out=h_w[half][:].bitcast(FP8X4), scales=h_s[:, half_cols(half)], in_=h_g[half][:])
@@ -279,7 +295,7 @@ def tile_list_uwb_range_correction_kernel(
         both_acc, e_acc, weighted = {}, {}, {}
 
         def open_both(half, n):
-            both_acc[half, n] = bank((2 * N_TILES * half + n) % BANKS)
+            both_acc[half, n] = bank(BOTH_BANKS[half][n])
             wx_passes(both_acc[half, n], n, half, False)
 
         def e_passes(half, n):
@@ -292,8 +308,9 @@ def tile_list_uwb_range_correction_kernel(
                 out=weighted[half, n][:], in0=both_acc[half, n][:], in1=conf_of[half, n], op=ALU.mult
             )
 
-        def finish(half, n, engine, e_values, tag=None):
-            y = sbuf("y%d%d" % (half, n), [P, COLS], F32, tag=tag)
+        def finish(half, n, engine, e_values, offset=None):
+            name = "y%d%d" % (half, n)
+            y = sbuf(name, [P, COLS], F32) if offset is None else placed(name, [P, COLS], F32, offset)
             engine.tensor_tensor(out=y[:], in0=weighted[half, n][:], in1=e_values, op=ALU.subtract)
             nc.sync.dma_start(out=out_0[tile_cols(n), half_cols(half)], in_=y[:])
 
@@ -309,16 +326,20 @@ def tile_list_uwb_range_correction_kernel(
             return values[:]
 
         code_stage(0)
-        interleave(nc.scalar.copy, h_g[0][:, 0 : PACK * H_SPLIT], h_sb[0][:, :, 0:H_SPLIT])
-        interleave(nc.vector.tensor_copy, h_g[0][:, PACK * H_SPLIT : PACK * COLS], h_sb[0][:, :, H_SPLIT:COLS])
+        interleave(nc.vector.tensor_copy, h_g[0][:], h_sb[0][:])
+        code_stage(1, range(0, 1))
         quantize_h(0)
-        code_stage(1)
-        e_first = copy_e(0, 0)
-        for t0 in range(0, PACK, 2):
+        code_stage(1, range(1, PACK))
+
+        def interleave_pair(t0):
             nc.scalar.copy(
                 out=h_g[1][:].rearrange("p (c i t) -> p c t i", i=4, t=PACK)[:, :, t0 : t0 + 2, :],
                 in_=h_sb[1][:, t0 : t0 + 2, :].rearrange("p t (c i) -> p c t i", i=4),
             )
+
+        interleave_pair(0)
+        e_first = copy_e(0, 0)
+        interleave_pair(2)
         for n in range(N_TILES):
             close_both(0, n)
         for n in (2, 1):
@@ -327,21 +348,21 @@ def tile_list_uwb_range_correction_kernel(
             weigh(0, n)
         quantize_h(1)
         finish(0, 0, nc.gpsimd, e_first)
-        finish(0, 1, nc.gpsimd, copy_e(0, 1), tag="h_g1")
-        finish(0, 2, nc.vector, e_acc[0, 2][:])
+        finish(0, 1, nc.gpsimd, copy_e(0, 1), H_G1_AT)
+        finish(0, 2, nc.vector, e_acc[0, 2][:], H_G1_AT + 4 * COLS)
         open_both(1, N_TILES - 1)
-        e_passes(1, 0)
+        e_passes(1, 1)
         for n in range(N_TILES):
             close_both(1, n)
-        for n in range(1, N_TILES):
+        for n in (0, 2):
             e_passes(1, n)
-        weigh(1, 0)
-        finish(1, 0, nc.gpsimd, copy_e(1, 0))
         for q in range(QUADS):
-            nc.scalar.dma_start(
+            nc.sync.dma_start(
                 out=out_3[0, 4 * q : 4 * q + 4, :].bitcast(I32), in_=h_s[scale_rows(q), :].bitcast(I32)
             )
-        for n in range(1, N_TILES):
-            weigh(1, n)
-        for n in range(1, N_TILES):
-            finish(1, n, nc.vector, e_acc[1, n][:])
+        weigh(1, 0)
+        weigh(1, 1)
+        finish(1, 0, nc.vector, e_acc[1, 0][:])
+        finish(1, 1, nc.gpsimd, copy_e(1, 1))
+        weigh(1, 2)
+        finish(1, 2, nc.vector, e_acc[1, 2][:])

@@ -27,7 +27,10 @@ QUADS = 4
 SCALE_ROWS = 16
 LIST_ROWS = 16
 
-TAB_S_ROW = [96, 112]
+FIRST_ROW = P - PASSES * SCALE_ROWS
+WA_S_COL = S
+WX_S_COL = WA_S_COL + H
+ROW_BYTES = WX_S_COL + N
 WB_SPLIT = 320
 A_BANKS = [[0, 1, 2, 3], [4, 5, 6, 0]]
 B_BANKS = [[0, 1, 2, 3], [4, 1, 2, 7]]
@@ -38,15 +41,15 @@ TAB_W_BYTES = 4 * T
 WB_COL_BYTES = 4 * PACK
 WB0_AT = TAB_W_BYTES
 TAB_W_AT = [0, WB0_AT + WB_COL_BYTES * H]
-TAB_S_AT = TAB_W_AT[1] - T // 2
+PICKED_S_AT = TAB_W_AT[1] - S // 2
+CONF_FROM = TAB_W_AT[1] - T // 2
 WB1_AT = TAB_W_AT[0]
 TANH_AT = {(1, 1): WB1_AT, (1, 2): WB1_AT + 4 * COLS}
 WH_AT = WB1_AT + WB_COL_BYTES * H
 GAIN_AT = WH_AT + WB_COL_BYTES * N
-WX_S_AT = GAIN_AT + 64
-CONF_BYTES = 4 * S
-CONF_AT = [TAB_S_AT + CONF_BYTES, TAB_S_AT + 2 * CONF_BYTES, TAB_S_AT]
-WX_W_AT = TAB_S_AT + N_TILES * CONF_BYTES
+CONF_OUTER_AT = CONF_FROM
+CONF_MID_AT = CONF_OUTER_AT + 4 * 2 * S
+WX_W_AT = CONF_MID_AT + 4 * S
 H_G1_AT = TAB_W_AT[1] + TAB_W_BYTES
 
 
@@ -78,28 +81,26 @@ def tile_list_uwb_range_correction_kernel(
         def scale_rows(q):
             return slice(32 * q, 32 * q + 4)
 
-        def load_weight_scales(queue, dst, src):
-            for q in range(QUADS):
-                queue.dma_start(
-                    out=dst[scale_rows(q), :, :].bitcast(I32),
-                    in_=src[:, 4 * q : 4 * q + 4, :].rearrange("a r c -> r a c").bitcast(I32),
-                )
+        def load_scale_rows(dst, src):
+            nc.sync.dma_start(out=dst.bitcast(I32), in_=src.rearrange("a q c -> (a q) c").bitcast(I32))
 
+        tab_s = sbuf("tab_s", [P, T], U8)
+        wa_s_raw = sbuf("wa_s_raw", [P, H], U8)
+        staged = sbuf("staged", [P, ROW_BYTES], U8)
+        nc.vector.memset(wa_s_raw[0:FIRST_ROW, :].bitcast(I32), 0)
+        nc.vector.memset(tab_s[0:FIRST_ROW, :].bitcast(I32), 0)
+
+        load_scale_rows(wa_s_raw[FIRST_ROW:P, :], wa_scales)
         offsets = keep.tile([P, S // LIST_ROWS], U16, name="offsets")
         nc.sync.dma_start(offsets[:], offs)
-
-        tab_s = placed("tab_s", [P, T], U8, TAB_S_AT)
-        wa_s_raw = sbuf("wa_s_raw", [P, PASSES, H], U8)
-        v_s = sbuf("v_s", [P, PASSES, S], U8)
-        nc.vector.memset(wa_s_raw[:].bitcast(I32), 0)
-        nc.vector.memset(tab_s[0 : TAB_S_ROW[0], :].bitcast(I32), 0)
-
-        nc.sync.dma_start(
-            out=tab_s[TAB_S_ROW[0] : P, :].bitcast(I32), in_=tab_scales.rearrange("a q t -> (a q) t").bitcast(I32)
-        )
+        load_scale_rows(tab_s[FIRST_ROW:P, :], tab_scales)
+        load_scale_rows(staged[FIRST_ROW:P, WX_S_COL:ROW_BYTES], wx_scales)
         wa_raw = sbuf("wa_raw", [P, PASSES, 2 * H], U8)
         nc.sync.dma_start(out=wa_raw[:].bitcast(I32), in_=wa_words.rearrange("a p c -> p a c").bitcast(I32))
-        load_weight_scales(nc.sync, wa_s_raw, wa_scales)
+        nc.vector.tensor_copy(
+            out=staged[:, WA_S_COL:WX_S_COL].rearrange("p (t m) -> p t m", t=PACK),
+            in_=wa_s_raw[:].rearrange("p (m t) -> p t m", t=PACK),
+        )
 
         def load_table(a):
             words = placed("tab_w%d" % a, [P, T], I32, TAB_W_AT[a])
@@ -108,14 +109,17 @@ def tile_list_uwb_range_correction_kernel(
 
         tab_w = [load_table(0)]
 
-        picked_s = sbuf("picked_s", [P, S], U8)
+        picked_s = placed("picked_s", [P, S], U8, PICKED_S_AT)
         nc.vector.tensor_copy(out=picked_s[:], in_=tab_s[:].indirect(offsets[:]))
+        nc.vector.tensor_copy(out=staged[FIRST_ROW:P, 0:S].bitcast(I32), in_=picked_s[FIRST_ROW:P, :].bitcast(I32))
+        planes = sbuf("planes", [P, PASSES, ROW_BYTES], U8)
+        v_s, wa_s, wx_s = planes[:, :, 0:S], planes[:, :, WA_S_COL:WX_S_COL], planes[:, :, WX_S_COL:ROW_BYTES]
 
         def place_scales(a):
             for q in range(QUADS):
-                row = TAB_S_ROW[a] + 4 * q
+                row = FIRST_ROW + SCALE_ROWS * a + 4 * q
                 nc.sync.dma_start(
-                    out=v_s[scale_rows(q), a, :].bitcast(I32), in_=picked_s[row : row + 4, :].bitcast(I32)
+                    out=planes[scale_rows(q), a, :].bitcast(I32), in_=staged[row : row + 4, :].bitcast(I32)
                 )
 
         place_scales(0)
@@ -123,7 +127,6 @@ def tile_list_uwb_range_correction_kernel(
         place_scales(1)
 
         wa_w = sbuf("wa_w", [P, PASSES, 2 * H], U8)
-        wa_s = sbuf("wa_s", [P, PASSES, H], U8)
         nc.vector.tensor_copy(
             out=wa_w[:].bitcast(U16).rearrange("p a (t m) -> p a t m", t=PACK),
             in_=wa_raw[:].bitcast(U16).rearrange("p a (m t) -> p a t m", t=PACK),
@@ -145,18 +148,12 @@ def tile_list_uwb_range_correction_kernel(
             return rows
 
         wb_raw = [load_wb(0, WB0_AT)]
-        nc.vector.tensor_copy(
-            out=wa_s[:].rearrange("p a (t m) -> p a t m", t=PACK),
-            in_=wa_s_raw[:].rearrange("p a (m t) -> p a t m", t=PACK),
-        )
         gather_words(0)
         wb_raw.append(load_wb(1, WB1_AT))
         gain_sb = placed("gain_sb", [P, PACK], F32, GAIN_AT)
         nc.sync.dma_start(out=gain_sb[:], in_=gain.rearrange("(p t) -> p t", t=PACK))
         wh_raw = placed("wh_raw", [P, PACK, N], F32, WH_AT)
         nc.sync.dma_start(out=wh_raw[:], in_=wh.rearrange("(p j) c -> p j c", j=PACK))
-        wx_s = placed("wx_s", [P, PASSES, N], U8, WX_S_AT)
-        load_weight_scales(nc.sync, wx_s, wx_scales)
         gather_words(1)
         wx_w = placed("wx_w", [P, PASSES, N], I32, WX_W_AT)
         nc.sync.dma_start(out=wx_w[:], in_=wx_words.rearrange("a p c i -> p a (c i)").bitcast(I32))
@@ -164,9 +161,9 @@ def tile_list_uwb_range_correction_kernel(
         conf_rows = conf.rearrange("(n p) j -> p n j", p=P)
         conf_of = {}
         for half in range(HALVES):
-            pair = placed("conf_pair%d" % half, [P, 2, COLS], F32, CONF_AT[half])
-            nc.sync.dma_start(out=pair[:], in_=conf_rows[:, 0:2, half_cols(half)])
-            conf_of[half, 0], conf_of[half, 1] = pair[:, 0, :], pair[:, 1, :]
+            mid = placed("conf_mid%d" % half, [P, COLS], F32, CONF_MID_AT + 4 * COLS * half)
+            nc.sync.dma_start(out=mid[:], in_=conf_rows[:, 1, half_cols(half)])
+            conf_of[half, 1] = mid[:]
 
         def times_v(acc, words, scales, a, half, start, stop):
             nc.tensor.matmul_mx(
@@ -218,10 +215,11 @@ def tile_list_uwb_range_correction_kernel(
             wb_w.append(codes)
             wb_s.append(scales)
 
-        conf_last = placed("conf_last", [P, S], F32, CONF_AT[2])
-        nc.sync.dma_start(out=conf_last[:], in_=conf_rows[:, 2, :])
+        conf_outer = placed("conf_outer", [P, 2, S], F32, CONF_OUTER_AT)
+        nc.sync.dma_start(out=conf_outer[:], in_=conf_rows[:, 0:N_TILES:2, :])
         for half in range(HALVES):
-            conf_of[half, 2] = conf_last[:, half_cols(half)]
+            conf_of[half, 0] = conf_outer[:, 0, half_cols(half)]
+            conf_of[half, 2] = conf_outer[:, 1, half_cols(half)]
 
         def wb_pass(acc, half, t, a):
             words = wb_w[a][:, tile_cols(t)].bitcast(FP8X4)
@@ -229,7 +227,7 @@ def tile_list_uwb_range_correction_kernel(
 
         exp_b = [sbuf("exp_b%d" % half, [P, PACK, COLS], F32) for half in range(HALVES)]
         h_sb = [sbuf("h_sb%d" % half, [P, PACK, COLS], F32) for half in range(HALVES)]
-        h_w = [sbuf("h_w0", [P, COLS], U32), placed("h_w1", [P, COLS], U32, CONF_AT[0])]
+        h_w = [sbuf("h_w0", [P, COLS], U32), placed("h_w1", [P, COLS], U32, CONF_MID_AT)]
         h_s = sbuf("h_s", [P, S], U8)
         h_rows = out_1.rearrange("(p t) j -> p t j", t=PACK)
 

@@ -31,26 +31,23 @@ FIRST_ROW = P - PASSES * SCALE_ROWS
 WA_S_COL = S
 WX_S_COL = WA_S_COL + H
 ROW_BYTES = WX_S_COL + N
-WB_SPLIT = 320
-A_BANKS = [[0, 1, 2, 3], [4, 5, 6, 0]]
-B_BANKS = [[0, 1, 2, 3], [4, 1, 2, 7]]
-BOTH_BANKS = [[5, 6, 3], [4, 1, 5]]
-E_BANKS = [[0, 7, 2], [6, 0, 3]]
+H_SPLIT = 384
+A_BANKS = [[0, 1, 2, 3], [4, 5, 6, 7]]
+B_BANKS = [[0, 1, 2, 3], [4, 5, 0, 1]]
+BOTH_BANKS = [[6, 7, 2], [3, 4, 5]]
+E_BANKS = [[0, 1, 6], [2, 7, 4]]
 
 TAB_W_BYTES = 4 * T
 WB_COL_BYTES = 4 * PACK
 WB0_AT = TAB_W_BYTES
 TAB_W_AT = [0, WB0_AT + WB_COL_BYTES * H]
 PICKED_S_AT = TAB_W_AT[1] - S // 2
-CONF_FROM = TAB_W_AT[1] - T // 2
 WB1_AT = TAB_W_AT[0]
-TANH_AT = {(1, 1): WB1_AT, (1, 2): WB1_AT + 4 * COLS}
 WH_AT = WB1_AT + WB_COL_BYTES * H
 GAIN_AT = WH_AT + WB_COL_BYTES * N
-CONF_OUTER_AT = CONF_FROM
-CONF_MID_AT = CONF_OUTER_AT + 4 * 2 * S
-WX_W_AT = CONF_MID_AT + 4 * S
-H_G1_AT = TAB_W_AT[1] + TAB_W_BYTES
+CONF_AT = TAB_W_AT[1]
+WX_W_AT = CONF_AT + 4 * N_TILES * S
+EXP1_AT = TAB_W_AT[1] + TAB_W_BYTES
 
 
 def tile_list_uwb_range_correction_kernel(
@@ -158,12 +155,8 @@ def tile_list_uwb_range_correction_kernel(
         wx_w = placed("wx_w", [P, PASSES, N], I32, WX_W_AT)
         nc.sync.dma_start(out=wx_w[:], in_=wx_words.rearrange("a p c i -> p a (c i)").bitcast(I32))
 
-        conf_rows = conf.rearrange("(n p) j -> p n j", p=P)
-        conf_of = {}
-        for half in range(HALVES):
-            mid = placed("conf_mid%d" % half, [P, COLS], F32, CONF_MID_AT + 4 * COLS * half)
-            nc.sync.dma_start(out=mid[:], in_=conf_rows[:, 1, half_cols(half)])
-            conf_of[half, 1] = mid[:]
+        conf_sb = placed("conf_sb", [P, N_TILES, S], F32, CONF_AT)
+        nc.sync.dma_start(out=conf_sb[:], in_=conf.rearrange("(n p) j -> p n j", p=P))
 
         def times_v(acc, words, scales, a, half, start, stop):
             nc.tensor.matmul_mx(
@@ -180,19 +173,14 @@ def tile_list_uwb_range_correction_kernel(
         tiles = [(half, t) for half in range(HALVES) for t in range(PACK)]
 
         def tanh_of(half, t):
-            name = "tanh_a%d%d" % (half, t)
-            if (half, t) in TANH_AT:
-                tanh_a[half, t] = placed(name, [P, COLS], F32, TANH_AT[half, t])
-            else:
-                tanh_a[half, t] = sbuf(name, [P, COLS], F32)
+            tanh_a[half, t] = sbuf("tanh_a%d%d" % (half, t), [P, COLS], F32)
             nc.scalar.activation(out=tanh_a[half, t][:], in_=a_acc[half, t][:], func=ACT.Tanh)
 
-        for half, t in tiles[:-1]:
+        for half, t in tiles:
             a_acc[half, t] = bank(A_BANKS[half][t])
             wa_pass(a_acc[half, t], t, 0, half)
-        for half, t in tiles[:-1]:
+        for half, t in tiles:
             wa_pass(a_acc[half, t], t, 1, half)
-        for half, t in tiles[:PACK]:
             tanh_of(half, t)
 
         wb_w, wb_s = [], []
@@ -200,10 +188,7 @@ def tile_list_uwb_range_correction_kernel(
             grouped = sbuf("wb_g%d" % a, [P, PACK * H], BF16)
             dealt = grouped[:].rearrange("p (t m j) -> p m t j", t=PACK, j=PACK)
             rows = wb_raw[a][:].rearrange("p j (m t) -> p m t j", t=PACK)
-            share = (H if a == 0 else WB_SPLIT) // PACK
-            nc.vector.tensor_copy(out=dealt[:, 0:share, :, :], in_=rows[:, 0:share, :, :])
-            if share < P:
-                nc.scalar.copy(out=dealt[:, share:P, :, :], in_=rows[:, share:P, :, :])
+            nc.vector.tensor_copy(out=dealt, in_=rows)
             codes = sbuf("wb_w%d" % a, [P, H], U32)
             scales = sbuf("wb_s%d" % a, [P, H], U8)
             width = H // 2 if a == PASSES - 1 else H
@@ -215,19 +200,13 @@ def tile_list_uwb_range_correction_kernel(
             wb_w.append(codes)
             wb_s.append(scales)
 
-        conf_outer = placed("conf_outer", [P, 2, S], F32, CONF_OUTER_AT)
-        nc.sync.dma_start(out=conf_outer[:], in_=conf_rows[:, 0:N_TILES:2, :])
-        for half in range(HALVES):
-            conf_of[half, 0] = conf_outer[:, 0, half_cols(half)]
-            conf_of[half, 2] = conf_outer[:, 1, half_cols(half)]
-
         def wb_pass(acc, half, t, a):
             words = wb_w[a][:, tile_cols(t)].bitcast(FP8X4)
             times_v(acc, words, wb_s[a][:, tile_cols(t)], a, half, a == 0, a == PASSES - 1)
 
-        exp_b = [sbuf("exp_b%d" % half, [P, PACK, COLS], F32) for half in range(HALVES)]
+        exp_b = [sbuf("exp_b0", [P, PACK, COLS], F32), placed("exp_b1", [P, PACK, COLS], F32, EXP1_AT)]
         h_sb = [sbuf("h_sb%d" % half, [P, PACK, COLS], F32) for half in range(HALVES)]
-        h_w = [sbuf("h_w0", [P, COLS], U32), placed("h_w1", [P, COLS], U32, CONF_MID_AT)]
+        h_w = [sbuf("h_w%d" % half, [P, COLS], U32) for half in range(HALVES)]
         h_s = sbuf("h_s", [P, S], U8)
         h_rows = out_1.rearrange("(p t) j -> p t j", t=PACK)
 
@@ -238,8 +217,8 @@ def tile_list_uwb_range_correction_kernel(
                     wb_pass(acc, half, t, a)
                 nc.scalar.activation(out=exp_b[half][:, t, :], in_=acc[:], func=ACT.Exp)
 
-        def code_stage(half, planes=range(PACK)):
-            for t in planes:
+        def code_stage(half):
+            for t in range(PACK):
                 nc.vector.scalar_tensor_tensor(
                     out=h_sb[half][:, t, :], in0=tanh_a[half, t][:], scalar=gain_sb[:, t : t + 1],
                     in1=exp_b[half][:, t, :], op0=ALU.mult, op1=ALU.mult,
@@ -256,12 +235,6 @@ def tile_list_uwb_range_correction_kernel(
             )
 
         exp_stage(0)
-        half, t = tiles[-1]
-        a_acc[half, t] = bank(A_BANKS[half][t])
-        for a in range(PASSES):
-            wa_pass(a_acc[half, t], t, a, half)
-        for half, t in tiles[PACK:]:
-            tanh_of(half, t)
         exp_stage(1)
         wh_g = sbuf("wh_g", [P, PACK * N], BF16)
         wh_w = sbuf("wh_w", [P, N], U32)
@@ -269,7 +242,7 @@ def tile_list_uwb_range_correction_kernel(
         interleave(nc.vector.tensor_copy, wh_g[:], wh_raw[:])
         nc.vector.quantize_mx(out=wh_w[:].bitcast(FP8X4), scales=wh_s[:], in_=wh_g[:])
 
-        h_g = [sbuf("h_g0", [P, PACK * COLS], BF16), placed("h_g1", [P, PACK * COLS], BF16, H_G1_AT)]
+        h_g = [sbuf("h_g%d" % half, [P, PACK * COLS], BF16) for half in range(HALVES)]
 
         def quantize_h(half):
             nc.vector.quantize_mx(out=h_w[half][:].bitcast(FP8X4), scales=h_s[:, half_cols(half)], in_=h_g[half][:])
@@ -303,64 +276,50 @@ def tile_list_uwb_range_correction_kernel(
         def weigh(half, n):
             weighted[half, n] = sbuf("weighted%d%d" % (half, n), [P, COLS], F32)
             nc.vector.tensor_tensor(
-                out=weighted[half, n][:], in0=both_acc[half, n][:], in1=conf_of[half, n], op=ALU.mult
+                out=weighted[half, n][:], in0=both_acc[half, n][:], in1=conf_sb[:, n, half_cols(half)], op=ALU.mult
             )
 
-        def finish(half, n, engine, e_values, offset=None):
-            name = "y%d%d" % (half, n)
-            y = sbuf(name, [P, COLS], F32) if offset is None else placed(name, [P, COLS], F32, offset)
+        def finish(half, n, engine, e_values):
+            y = sbuf("y%d%d" % (half, n), [P, COLS], F32)
             engine.tensor_tensor(out=y[:], in0=weighted[half, n][:], in1=e_values, op=ALU.subtract)
             nc.sync.dma_start(out=out_0[tile_cols(n), half_cols(half)], in_=y[:])
 
-        for n in range(N_TILES):
-            open_both(0, n)
-        e_passes(0, 0)
-        for n in range(N_TILES - 1):
-            open_both(1, n)
-
         def copy_e(half, n):
-            values = sbuf("e_sb%d%d" % (half, n), [P, COLS], F32)
+            values = placed("e_sb%d%d" % (half, n), [P, COLS], F32, EXP1_AT + 4 * COLS * (n + half))
             nc.scalar.copy(out=values[:], in_=e_acc[half, n][:])
             return values[:]
 
+        for half in range(HALVES):
+            for n in range(N_TILES):
+                open_both(half, n)
+        e_passes(0, 0)
+        e_passes(0, 1)
         code_stage(0)
-        interleave(nc.vector.tensor_copy, h_g[0][:], h_sb[0][:])
-        code_stage(1, range(0, 1))
-        quantize_h(0)
-        code_stage(1, range(1, PACK))
-
-        def interleave_pair(t0):
-            nc.scalar.copy(
-                out=h_g[1][:].rearrange("p (c i t) -> p c t i", i=4, t=PACK)[:, :, t0 : t0 + 2, :],
-                in_=h_sb[1][:, t0 : t0 + 2, :].rearrange("p t (c i) -> p c t i", i=4),
-            )
-
-        interleave_pair(0)
-        e_first = copy_e(0, 0)
-        interleave_pair(2)
-        for n in range(N_TILES):
-            close_both(0, n)
-        for n in (2, 1):
-            e_passes(0, n)
-        for n in range(N_TILES):
-            weigh(0, n)
-        quantize_h(1)
-        finish(0, 0, nc.gpsimd, e_first)
-        finish(0, 1, nc.gpsimd, copy_e(0, 1), H_G1_AT)
-        finish(0, 2, nc.vector, e_acc[0, 2][:], H_G1_AT + 4 * COLS)
-        open_both(1, N_TILES - 1)
-        e_passes(1, 1)
-        for n in range(N_TILES):
-            close_both(1, n)
-        for n in (0, 2):
-            e_passes(1, n)
+        code_stage(1)
+        interleave(nc.scalar.copy, h_g[0][:], h_sb[0][:])
+        interleave(nc.vector.tensor_copy, h_g[1][:, 0 : PACK * H_SPLIT], h_sb[1][:, :, 0:H_SPLIT])
+        interleave(nc.scalar.copy, h_g[1][:, PACK * H_SPLIT : PACK * COLS], h_sb[1][:, :, H_SPLIT:COLS])
+        e_sb = {(0, n): copy_e(0, n) for n in (0, 1)}
+        for half in range(HALVES):
+            quantize_h(half)
+        for half in range(HALVES):
+            for n in range(N_TILES):
+                close_both(half, n)
         for q in range(QUADS):
             nc.sync.dma_start(
                 out=out_3[0, 4 * q : 4 * q + 4, :].bitcast(I32), in_=h_s[scale_rows(q), :].bitcast(I32)
             )
-        weigh(1, 0)
+        for n in (0, 1):
+            weigh(0, n)
+            finish(0, n, nc.gpsimd, e_sb[0, n])
+        e_passes(0, 2)
+        e_passes(1, 1)
+        weigh(0, 2)
+        finish(0, 2, nc.vector, e_acc[0, 2][:])
+        e_passes(1, 0)
         weigh(1, 1)
-        finish(1, 0, nc.vector, e_acc[1, 0][:])
         finish(1, 1, nc.gpsimd, copy_e(1, 1))
-        weigh(1, 2)
-        finish(1, 2, nc.vector, e_acc[1, 2][:])
+        e_passes(1, 2)
+        for n in (0, 2):
+            weigh(1, n)
+            finish(1, n, nc.vector, e_acc[1, n][:])

@@ -31,11 +31,11 @@ FIRST_ROW = P - PASSES * SCALE_ROWS
 WA_S_COL = S
 WX_S_COL = WA_S_COL + H
 ROW_BYTES = WX_S_COL + N
-H_SPLIT = 384
+H_SPLIT = [384, 256]
 A_BANKS = [[0, 1, 2, 3], [4, 5, 6, 7]]
 B_BANKS = [[0, 1, 2, 3], [4, 5, 0, 1]]
 BOTH_BANKS = [[6, 7, 2], [3, 4, 5]]
-E_BANKS = [[0, 1, 6], [2, 7, 4]]
+E_BANKS = [[6, 0, 1], [7, 2, 0]]
 
 TAB_W_BYTES = 4 * T
 WB_COL_BYTES = 4 * PACK
@@ -47,7 +47,6 @@ WH_AT = WB1_AT + WB_COL_BYTES * H
 GAIN_AT = WH_AT + WB_COL_BYTES * N
 CONF_AT = TAB_W_AT[1]
 WX_W_AT = CONF_AT + 4 * N_TILES * S
-EXP1_AT = TAB_W_AT[1] + TAB_W_BYTES
 
 
 def tile_list_uwb_range_correction_kernel(
@@ -204,7 +203,7 @@ def tile_list_uwb_range_correction_kernel(
             words = wb_w[a][:, tile_cols(t)].bitcast(FP8X4)
             times_v(acc, words, wb_s[a][:, tile_cols(t)], a, half, a == 0, a == PASSES - 1)
 
-        exp_b = [sbuf("exp_b0", [P, PACK, COLS], F32), placed("exp_b1", [P, PACK, COLS], F32, EXP1_AT)]
+        exp_b = [sbuf("exp_b%d" % half, [P, PACK, COLS], F32) for half in range(HALVES)]
         h_sb = [sbuf("h_sb%d" % half, [P, PACK, COLS], F32) for half in range(HALVES)]
         h_w = [sbuf("h_w%d" % half, [P, COLS], U32) for half in range(HALVES)]
         h_s = sbuf("h_s", [P, S], U8)
@@ -273,34 +272,41 @@ def tile_list_uwb_range_correction_kernel(
             e_acc[half, n] = bank(E_BANKS[half][n])
             wx_passes(e_acc[half, n], n, half, True)
 
-        def weigh(half, n):
+        def weigh(half, n, engine, bracket):
             weighted[half, n] = sbuf("weighted%d%d" % (half, n), [P, COLS], F32)
-            nc.vector.tensor_tensor(
-                out=weighted[half, n][:], in0=both_acc[half, n][:], in1=conf_sb[:, n, half_cols(half)], op=ALU.mult
+            engine.tensor_tensor(
+                out=weighted[half, n][:], in0=bracket[:], in1=conf_sb[:, n, half_cols(half)], op=ALU.mult
             )
 
-        def finish(half, n, engine, e_values):
-            y = sbuf("y%d%d" % (half, n), [P, COLS], F32)
-            engine.tensor_tensor(out=y[:], in0=weighted[half, n][:], in1=e_values, op=ALU.subtract)
-            nc.sync.dma_start(out=out_0[tile_cols(n), half_cols(half)], in_=y[:])
+        def weigh_on_vector(half, n):
+            weigh(half, n, nc.vector, both_acc[half, n])
 
-        def copy_e(half, n):
-            values = placed("e_sb%d%d" % (half, n), [P, COLS], F32, EXP1_AT + 4 * COLS * (n + half))
-            nc.scalar.copy(out=values[:], in_=e_acc[half, n][:])
-            return values[:]
+        def weigh_on_gpsimd(half, n):
+            bracket = sbuf("bracket%d%d" % (half, n), [P, COLS], F32)
+            nc.scalar.copy(out=bracket[:], in_=both_acc[half, n][:])
+            weigh(half, n, nc.gpsimd, bracket)
+
+        def finish(half, n, pieces=1):
+            width = COLS // pieces
+            for c0 in range(0, COLS, width):
+                y = sbuf("y%d%d_%d" % (half, n, c0), [P, width], F32)
+                nc.vector.tensor_tensor(
+                    out=y[:], in0=weighted[half, n][:, c0 : c0 + width], in1=e_acc[half, n][:, c0 : c0 + width],
+                    op=ALU.subtract,
+                )
+                nc.sync.dma_start(out=out_0[tile_cols(n), half * COLS + c0 : half * COLS + c0 + width], in_=y[:])
 
         for half in range(HALVES):
             for n in range(N_TILES):
                 open_both(half, n)
-        e_passes(0, 0)
         e_passes(0, 1)
+        e_passes(0, 2)
         code_stage(0)
         code_stage(1)
-        interleave(nc.scalar.copy, h_g[0][:], h_sb[0][:])
-        interleave(nc.vector.tensor_copy, h_g[1][:, 0 : PACK * H_SPLIT], h_sb[1][:, :, 0:H_SPLIT])
-        interleave(nc.scalar.copy, h_g[1][:, PACK * H_SPLIT : PACK * COLS], h_sb[1][:, :, H_SPLIT:COLS])
-        e_sb = {(0, n): copy_e(0, n) for n in (0, 1)}
         for half in range(HALVES):
+            split = H_SPLIT[half]
+            interleave(nc.scalar.copy, h_g[half][:, 0 : PACK * split], h_sb[half][:, :, 0:split])
+            interleave(nc.vector.tensor_copy, h_g[half][:, PACK * split : PACK * COLS], h_sb[half][:, :, split:COLS])
             quantize_h(half)
         for half in range(HALVES):
             for n in range(N_TILES):
@@ -309,17 +315,17 @@ def tile_list_uwb_range_correction_kernel(
             nc.sync.dma_start(
                 out=out_3[0, 4 * q : 4 * q + 4, :].bitcast(I32), in_=h_s[scale_rows(q), :].bitcast(I32)
             )
+        weigh_on_gpsimd(0, 0)
+        for n in (1, 2):
+            weigh_on_vector(0, n)
+            finish(0, n)
         for n in (0, 1):
-            weigh(0, n)
-            finish(0, n, nc.gpsimd, e_sb[0, n])
-        e_passes(0, 2)
-        e_passes(1, 1)
-        weigh(0, 2)
-        finish(0, 2, nc.vector, e_acc[0, 2][:])
-        e_passes(1, 0)
-        weigh(1, 1)
-        finish(1, 1, nc.gpsimd, copy_e(1, 1))
-        e_passes(1, 2)
+            weigh_on_gpsimd(1, n)
+        e_passes(0, 0)
+        finish(0, 0)
+        for n in (0, 2, 1):
+            e_passes(1, n)
+        weigh_on_vector(1, 2)
         for n in (0, 2):
-            weigh(1, n)
-            finish(1, n, nc.vector, e_acc[1, n][:])
+            finish(1, n)
+        finish(1, 1, pieces=2)

@@ -35,7 +35,7 @@ H_SPLIT = [384, 256]
 A_BANKS = [[0, 1, 2, 3], [4, 5, 6, 7]]
 B_BANKS = [[0, 1, 2, 3], [4, 5, 0, 1]]
 BOTH_BANKS = [[6, 7, 2], [3, 4, 5]]
-E_BANKS = [[6, 0, 1], [7, 2, 0]]
+E_BANKS = [[7, 0, 1], [0, 1, 2]]
 
 TAB_W_BYTES = 4 * T
 WB_COL_BYTES = 4 * PACK
@@ -182,22 +182,26 @@ def tile_list_uwb_range_correction_kernel(
             wa_pass(a_acc[half, t], t, 1, half)
             tanh_of(half, t)
 
-        wb_w, wb_s = [], []
-        for a in range(PASSES):
-            grouped = sbuf("wb_g%d" % a, [P, PACK * H], BF16)
-            dealt = grouped[:].rearrange("p (t m j) -> p m t j", t=PACK, j=PACK)
+        wb_g = [sbuf("wb_g%d" % a, [P, PACK * H], BF16) for a in range(PASSES)]
+        wb_w = [sbuf("wb_w%d" % a, [P, H], U32) for a in range(PASSES)]
+        wb_s = [sbuf("wb_s%d" % a, [P, H], U8) for a in range(PASSES)]
+
+        def round_wb(a, t0, t1):
+            dealt = wb_g[a][:].rearrange("p (t m j) -> p m t j", t=PACK, j=PACK)
             rows = wb_raw[a][:].rearrange("p j (m t) -> p m t j", t=PACK)
-            nc.vector.tensor_copy(out=dealt, in_=rows)
-            codes = sbuf("wb_w%d" % a, [P, H], U32)
-            scales = sbuf("wb_s%d" % a, [P, H], U8)
-            width = H // 2 if a == PASSES - 1 else H
-            for c0 in range(0, H, width):
-                nc.vector.quantize_mx(
-                    out=codes[:, c0 : c0 + width].bitcast(FP8X4), scales=scales[:, c0 : c0 + width],
-                    in_=grouped[:, PACK * c0 : PACK * (c0 + width)],
-                )
-            wb_w.append(codes)
-            wb_s.append(scales)
+            nc.vector.tensor_copy(out=dealt[:, :, t0:t1, :], in_=rows[:, :, t0:t1, :])
+
+        def quantize_wb(a, t0, t1):
+            cols = slice(P * t0, P * t1)
+            nc.vector.quantize_mx(
+                out=wb_w[a][:, cols].bitcast(FP8X4), scales=wb_s[a][:, cols],
+                in_=wb_g[a][:, K_PASS * t0 : K_PASS * t1],
+            )
+
+        for a in range(PASSES):
+            for step in (round_wb, quantize_wb):
+                step(a, 0, 2)
+                step(a, 2, PACK)
 
         def wb_pass(acc, half, t, a):
             words = wb_w[a][:, tile_cols(t)].bitcast(FP8X4)
@@ -238,13 +242,26 @@ def tile_list_uwb_range_correction_kernel(
         wh_g = sbuf("wh_g", [P, PACK * N], BF16)
         wh_w = sbuf("wh_w", [P, N], U32)
         wh_s = sbuf("wh_s", [P, N], U8)
-        interleave(nc.vector.tensor_copy, wh_g[:], wh_raw[:])
-        nc.vector.quantize_mx(out=wh_w[:].bitcast(FP8X4), scales=wh_s[:], in_=wh_g[:])
+        wh_pieces = ((0, 2 * P), (2 * P, N))
+        for c0, c1 in wh_pieces:
+            interleave(nc.vector.tensor_copy, wh_g[:, PACK * c0 : PACK * c1], wh_raw[:, :, c0:c1])
+        for c0, c1 in wh_pieces:
+            nc.vector.quantize_mx(
+                out=wh_w[:, c0:c1].bitcast(FP8X4), scales=wh_s[:, c0:c1], in_=wh_g[:, PACK * c0 : PACK * c1]
+            )
 
         h_g = [sbuf("h_g%d" % half, [P, PACK * COLS], BF16) for half in range(HALVES)]
 
-        def quantize_h(half):
-            nc.vector.quantize_mx(out=h_w[half][:].bitcast(FP8X4), scales=h_s[:, half_cols(half)], in_=h_g[half][:])
+        def round_h(copy, half, c0, c1):
+            interleave(copy, h_g[half][:, PACK * c0 : PACK * c1], h_sb[half][:, :, c0:c1])
+
+        def quantize_h(half, c0, c1):
+            nc.vector.quantize_mx(
+                out=h_w[half][:, c0:c1].bitcast(FP8X4), scales=h_s[:, half * COLS + c0 : half * COLS + c1],
+                in_=h_g[half][:, PACK * c0 : PACK * c1],
+            )
+
+        def store_codes(half):
             nc.sync.dma_start(
                 out=out_2[0, :, half_cols(half), :].rearrange("p m t -> p (m t)").bitcast(I32),
                 in_=h_w[half][:].bitcast(I32),
@@ -303,18 +320,21 @@ def tile_list_uwb_range_correction_kernel(
         e_passes(0, 2)
         code_stage(0)
         code_stage(1)
-        for half in range(HALVES):
-            split = H_SPLIT[half]
-            interleave(nc.scalar.copy, h_g[half][:, 0 : PACK * split], h_sb[half][:, :, 0:split])
-            interleave(nc.vector.tensor_copy, h_g[half][:, PACK * split : PACK * COLS], h_sb[half][:, :, split:COLS])
-            quantize_h(half)
+        round_h(nc.scalar.copy, 0, 0, H_SPLIT[0])
+        round_h(nc.vector.tensor_copy, 0, H_SPLIT[0], COLS)
+        quantize_h(0, 0, H_SPLIT[0])
+        quantize_h(0, H_SPLIT[0], COLS)
+        store_codes(0)
+        round_h(nc.scalar.copy, 1, 0, H_SPLIT[1])
+        round_h(nc.vector.tensor_copy, 1, H_SPLIT[1], COLS)
+        quantize_h(1, 0, H_SPLIT[1])
+        quantize_h(1, H_SPLIT[1], COLS)
+        store_codes(1)
         for half in range(HALVES):
             for n in range(N_TILES):
                 close_both(half, n)
-        for q in range(QUADS):
-            nc.sync.dma_start(
-                out=out_3[0, 4 * q : 4 * q + 4, :].bitcast(I32), in_=h_s[scale_rows(q), :].bitcast(I32)
-            )
+        for r in range(4):
+            nc.sync.dma_start(out=out_3[0, r:SCALE_ROWS:4, :].bitcast(I32), in_=h_s[r:P:32, :].bitcast(I32))
         weigh_on_gpsimd(0, 0)
         for n in (1, 2):
             weigh_on_vector(0, n)

@@ -31,7 +31,7 @@ FIRST_ROW = P - PASSES * SCALE_ROWS
 WA_S_COL = S
 WX_S_COL = WA_S_COL + H
 ROW_BYTES = WX_S_COL + N
-H_SPLIT = [384, 256]
+H_SPLIT = [256, 256]
 A_BANKS = [[0, 1, 2, 3], [4, 5, 6, 7]]
 B_BANKS = [[0, 1, 2, 3], [4, 5, 0, 1]]
 BOTH_BANKS = [[6, 7, 2], [3, 4, 5]]

@@ -146,10 +146,10 @@ def tile_list_uwb_range_correction_kernel(
         wb_raw = [load_wb(0, WB0_AT)]
         gather_words(0)
         wb_raw.append(load_wb(1, WB1_AT))
-        gain_sb = placed("gain_sb", [P, PACK], F32, GAIN_AT)
-        nc.sync.dma_start(out=gain_sb[:], in_=gain.rearrange("(p t) -> p t", t=PACK))
         wh_raw = placed("wh_raw", [P, PACK, N], F32, WH_AT)
         nc.sync.dma_start(out=wh_raw[:], in_=wh.rearrange("(p j) c -> p j c", j=PACK))
+        gain_sb = placed("gain_sb", [P, PACK], F32, GAIN_AT)
+        nc.sync.dma_start(out=gain_sb[:], in_=gain.rearrange("(p t) -> p t", t=PACK))
         gather_words(1)
         wx_w = placed("wx_w", [P, PASSES, N], I32, WX_W_AT)
         nc.sync.dma_start(out=wx_w[:], in_=wx_words.rearrange("a p c i -> p a (c i)").bitcast(I32))

@@ -31,7 +31,7 @@ FIRST_ROW = P - PASSES * SCALE_ROWS
 WA_S_COL = S
 WX_S_COL = WA_S_COL + H
 ROW_BYTES = WX_S_COL + N
-H_SPLIT = [256, 256]
+H_SPLIT = 256
 A_BANKS = [[0, 1, 2, 3], [4, 5, 6, 7]]
 B_BANKS = [[0, 1, 2, 3], [4, 5, 0, 1]]
 BOTH_BANKS = [[6, 7, 2], [3, 4, 5]]
@@ -59,8 +59,8 @@ def tile_list_uwb_range_correction_kernel(
         reuse = ctx.enter_context(tc.tile_pool(name="reuse", bufs=1))
         psum = ctx.enter_context(tc.psum_pool(name="psum", bufs=1))
 
-        def sbuf(name, shape, dtype, tag=None):
-            return keep.tile(shape, dtype, name=name, tag=tag or name, align_bytes=64)
+        def sbuf(name, shape, dtype):
+            return keep.tile(shape, dtype, name=name, align_bytes=64)
 
         def placed(name, shape, dtype, offset):
             return reuse.tile(shape, dtype, name=name, offset=offset, align_bytes=64)
@@ -74,11 +74,8 @@ def tile_list_uwb_range_correction_kernel(
         def tile_cols(i):
             return slice(P * i, P * (i + 1))
 
-        def scale_rows(q):
-            return slice(32 * q, 32 * q + 4)
-
         def load_scale_rows(dst, src):
-            nc.sync.dma_start(out=dst.bitcast(I32), in_=src.rearrange("a q c -> (a q) c").bitcast(I32))
+            nc.sync.dma_start(out=dst.bitcast(I32), in_=src.rearrange("a q c -> q a c").bitcast(I32))
 
         tab_s = sbuf("tab_s", [P, T], U8)
         wa_s_raw = sbuf("wa_s_raw", [P, H], U8)
@@ -111,16 +108,13 @@ def tile_list_uwb_range_correction_kernel(
         planes = sbuf("planes", [P, PASSES, ROW_BYTES], U8)
         v_s, wa_s, wx_s = planes[:, :, 0:S], planes[:, :, WA_S_COL:WX_S_COL], planes[:, :, WX_S_COL:ROW_BYTES]
 
-        def place_scales(a):
-            for q in range(QUADS):
-                row = FIRST_ROW + SCALE_ROWS * a + 4 * q
-                nc.sync.dma_start(
-                    out=planes[scale_rows(q), a, :].bitcast(I32), in_=staged[row : row + 4, :].bitcast(I32)
-                )
-
-        place_scales(0)
+        for quad in (0, 2, 1, 3):
+            row = FIRST_ROW + 4 * PASSES * quad
+            nc.sync.dma_start(
+                out=planes[32 * quad : 32 * quad + 4, :, :].bitcast(I32),
+                in_=staged[row : row + 4 * PASSES, :].bitcast(I32),
+            )
         tab_w.append(load_table(1))
-        place_scales(1)
 
         wa_w = sbuf("wa_w", [P, PASSES, 2 * H], U8)
         nc.vector.tensor_copy(
@@ -153,7 +147,6 @@ def tile_list_uwb_range_correction_kernel(
         gather_words(1)
         wx_w = placed("wx_w", [P, PASSES, N], I32, WX_W_AT)
         nc.sync.dma_start(out=wx_w[:], in_=wx_words.rearrange("a p c i -> p a (c i)").bitcast(I32))
-
         conf_sb = placed("conf_sb", [P, N_TILES, S], F32, CONF_AT)
         nc.sync.dma_start(out=conf_sb[:], in_=conf.rearrange("(n p) j -> p n j", p=P))
 
@@ -171,16 +164,13 @@ def tile_list_uwb_range_correction_kernel(
         a_acc, tanh_a = {}, {}
         tiles = [(half, t) for half in range(HALVES) for t in range(PACK)]
 
-        def tanh_of(half, t):
-            tanh_a[half, t] = sbuf("tanh_a%d%d" % (half, t), [P, COLS], F32)
-            nc.scalar.activation(out=tanh_a[half, t][:], in_=a_acc[half, t][:], func=ACT.Tanh)
-
         for half, t in tiles:
             a_acc[half, t] = bank(A_BANKS[half][t])
             wa_pass(a_acc[half, t], t, 0, half)
         for half, t in tiles:
             wa_pass(a_acc[half, t], t, 1, half)
-            tanh_of(half, t)
+            tanh_a[half, t] = sbuf("tanh_a%d%d" % (half, t), [P, COLS], F32)
+            nc.scalar.activation(out=tanh_a[half, t][:], in_=a_acc[half, t][:], func=ACT.Tanh)
 
         wb_g = [sbuf("wb_g%d" % a, [P, PACK * H], BF16) for a in range(PASSES)]
         wb_w = [sbuf("wb_w%d" % a, [P, H], U32) for a in range(PASSES)]
@@ -198,38 +188,11 @@ def tile_list_uwb_range_correction_kernel(
                 in_=wb_g[a][:, K_PASS * t0 : K_PASS * t1],
             )
 
-        for a in range(PASSES):
-            for step in (round_wb, quantize_wb):
-                step(a, 0, 2)
-                step(a, 2, PACK)
-
-        def wb_pass(acc, half, t, a):
-            words = wb_w[a][:, tile_cols(t)].bitcast(FP8X4)
-            times_v(acc, words, wb_s[a][:, tile_cols(t)], a, half, a == 0, a == PASSES - 1)
-
         exp_b = [sbuf("exp_b%d" % half, [P, PACK, COLS], F32) for half in range(HALVES)]
         h_sb = [sbuf("h_sb%d" % half, [P, PACK, COLS], F32) for half in range(HALVES)]
         h_w = [sbuf("h_w%d" % half, [P, COLS], U32) for half in range(HALVES)]
         h_s = sbuf("h_s", [P, S], U8)
         h_rows = out_1.rearrange("(p t) j -> p t j", t=PACK)
-
-        def exp_stage(half):
-            for t in range(PACK):
-                acc = bank(B_BANKS[half][t])
-                for a in range(PASSES):
-                    wb_pass(acc, half, t, a)
-                nc.scalar.activation(out=exp_b[half][:, t, :], in_=acc[:], func=ACT.Exp)
-
-        def code_stage(half):
-            for t in range(PACK):
-                nc.vector.scalar_tensor_tensor(
-                    out=h_sb[half][:, t, :], in0=tanh_a[half, t][:], scalar=gain_sb[:, t : t + 1],
-                    in1=exp_b[half][:, t, :], op0=ALU.mult, op1=ALU.mult,
-                )
-                if t % 2 == 1:
-                    nc.sync.dma_start(
-                        out=h_rows[:, t - 1 : t + 1, half_cols(half)], in_=h_sb[half][:, t - 1 : t + 1, :]
-                    )
 
         def interleave(copy, dst, src):
             copy(
@@ -237,66 +200,92 @@ def tile_list_uwb_range_correction_kernel(
                 in_=src.rearrange("p t (c i) -> p c t i", i=4),
             )
 
-        exp_stage(0)
-        exp_stage(1)
         wh_g = sbuf("wh_g", [P, PACK * N], BF16)
         wh_w = sbuf("wh_w", [P, N], U32)
         wh_s = sbuf("wh_s", [P, N], U8)
-        wh_pieces = ((0, 2 * P), (2 * P, N))
-        for c0, c1 in wh_pieces:
-            interleave(nc.vector.tensor_copy, wh_g[:, PACK * c0 : PACK * c1], wh_raw[:, :, c0:c1])
-        for c0, c1 in wh_pieces:
+
+        def round_wh(copy, c0, c1):
+            interleave(copy, wh_g[:, PACK * c0 : PACK * c1], wh_raw[:, :, c0:c1])
+
+        def quantize_wh(c0, c1):
             nc.vector.quantize_mx(
                 out=wh_w[:, c0:c1].bitcast(FP8X4), scales=wh_s[:, c0:c1], in_=wh_g[:, PACK * c0 : PACK * c1]
             )
 
+        for a in range(PASSES):
+            for step in (round_wb, quantize_wb):
+                step(a, 0, 2)
+                step(a, 2, PACK)
+
+        for half, t in tiles:
+            acc = bank(B_BANKS[half][t])
+            for a in range(PASSES):
+                words = wb_w[a][:, tile_cols(t)].bitcast(FP8X4)
+                times_v(acc, words, wb_s[a][:, tile_cols(t)], a, half, a == 0, a == PASSES - 1)
+            nc.scalar.activation(out=exp_b[half][:, t, :], in_=acc[:], func=ACT.Exp)
+
+        wh_pieces = ((0, 2 * P), (2 * P, N))
+        for c0, c1 in wh_pieces:
+            round_wh(nc.vector.tensor_copy, c0, c1)
+        for c0, c1 in wh_pieces:
+            quantize_wh(c0, c1)
+
         h_g = [sbuf("h_g%d" % half, [P, PACK * COLS], BF16) for half in range(HALVES)]
-
-        def round_h(copy, half, c0, c1):
-            interleave(copy, h_g[half][:, PACK * c0 : PACK * c1], h_sb[half][:, :, c0:c1])
-
-        def quantize_h(half, c0, c1):
-            nc.vector.quantize_mx(
-                out=h_w[half][:, c0:c1].bitcast(FP8X4), scales=h_s[:, half * COLS + c0 : half * COLS + c1],
-                in_=h_g[half][:, PACK * c0 : PACK * c1],
-            )
-
-        def store_codes(half):
-            nc.sync.dma_start(
-                out=out_2[0, :, half_cols(half), :].rearrange("p m t -> p (m t)").bitcast(I32),
-                in_=h_w[half][:].bitcast(I32),
-            )
 
         def wx_passes(acc, n, half, closes):
             for a in range(PASSES):
                 words = wx_w[:, a, tile_cols(n)].bitcast(FP8X4)
                 times_v(acc, words, wx_s[:, a, tile_cols(n)], a, half, a == 0, closes and a == PASSES - 1)
 
-        def close_both(half, n):
-            nc.tensor.matmul_mx(
-                out=both_acc[half, n][:], lhsT=wh_w[:, tile_cols(n)].bitcast(FP8X4), lhsT_scale=wh_s[:, tile_cols(n)],
-                rhs=h_w[half][:].bitcast(FP8X4), rhs_scale=h_s[:, half_cols(half)],
-                start=False, stop=True,
-            )
-
         both_acc, e_acc, weighted = {}, {}, {}
-
-        def open_both(half, n):
-            both_acc[half, n] = bank(BOTH_BANKS[half][n])
-            wx_passes(both_acc[half, n], n, half, False)
 
         def e_passes(half, n):
             e_acc[half, n] = bank(E_BANKS[half][n])
             wx_passes(e_acc[half, n], n, half, True)
+
+        for half in range(HALVES):
+            for n in range(N_TILES):
+                both_acc[half, n] = bank(BOTH_BANKS[half][n])
+                wx_passes(both_acc[half, n], n, half, False)
+        e_passes(0, 1)
+        e_passes(0, 2)
+
+        for half, t in tiles:
+            nc.vector.scalar_tensor_tensor(
+                out=h_sb[half][:, t, :], in0=tanh_a[half, t][:], scalar=gain_sb[:, t : t + 1],
+                in1=exp_b[half][:, t, :], op0=ALU.mult, op1=ALU.mult,
+            )
+            if t % 2 == 1:
+                nc.sync.dma_start(out=h_rows[:, t - 1 : t + 1, half_cols(half)], in_=h_sb[half][:, t - 1 : t + 1, :])
+
+        for half in range(HALVES):
+            pieces = ((nc.scalar.copy, 0, H_SPLIT), (nc.vector.tensor_copy, H_SPLIT, COLS))
+            for copy, c0, c1 in pieces:
+                interleave(copy, h_g[half][:, PACK * c0 : PACK * c1], h_sb[half][:, :, c0:c1])
+            for copy, c0, c1 in pieces:
+                nc.vector.quantize_mx(
+                    out=h_w[half][:, c0:c1].bitcast(FP8X4), scales=h_s[:, half * COLS + c0 : half * COLS + c1],
+                    in_=h_g[half][:, PACK * c0 : PACK * c1],
+                )
+            nc.sync.dma_start(
+                out=out_2[0, :, half_cols(half), :].rearrange("p m t -> p (m t)").bitcast(I32),
+                in_=h_w[half][:].bitcast(I32),
+            )
+        for half in range(HALVES):
+            for n in range(N_TILES):
+                nc.tensor.matmul_mx(
+                    out=both_acc[half, n][:], lhsT=wh_w[:, tile_cols(n)].bitcast(FP8X4), lhsT_scale=wh_s[:, tile_cols(n)],
+                    rhs=h_w[half][:].bitcast(FP8X4), rhs_scale=h_s[:, half_cols(half)],
+                    start=False, stop=True,
+                )
+        for r in range(4):
+            nc.sync.dma_start(out=out_3[0, r:SCALE_ROWS:4, :].bitcast(I32), in_=h_s[r:P:32, :].bitcast(I32))
 
         def weigh(half, n, engine, bracket):
             weighted[half, n] = sbuf("weighted%d%d" % (half, n), [P, COLS], F32)
             engine.tensor_tensor(
                 out=weighted[half, n][:], in0=bracket[:], in1=conf_sb[:, n, half_cols(half)], op=ALU.mult
             )
-
-        def weigh_on_vector(half, n):
-            weigh(half, n, nc.vector, both_acc[half, n])
 
         def weigh_on_gpsimd(half, n):
             bracket = sbuf("bracket%d%d" % (half, n), [P, COLS], F32)
@@ -313,31 +302,9 @@ def tile_list_uwb_range_correction_kernel(
                 )
                 nc.sync.dma_start(out=out_0[tile_cols(n), half * COLS + c0 : half * COLS + c0 + width], in_=y[:])
 
-        for half in range(HALVES):
-            for n in range(N_TILES):
-                open_both(half, n)
-        e_passes(0, 1)
-        e_passes(0, 2)
-        code_stage(0)
-        code_stage(1)
-        round_h(nc.scalar.copy, 0, 0, H_SPLIT[0])
-        round_h(nc.vector.tensor_copy, 0, H_SPLIT[0], COLS)
-        quantize_h(0, 0, H_SPLIT[0])
-        quantize_h(0, H_SPLIT[0], COLS)
-        store_codes(0)
-        round_h(nc.scalar.copy, 1, 0, H_SPLIT[1])
-        round_h(nc.vector.tensor_copy, 1, H_SPLIT[1], COLS)
-        quantize_h(1, 0, H_SPLIT[1])
-        quantize_h(1, H_SPLIT[1], COLS)
-        store_codes(1)
-        for half in range(HALVES):
-            for n in range(N_TILES):
-                close_both(half, n)
-        for r in range(4):
-            nc.sync.dma_start(out=out_3[0, r:SCALE_ROWS:4, :].bitcast(I32), in_=h_s[r:P:32, :].bitcast(I32))
         weigh_on_gpsimd(0, 0)
         for n in (1, 2):
-            weigh_on_vector(0, n)
+            weigh(0, n, nc.vector, both_acc[0, n])
             finish(0, n)
         for n in (0, 1):
             weigh_on_gpsimd(1, n)
@@ -345,7 +312,7 @@ def tile_list_uwb_range_correction_kernel(
         finish(0, 0)
         for n in (0, 2, 1):
             e_passes(1, n)
-        weigh_on_vector(1, 2)
+        weigh(1, 2, nc.vector, both_acc[1, 2])
         for n in (0, 2):
             finish(1, n)
         finish(1, 1, pieces=2)

@@ -32,10 +32,12 @@ WA_S_COL = S
 WX_S_COL = WA_S_COL + H
 ROW_BYTES = WX_S_COL + N
 H_SPLIT = 256
+WB_SPLIT = 64
 A_BANKS = [[0, 1, 2, 3], [4, 5, 6, 7]]
-B_BANKS = [[0, 1, 2, 3], [4, 5, 0, 1]]
-BOTH_BANKS = [[6, 7, 2], [3, 4, 5]]
-E_BANKS = [[7, 0, 1], [0, 1, 2]]
+A_PIECES = [(0, 0, COLS // 2), (1, 0, COLS), (0, COLS // 2, COLS)]
+B_BANKS = [[4, 5, 6, 7], [0, 1, 4, 5]]
+BOTH_BANKS = [[2, 3, 6], [7, 0, 1]]
+E_BANKS = [[3, 4, 2], [4, 7, 6]]
 
 TAB_W_BYTES = 4 * T
 WB_COL_BYTES = 4 * PACK
@@ -123,12 +125,12 @@ def tile_list_uwb_range_correction_kernel(
         )
         v_w = {}
 
-        def gather_words(a):
+        def gather_words(a, pieces):
             for half in range(HALVES):
-                picked = sbuf("v_w%d%d" % (a, half), [P, COLS], U32)
-                entries = offsets[:, half * COLS // LIST_ROWS : (half + 1) * COLS // LIST_ROWS]
-                nc.vector.tensor_copy(out=picked[:], in_=tab_w[a][:].bitcast(U32).indirect(entries))
-                v_w[a, half] = picked
+                v_w[a, half] = sbuf("v_w%d%d" % (a, half), [P, COLS], U32)
+            for half, c0, c1 in pieces:
+                entries = offsets[:, (half * COLS + c0) // LIST_ROWS : (half * COLS + c1) // LIST_ROWS]
+                nc.vector.tensor_copy(out=v_w[a, half][:, c0:c1], in_=tab_w[a][:].bitcast(U32).indirect(entries))
 
         def load_wb(a, offset):
             rows = placed("wb_raw%d" % a, [P, PACK, H], F32, offset)
@@ -138,48 +140,56 @@ def tile_list_uwb_range_correction_kernel(
             return rows
 
         wb_raw = [load_wb(0, WB0_AT)]
-        gather_words(0)
+        gather_words(0, [(half, 0, COLS) for half in range(HALVES)])
         wb_raw.append(load_wb(1, WB1_AT))
         wh_raw = placed("wh_raw", [P, PACK, N], F32, WH_AT)
         nc.sync.dma_start(out=wh_raw[:], in_=wh.rearrange("(p j) c -> p j c", j=PACK))
         gain_sb = placed("gain_sb", [P, PACK], F32, GAIN_AT)
         nc.sync.dma_start(out=gain_sb[:], in_=gain.rearrange("(p t) -> p t", t=PACK))
-        gather_words(1)
+        gather_words(1, A_PIECES)
         wx_w = placed("wx_w", [P, PASSES, N], I32, WX_W_AT)
         nc.sync.dma_start(out=wx_w[:], in_=wx_words.rearrange("a p c i -> p a (c i)").bitcast(I32))
         conf_sb = placed("conf_sb", [P, N_TILES, S], F32, CONF_AT)
         nc.sync.dma_start(out=conf_sb[:], in_=conf.rearrange("(n p) j -> p n j", p=P))
 
-        def times_v(acc, words, scales, a, half, start, stop):
+        def times_v(acc, words, scales, a, half, start, stop, c0=0, c1=COLS):
             nc.tensor.matmul_mx(
-                out=acc[:], lhsT=words, lhsT_scale=scales,
-                rhs=v_w[a, half][:].bitcast(FP8X4), rhs_scale=v_s[:, a, half_cols(half)],
+                out=acc[:, c0:c1], lhsT=words, lhsT_scale=scales,
+                rhs=v_w[a, half][:, c0:c1].bitcast(FP8X4), rhs_scale=v_s[:, a, half * COLS + c0 : half * COLS + c1],
                 start=start, stop=stop,
             )
 
-        def wa_pass(acc, t, a, half):
+        def wa_pass(t, a, half, c0, c1):
             words = wa_w[:, a, 2 * P * t : 2 * P * (t + 1)].bitcast(FP4X4)
-            times_v(acc, words, wa_s[:, a, tile_cols(t)], a, half, a == 0, a == PASSES - 1)
+            times_v(a_acc[half, t], words, wa_s[:, a, tile_cols(t)], a, half, a == 0, a == PASSES - 1, c0, c1)
 
         a_acc, tanh_a = {}, {}
         tiles = [(half, t) for half in range(HALVES) for t in range(PACK)]
 
         for half, t in tiles:
             a_acc[half, t] = bank(A_BANKS[half][t])
-            wa_pass(a_acc[half, t], t, 0, half)
-        for half, t in tiles:
-            wa_pass(a_acc[half, t], t, 1, half)
             tanh_a[half, t] = sbuf("tanh_a%d%d" % (half, t), [P, COLS], F32)
-            nc.scalar.activation(out=tanh_a[half, t][:], in_=a_acc[half, t][:], func=ACT.Tanh)
+        for piece in A_PIECES[:2]:
+            for t in range(PACK):
+                wa_pass(t, 0, *piece)
+
+        def tanh_piece(passes, half, c0, c1):
+            for t in range(PACK):
+                for a in passes:
+                    wa_pass(t, a, half, c0, c1)
+                nc.scalar.activation(out=tanh_a[half, t][:, c0:c1], in_=a_acc[half, t][:, c0:c1], func=ACT.Tanh)
+
+        for piece in A_PIECES[:2]:
+            tanh_piece([1], *piece)
 
         wb_g = [sbuf("wb_g%d" % a, [P, PACK * H], BF16) for a in range(PASSES)]
         wb_w = [sbuf("wb_w%d" % a, [P, H], U32) for a in range(PASSES)]
         wb_s = [sbuf("wb_s%d" % a, [P, H], U8) for a in range(PASSES)]
 
-        def round_wb(a, t0, t1):
-            dealt = wb_g[a][:].rearrange("p (t m j) -> p m t j", t=PACK, j=PACK)
-            rows = wb_raw[a][:].rearrange("p j (m t) -> p m t j", t=PACK)
-            nc.vector.tensor_copy(out=dealt[:, :, t0:t1, :], in_=rows[:, :, t0:t1, :])
+        def round_wb(a, t0, t1, copy=nc.vector.tensor_copy, m0=0, m1=P):
+            dealt = wb_g[a][:].rearrange("p (t m j) -> p m j t", t=PACK, j=PACK)
+            rows = wb_raw[a][:].rearrange("p j (m t) -> p m j t", t=PACK)
+            copy(out=dealt[:, m0:m1, :, t0:t1], in_=rows[:, m0:m1, :, t0:t1])
 
         def quantize_wb(a, t0, t1):
             cols = slice(P * t0, P * t1)
@@ -212,10 +222,15 @@ def tile_list_uwb_range_correction_kernel(
                 out=wh_w[:, c0:c1].bitcast(FP8X4), scales=wh_s[:, c0:c1], in_=wh_g[:, PACK * c0 : PACK * c1]
             )
 
-        for a in range(PASSES):
-            for step in (round_wb, quantize_wb):
-                step(a, 0, 2)
-                step(a, 2, PACK)
+        for step in (round_wb, quantize_wb):
+            step(0, 0, 2)
+            step(0, 2, PACK)
+        round_wb(1, 2, PACK, nc.scalar.copy, m0=WB_SPLIT)
+        tanh_piece(range(PASSES), *A_PIECES[2])
+        round_wb(1, 0, 2)
+        round_wb(1, 2, PACK, m1=WB_SPLIT)
+        quantize_wb(1, 0, 2)
+        quantize_wb(1, 2, PACK)
 
         for half, t in tiles:
             acc = bank(B_BANKS[half][t])
@@ -248,7 +263,6 @@ def tile_list_uwb_range_correction_kernel(
                 both_acc[half, n] = bank(BOTH_BANKS[half][n])
                 wx_passes(both_acc[half, n], n, half, False)
         e_passes(0, 1)
-        e_passes(0, 2)
 
         for half, t in tiles:
             nc.vector.scalar_tensor_tensor(
@@ -281,11 +295,14 @@ def tile_list_uwb_range_correction_kernel(
         for r in range(4):
             nc.sync.dma_start(out=out_3[0, r:SCALE_ROWS:4, :].bitcast(I32), in_=h_s[r:P:32, :].bitcast(I32))
 
-        def weigh(half, n, engine, bracket):
+        def weigh(half, n, engine, bracket, pieces=1):
             weighted[half, n] = sbuf("weighted%d%d" % (half, n), [P, COLS], F32)
-            engine.tensor_tensor(
-                out=weighted[half, n][:], in0=bracket[:], in1=conf_sb[:, n, half_cols(half)], op=ALU.mult
-            )
+            width = COLS // pieces
+            for c0 in range(0, COLS, width):
+                engine.tensor_tensor(
+                    out=weighted[half, n][:, c0 : c0 + width], in0=bracket[:, c0 : c0 + width],
+                    in1=conf_sb[:, n, half * COLS + c0 : half * COLS + c0 + width], op=ALU.mult,
+                )
 
         def weigh_on_gpsimd(half, n):
             bracket = sbuf("bracket%d%d" % (half, n), [P, COLS], F32)
@@ -303,6 +320,7 @@ def tile_list_uwb_range_correction_kernel(
                 nc.sync.dma_start(out=out_0[tile_cols(n), half * COLS + c0 : half * COLS + c0 + width], in_=y[:])
 
         weigh_on_gpsimd(0, 0)
+        e_passes(0, 2)
         for n in (1, 2):
             weigh(0, n, nc.vector, both_acc[0, n])
             finish(0, n)
@@ -312,7 +330,7 @@ def tile_list_uwb_range_correction_kernel(
         finish(0, 0)
         for n in (0, 2, 1):
             e_passes(1, n)
-        weigh(1, 2, nc.vector, both_acc[1, 2])
-        for n in (0, 2):
-            finish(1, n)
+        finish(1, 0)
+        weigh(1, 2, nc.vector, both_acc[1, 2], pieces=2)
+        finish(1, 2, pieces=2)
         finish(1, 1, pieces=2)

@@ -29,8 +29,7 @@ LIST_ROWS = 16
 
 FIRST_ROW = P - PASSES * SCALE_ROWS
 WA_S_COL = S
-WX_S_COL = WA_S_COL + H
-ROW_BYTES = WX_S_COL + N
+ROW_BYTES = WA_S_COL + H
 H_SPLIT = 256
 WB_SPLIT = 64
 A_BANKS = [[0, 1, 2, 3], [4, 5, 6, 7]]
@@ -49,6 +48,7 @@ WH_AT = WB1_AT + WB_COL_BYTES * H
 GAIN_AT = WH_AT + WB_COL_BYTES * N
 CONF_AT = TAB_W_AT[1]
 WX_W_AT = CONF_AT + 4 * N_TILES * S
+WX_S_AT = WX_W_AT + 4 * PASSES * N
 
 
 def tile_list_uwb_range_correction_kernel(
@@ -85,15 +85,12 @@ def tile_list_uwb_range_correction_kernel(
         nc.vector.memset(wa_s_raw[0:FIRST_ROW, :].bitcast(I32), 0)
         nc.vector.memset(tab_s[0:FIRST_ROW, :].bitcast(I32), 0)
 
-        load_scale_rows(wa_s_raw[FIRST_ROW:P, :], wa_scales)
         offsets = keep.tile([P, S // LIST_ROWS], U16, name="offsets")
         nc.sync.dma_start(offsets[:], offs)
         load_scale_rows(tab_s[FIRST_ROW:P, :], tab_scales)
-        load_scale_rows(staged[FIRST_ROW:P, WX_S_COL:ROW_BYTES], wx_scales)
-        wa_raw = sbuf("wa_raw", [P, PASSES, 2 * H], U8)
-        nc.sync.dma_start(out=wa_raw[:].bitcast(I32), in_=wa_words.rearrange("a p c -> p a c").bitcast(I32))
+        load_scale_rows(wa_s_raw[FIRST_ROW:P, :], wa_scales)
         nc.vector.tensor_copy(
-            out=staged[:, WA_S_COL:WX_S_COL].rearrange("p (t m) -> p t m", t=PACK),
+            out=staged[:, WA_S_COL:ROW_BYTES].rearrange("p (t m) -> p t m", t=PACK),
             in_=wa_s_raw[:].rearrange("p (m t) -> p t m", t=PACK),
         )
 
@@ -103,12 +100,14 @@ def tile_list_uwb_range_correction_kernel(
             return words
 
         tab_w = [load_table(0)]
+        wa_raw = sbuf("wa_raw", [P, PASSES, 2 * H], U8)
+        nc.sync.dma_start(out=wa_raw[:].bitcast(I32), in_=wa_words.rearrange("a p c -> p a c").bitcast(I32))
 
         picked_s = placed("picked_s", [P, S], U8, PICKED_S_AT)
         nc.vector.tensor_copy(out=picked_s[:], in_=tab_s[:].indirect(offsets[:]))
         nc.vector.tensor_copy(out=staged[FIRST_ROW:P, 0:S].bitcast(I32), in_=picked_s[FIRST_ROW:P, :].bitcast(I32))
         planes = sbuf("planes", [P, PASSES, ROW_BYTES], U8)
-        v_s, wa_s, wx_s = planes[:, :, 0:S], planes[:, :, WA_S_COL:WX_S_COL], planes[:, :, WX_S_COL:ROW_BYTES]
+        v_s, wa_s = planes[:, :, 0:S], planes[:, :, WA_S_COL:ROW_BYTES]
 
         for quad in (0, 2, 1, 3):
             row = FIRST_ROW + 4 * PASSES * quad
@@ -147,6 +146,12 @@ def tile_list_uwb_range_correction_kernel(
         gain_sb = placed("gain_sb", [P, PACK], F32, GAIN_AT)
         nc.sync.dma_start(out=gain_sb[:], in_=gain.rearrange("(p t) -> p t", t=PACK))
         gather_words(1, A_PIECES)
+        wx_s = placed("wx_s", [P, N], U8, WX_S_AT)
+        for quad in (0, 2, 1, 3):
+            nc.sync.dma_start(
+                out=wx_s[32 * quad + 4 : 32 * quad + 12, :].bitcast(I32),
+                in_=wx_scales[:, 4 * quad : 4 * quad + 4, :].bitcast(I32),
+            )
         wx_w = placed("wx_w", [P, PASSES, N], I32, WX_W_AT)
         nc.sync.dma_start(out=wx_w[:], in_=wx_words.rearrange("a p c i -> p a (c i)").bitcast(I32))
         conf_sb = placed("conf_sb", [P, N_TILES, S], F32, CONF_AT)
@@ -250,7 +255,7 @@ def tile_list_uwb_range_correction_kernel(
         def wx_passes(acc, n, half, closes):
             for a in range(PASSES):
                 words = wx_w[:, a, tile_cols(n)].bitcast(FP8X4)
-                times_v(acc, words, wx_s[:, a, tile_cols(n)], a, half, a == 0, closes and a == PASSES - 1)
+                times_v(acc, words, wx_s[4 + 4 * a : P, tile_cols(n)], a, half, a == 0, closes and a == PASSES - 1)
 
         both_acc, e_acc, weighted = {}, {}, {}
 

@@ -85,6 +85,11 @@ def tile_list_uwb_range_correction_kernel(
         nc.vector.memset(wa_s_raw[0:FIRST_ROW, :].bitcast(I32), 0)
         nc.vector.memset(tab_s[0:FIRST_ROW, :].bitcast(I32), 0)
 
+        warm_in = sbuf("warm_in", [P, 16], F32)
+        warm_out = sbuf("warm_out", [P, 16], F32)
+        nc.gpsimd.memset(warm_in[:], 1.0)
+        nc.gpsimd.tensor_tensor(out=warm_out[:], in0=warm_in[:], in1=warm_in[:], op=ALU.mult)
+
         offsets = keep.tile([P, S // LIST_ROWS], U16, name="offsets")
         nc.sync.dma_start(offsets[:], offs)
         load_scale_rows(tab_s[FIRST_ROW:P, :], tab_scales)

@@ -32,11 +32,11 @@ WA_S_COL = S
 ROW_BYTES = WA_S_COL + H
 H_SPLIT = 256
 WB_SPLIT = 64
-A_BANKS = [[0, 1, 2, 3], [4, 5, 6, 7]]
 A_PIECES = [(0, 0, COLS // 2), (1, 0, COLS), (0, COLS // 2, COLS)]
-B_BANKS = [[4, 5, 6, 7], [0, 1, 4, 5]]
-BOTH_BANKS = [[2, 3, 6], [7, 0, 1]]
-E_BANKS = [[3, 4, 2], [4, 7, 6]]
+A_BANKS = [[0, 1], [2, 3, 4, 5], [6, 7]]
+EARLY_B = 6
+BOTH_BANKS = [[0, 1, 2], [3, 4, 5]]
+E_BANKS = [[0, 6, 7], [1, 3, 2]]
 
 TAB_W_BYTES = 4 * T
 WB_COL_BYTES = 4 * PACK
@@ -49,6 +49,7 @@ GAIN_AT = WH_AT + WB_COL_BYTES * N
 CONF_AT = TAB_W_AT[1]
 WX_W_AT = CONF_AT + 4 * N_TILES * S
 WX_S_AT = WX_W_AT + 4 * PASSES * N
+WA_RAW_AT = TAB_W_AT[1] + TAB_W_BYTES
 
 
 def tile_list_uwb_range_correction_kernel(
@@ -105,7 +106,7 @@ def tile_list_uwb_range_correction_kernel(
             return words
 
         tab_w = [load_table(0)]
-        wa_raw = sbuf("wa_raw", [P, PASSES, 2 * H], U8)
+        wa_raw = placed("wa_raw", [P, PASSES, 2 * H], U8, WA_RAW_AT)
         nc.sync.dma_start(out=wa_raw[:].bitcast(I32), in_=wa_words.rearrange("a p c -> p a c").bitcast(I32))
 
         picked_s = placed("picked_s", [P, S], U8, PICKED_S_AT)
@@ -131,7 +132,10 @@ def tile_list_uwb_range_correction_kernel(
 
         def gather_words(a, pieces):
             for half in range(HALVES):
-                v_w[a, half] = sbuf("v_w%d%d" % (a, half), [P, COLS], U32)
+                if (a, half) == (0, 1):
+                    v_w[a, half] = placed("v_w01", [P, COLS], U32, WA_RAW_AT)
+                else:
+                    v_w[a, half] = sbuf("v_w%d%d" % (a, half), [P, COLS], U32)
             for half, c0, c1 in pieces:
                 entries = offsets[:, (half * COLS + c0) // LIST_ROWS : (half * COLS + c1) // LIST_ROWS]
                 nc.vector.tensor_copy(out=v_w[a, half][:, c0:c1], in_=tab_w[a][:].bitcast(U32).indirect(entries))
@@ -169,28 +173,38 @@ def tile_list_uwb_range_correction_kernel(
                 start=start, stop=stop,
             )
 
-        def wa_pass(t, a, half, c0, c1):
-            words = wa_w[:, a, 2 * P * t : 2 * P * (t + 1)].bitcast(FP4X4)
-            times_v(a_acc[half, t], words, wa_s[:, a, tile_cols(t)], a, half, a == 0, a == PASSES - 1, c0, c1)
-
-        a_acc, tanh_a = {}, {}
+        tanh_a = [sbuf("tanh_a%d" % half, [P, PACK, COLS], F32) for half in range(HALVES)]
         tiles = [(half, t) for half in range(HALVES) for t in range(PACK)]
+        a_acc = [[bank(i) for i in banks] for banks in A_BANKS]
 
-        for half, t in tiles:
-            a_acc[half, t] = bank(A_BANKS[half][t])
-            tanh_a[half, t] = sbuf("tanh_a%d%d" % (half, t), [P, COLS], F32)
-        for piece in A_PIECES[:2]:
-            for t in range(PACK):
-                wa_pass(t, 0, *piece)
+        def wa_passes(piece, i, a):
+            half, c0, c1 = A_PIECES[piece]
+            width = c1 - c0
+            shared = COLS // width
+            for j in range(shared):
+                t = shared * i + j
+                nc.tensor.matmul_mx(
+                    out=a_acc[piece][i][:, j * width : (j + 1) * width],
+                    lhsT=wa_w[:, a, 2 * P * t : 2 * P * (t + 1)].bitcast(FP4X4), lhsT_scale=wa_s[:, a, tile_cols(t)],
+                    rhs=v_w[a, half][:, c0:c1].bitcast(FP8X4), rhs_scale=v_s[:, a, half * COLS + c0 : half * COLS + c1],
+                    start=a == 0 and j == 0, stop=a == PASSES - 1 and j == shared - 1,
+                )
 
-        def tanh_piece(passes, half, c0, c1):
-            for t in range(PACK):
-                for a in passes:
-                    wa_pass(t, a, half, c0, c1)
-                nc.scalar.activation(out=tanh_a[half, t][:, c0:c1], in_=a_acc[half, t][:, c0:c1], func=ACT.Tanh)
+        def tanh_piece(piece):
+            half, c0, c1 = A_PIECES[piece]
+            shared = COLS // (c1 - c0)
+            for i, acc in enumerate(a_acc[piece]):
+                wa_passes(piece, i, 1)
+                nc.scalar.activation(
+                    out=tanh_a[half][:, shared * i : shared * (i + 1), c0:c1],
+                    in_=acc[:].rearrange("p (j c) -> p j c", j=shared), func=ACT.Tanh,
+                )
 
-        for piece in A_PIECES[:2]:
-            tanh_piece([1], *piece)
+        for piece in (0, 2, 1):
+            for i in range(len(A_BANKS[piece])):
+                wa_passes(piece, i, 0)
+        for piece in (0, 1):
+            tanh_piece(piece)
 
         wb_g = [sbuf("wb_g%d" % a, [P, PACK * H], BF16) for a in range(PASSES)]
         wb_w = [sbuf("wb_w%d" % a, [P, H], U32) for a in range(PASSES)]
@@ -236,18 +250,27 @@ def tile_list_uwb_range_correction_kernel(
             step(0, 0, 2)
             step(0, 2, PACK)
         round_wb(1, 2, PACK, nc.scalar.copy, m0=WB_SPLIT)
-        tanh_piece(range(PASSES), *A_PIECES[2])
+        tanh_piece(2)
         round_wb(1, 0, 2)
         round_wb(1, 2, PACK, m1=WB_SPLIT)
         quantize_wb(1, 0, 2)
         quantize_wb(1, 2, PACK)
 
-        for half, t in tiles:
-            acc = bank(B_BANKS[half][t])
-            for a in range(PASSES):
-                words = wb_w[a][:, tile_cols(t)].bitcast(FP8X4)
-                times_v(acc, words, wb_s[a][:, tile_cols(t)], a, half, a == 0, a == PASSES - 1)
-            nc.scalar.activation(out=exp_b[half][:, t, :], in_=acc[:], func=ACT.Exp)
+        b_acc = {}
+
+        def wb_pass(i, a):
+            half, t = tiles[i]
+            if a == 0:
+                b_acc[i] = bank(i)
+            words = wb_w[a][:, tile_cols(t)].bitcast(FP8X4)
+            times_v(b_acc[i], words, wb_s[a][:, tile_cols(t)], a, half, a == 0, a == PASSES - 1)
+
+        for i in range(EARLY_B):
+            wb_pass(i, 0)
+        for i, (half, t) in enumerate(tiles):
+            for a in range(1 if i < EARLY_B else 0, PASSES):
+                wb_pass(i, a)
+            nc.scalar.activation(out=exp_b[half][:, t, :], in_=b_acc[i][:], func=ACT.Exp)
 
         wh_pieces = ((0, 2 * P), (2 * P, N))
         for c0, c1 in wh_pieces:
@@ -276,7 +299,7 @@ def tile_list_uwb_range_correction_kernel(
 
         for half, t in tiles:
             nc.vector.scalar_tensor_tensor(
-                out=h_sb[half][:, t, :], in0=tanh_a[half, t][:], scalar=gain_sb[:, t : t + 1],
+                out=h_sb[half][:, t, :], in0=tanh_a[half][:, t, :], scalar=gain_sb[:, t : t + 1],
                 in1=exp_b[half][:, t, :], op0=ALU.mult, op1=ALU.mult,
             )
             if t % 2 == 1:
@@ -302,6 +325,8 @@ def tile_list_uwb_range_correction_kernel(
                     rhs=h_w[half][:].bitcast(FP8X4), rhs_scale=h_s[:, half_cols(half)],
                     start=False, stop=True,
                 )
+            if half == 0:
+                e_passes(0, 2)
         for r in range(4):
             nc.sync.dma_start(out=out_3[0, r:SCALE_ROWS:4, :].bitcast(I32), in_=h_s[r:P:32, :].bitcast(I32))
 
@@ -330,13 +355,12 @@ def tile_list_uwb_range_correction_kernel(
                 nc.sync.dma_start(out=out_0[tile_cols(n), half * COLS + c0 : half * COLS + c0 + width], in_=y[:])
 
         weigh_on_gpsimd(0, 0)
-        e_passes(0, 2)
+        e_passes(0, 0)
         for n in (1, 2):
             weigh(0, n, nc.vector, both_acc[0, n])
             finish(0, n)
         for n in (0, 1):
             weigh_on_gpsimd(1, n)
-        e_passes(0, 0)
         finish(0, 0)
         for n in (0, 2, 1):
             e_passes(1, n)

@@ -31,6 +31,7 @@ FIRST_ROW = P - PASSES * SCALE_ROWS
 WA_S_COL = S
 ROW_BYTES = WA_S_COL + H
 H_SPLIT = 256
+PIECE_BYTES = 4096
 WB_SPLIT = 64
 A_PIECES = [(0, 0, COLS // 2), (1, 0, COLS), (0, COLS // 2, COLS)]
 A_BANKS = [[0, 1], [2, 3, 4, 5], [6, 7]]
@@ -102,7 +103,9 @@ def tile_list_uwb_range_correction_kernel(
 
         def load_table(a):
             words = placed("tab_w%d" % a, [P, T], I32, TAB_W_AT[a])
-            nc.sync.dma_start(out=words[:], in_=tab_words[a].rearrange("p t i -> p (t i)").bitcast(I32))
+            nc.sync.dma_start(
+                out=words[:], in_=tab_words[a].rearrange("p t i -> p (t i)").bitcast(I32), max_dma_last_dim=PIECE_BYTES
+            )
             return words
 
         tab_w = [load_table(0)]
@@ -143,7 +146,8 @@ def tile_list_uwb_range_correction_kernel(
         def load_wb(a, offset):
             rows = placed("wb_raw%d" % a, [P, PACK, H], F32, offset)
             nc.sync.dma_start(
-                out=rows[:], in_=wb[K_PASS * a : K_PASS * (a + 1), :].rearrange("(p j) c -> p j c", j=PACK)
+                out=rows[:], in_=wb[K_PASS * a : K_PASS * (a + 1), :].rearrange("(p j) c -> p j c", j=PACK),
+                max_dma_last_dim=PIECE_BYTES,
             )
             return rows
 
@@ -344,15 +348,12 @@ def tile_list_uwb_range_correction_kernel(
             nc.scalar.copy(out=bracket[:], in_=both_acc[half, n][:])
             weigh(half, n, nc.gpsimd, bracket)
 
-        def finish(half, n, pieces=1):
-            width = COLS // pieces
-            for c0 in range(0, COLS, width):
-                y = sbuf("y%d%d_%d" % (half, n, c0), [P, width], F32)
-                nc.vector.tensor_tensor(
-                    out=y[:], in0=weighted[half, n][:, c0 : c0 + width], in1=e_acc[half, n][:, c0 : c0 + width],
-                    op=ALU.subtract,
-                )
-                nc.sync.dma_start(out=out_0[tile_cols(n), half * COLS + c0 : half * COLS + c0 + width], in_=y[:])
+        def finish(half, n, c0=0, c1=COLS):
+            y = sbuf("y%d%d_%d" % (half, n, c0), [P, c1 - c0], F32)
+            nc.vector.tensor_tensor(
+                out=y[:], in0=weighted[half, n][:, c0:c1], in1=e_acc[half, n][:, c0:c1], op=ALU.subtract
+            )
+            nc.sync.dma_start(out=out_0[tile_cols(n), half * COLS + c0 : half * COLS + c1], in_=y[:])
 
         weigh_on_gpsimd(0, 0)
         e_passes(0, 0)
@@ -366,5 +367,6 @@ def tile_list_uwb_range_correction_kernel(
             e_passes(1, n)
         finish(1, 0)
         weigh(1, 2, nc.vector, both_acc[1, 2], pieces=2)
-        finish(1, 2, pieces=2)
-        finish(1, 1, pieces=2)
+        for n, cuts in ((2, (0, 256, 512)), (1, (0, 256, 384, 512))):
+            for c0, c1 in zip(cuts, cuts[1:]):
+                finish(1, n, c0, c1)

from contextlib import ExitStack

import concourse.mybir as mybir

K, H, N, T, S = 1024, 512, 384, 4096, 1024
FLOPS = 2 * S * (2 * K * H + 2 * K * N + H * N)

F32 = mybir.dt.float32
BF16 = mybir.dt.bfloat16
I32 = mybir.dt.int32
U32 = mybir.dt.uint32
U16 = mybir.dt.uint16
U8 = mybir.dt.uint8
FP8X4 = mybir.dt.float8_e4m3fn_x4
FP4X4 = mybir.dt.float4_e2m1fn_x4
ACT = mybir.ActivationFunctionType
ALU = mybir.AluOpType

P = 128
PACK = 4
K_PASS = P * PACK
PASSES = K // K_PASS
COLS = 512
HALVES = S // COLS
N_TILES = N // P
QUADS = 4
SCALE_ROWS = 16
LIST_ROWS = 16

FIRST_ROW = P - PASSES * SCALE_ROWS
WA_S_COL = S
ROW_BYTES = WA_S_COL + H
H_SPLIT = 256
PIECE_BYTES = 4096
WB_SPLIT = 64
A_PIECES = [(0, 0, COLS // 2), (1, 0, COLS), (0, COLS // 2, COLS)]
A_BANKS = [[0, 1], [2, 3, 4, 5], [6, 7]]
EARLY_B = 6
BOTH_BANKS = [[0, 1, 2], [3, 4, 5]]
E_BANKS = [[0, 6, 7], [1, 3, 2]]

TAB_W_BYTES = 4 * T
WB_COL_BYTES = 4 * PACK
WB0_AT = TAB_W_BYTES
TAB_W_AT = [0, WB0_AT + WB_COL_BYTES * H]
PICKED_S_AT = TAB_W_AT[1] - S // 2
WB1_AT = TAB_W_AT[0]
WH_AT = WB1_AT + WB_COL_BYTES * H
GAIN_AT = WH_AT + WB_COL_BYTES * N
CONF_AT = TAB_W_AT[1]
WX_W_AT = CONF_AT + 4 * N_TILES * S
WX_S_AT = WX_W_AT + 4 * PASSES * N
WA_RAW_AT = TAB_W_AT[1] + TAB_W_BYTES


def tile_list_uwb_range_correction_kernel(
    tc, tab_words, tab_scales, offs, wa_words, wa_scales, wb, gain, wh, wx_words, wx_scales, conf,
    out_0, out_1, out_2, out_3,
):
    nc = tc.nc
    with ExitStack() as ctx:
        keep = ctx.enter_context(tc.tile_pool(name="keep", bufs=1))
        reuse = ctx.enter_context(tc.tile_pool(name="reuse", bufs=1))
        psum = ctx.enter_context(tc.psum_pool(name="psum", bufs=1))

        def sbuf(name, shape, dtype):
            return keep.tile(shape, dtype, name=name, align_bytes=64)

        def placed(name, shape, dtype, offset):
            return reuse.tile(shape, dtype, name=name, offset=offset, align_bytes=64)

        def bank(i):
            return psum.tile([P, COLS], F32, name="bank%d" % i)

        def half_cols(half):
            return slice(half * COLS, (half + 1) * COLS)

        def tile_cols(i):
            return slice(P * i, P * (i + 1))

        def load_scale_rows(dst, src):
            nc.sync.dma_start(out=dst.bitcast(I32), in_=src.rearrange("a q c -> q a c").bitcast(I32))

        tab_s = sbuf("tab_s", [P, T], U8)
        wa_s_raw = sbuf("wa_s_raw", [P, H], U8)
        staged = sbuf("staged", [P, ROW_BYTES], U8)
        nc.vector.memset(wa_s_raw[0:FIRST_ROW, :].bitcast(I32), 0)
        nc.vector.memset(tab_s[0:FIRST_ROW, :].bitcast(I32), 0)

        warm_in = sbuf("warm_in", [P, 16], F32)
        warm_out = sbuf("warm_out", [P, 16], F32)
        nc.gpsimd.memset(warm_in[:], 1.0)
        nc.gpsimd.tensor_tensor(out=warm_out[:], in0=warm_in[:], in1=warm_in[:], op=ALU.mult)

        offsets = keep.tile([P, S // LIST_ROWS], U16, name="offsets")
        nc.sync.dma_start(offsets[:], offs)
        load_scale_rows(tab_s[FIRST_ROW:P, :], tab_scales)
        load_scale_rows(wa_s_raw[FIRST_ROW:P, :], wa_scales)
        nc.vector.tensor_copy(
            out=staged[:, WA_S_COL:ROW_BYTES].rearrange("p (t m) -> p t m", t=PACK),
            in_=wa_s_raw[:].rearrange("p (m t) -> p t m", t=PACK),
        )

        def load_table(a):
            words = placed("tab_w%d" % a, [P, T], I32, TAB_W_AT[a])
            nc.sync.dma_start(
                out=words[:], in_=tab_words[a].rearrange("p t i -> p (t i)").bitcast(I32), max_dma_last_dim=PIECE_BYTES
            )
            return words

        tab_w = [load_table(0)]
        wa_raw = placed("wa_raw", [P, PASSES, 2 * H], U8, WA_RAW_AT)
        nc.sync.dma_start(out=wa_raw[:].bitcast(I32), in_=wa_words.rearrange("a p c -> p a c").bitcast(I32))

        picked_s = placed("picked_s", [P, S], U8, PICKED_S_AT)
        nc.vector.tensor_copy(out=picked_s[:], in_=tab_s[:].indirect(offsets[:]))
        nc.vector.tensor_copy(out=staged[FIRST_ROW:P, 0:S].bitcast(I32), in_=picked_s[FIRST_ROW:P, :].bitcast(I32))
        planes = sbuf("planes", [P, PASSES, ROW_BYTES], U8)
        v_s, wa_s = planes[:, :, 0:S], planes[:, :, WA_S_COL:ROW_BYTES]

        for quad in (0, 2, 1, 3):
            row = FIRST_ROW + 4 * PASSES * quad
            nc.sync.dma_start(
                out=planes[32 * quad : 32 * quad + 4, :, :].bitcast(I32),
                in_=staged[row : row + 4 * PASSES, :].bitcast(I32),
            )
        tab_w.append(load_table(1))

        wa_w = sbuf("wa_w", [P, PASSES, 2 * H], U8)
        nc.vector.tensor_copy(
            out=wa_w[:].bitcast(U16).rearrange("p a (t m) -> p a t m", t=PACK),
            in_=wa_raw[:].bitcast(U16).rearrange("p a (m t) -> p a t m", t=PACK),
        )
        v_w = {}

        def gather_words(a, pieces):
            for half in range(HALVES):
                if (a, half) == (0, 1):
                    v_w[a, half] = placed("v_w01", [P, COLS], U32, WA_RAW_AT)
                else:
                    v_w[a, half] = sbuf("v_w%d%d" % (a, half), [P, COLS], U32)
            for half, c0, c1 in pieces:
                entries = offsets[:, (half * COLS + c0) // LIST_ROWS : (half * COLS + c1) // LIST_ROWS]
                nc.vector.tensor_copy(out=v_w[a, half][:, c0:c1], in_=tab_w[a][:].bitcast(U32).indirect(entries))

        def load_wb(a, offset):
            rows = placed("wb_raw%d" % a, [P, PACK, H], F32, offset)
            nc.sync.dma_start(
                out=rows[:], in_=wb[K_PASS * a : K_PASS * (a + 1), :].rearrange("(p j) c -> p j c", j=PACK),
                max_dma_last_dim=PIECE_BYTES,
            )
            return rows

        wb_raw = [load_wb(0, WB0_AT)]
        gather_words(0, [(half, 0, COLS) for half in range(HALVES)])
        wb_raw.append(load_wb(1, WB1_AT))
        wh_raw = placed("wh_raw", [P, PACK, N], F32, WH_AT)
        nc.sync.dma_start(out=wh_raw[:], in_=wh.rearrange("(p j) c -> p j c", j=PACK))
        gain_sb = placed("gain_sb", [P, PACK], F32, GAIN_AT)
        nc.sync.dma_start(out=gain_sb[:], in_=gain.rearrange("(p t) -> p t", t=PACK))
        gather_words(1, A_PIECES)
        wx_s = placed("wx_s", [P, N], U8, WX_S_AT)
        for quad in (0, 2, 1, 3):
            nc.sync.dma_start(
                out=wx_s[32 * quad + 4 : 32 * quad + 12, :].bitcast(I32),
                in_=wx_scales[:, 4 * quad : 4 * quad + 4, :].bitcast(I32),
            )
        wx_w = placed("wx_w", [P, PASSES, N], I32, WX_W_AT)
        nc.sync.dma_start(out=wx_w[:], in_=wx_words.rearrange("a p c i -> p a (c i)").bitcast(I32))
        conf_sb = placed("conf_sb", [P, N_TILES, S], F32, CONF_AT)
        nc.sync.dma_start(out=conf_sb[:], in_=conf.rearrange("(n p) j -> p n j", p=P))

        def times_v(acc, words, scales, a, half, start, stop, c0=0, c1=COLS):
            nc.tensor.matmul_mx(
                out=acc[:, c0:c1], lhsT=words, lhsT_scale=scales,
                rhs=v_w[a, half][:, c0:c1].bitcast(FP8X4), rhs_scale=v_s[:, a, half * COLS + c0 : half * COLS + c1],
                start=start, stop=stop,
            )

        tanh_a = [sbuf("tanh_a%d" % half, [P, PACK, COLS], F32) for half in range(HALVES)]
        tiles = [(half, t) for half in range(HALVES) for t in range(PACK)]
        a_acc = [[bank(i) for i in banks] for banks in A_BANKS]

        def wa_passes(piece, i, a):
            half, c0, c1 = A_PIECES[piece]
            width = c1 - c0
            shared = COLS // width
            for j in range(shared):
                t = shared * i + j
                nc.tensor.matmul_mx(
                    out=a_acc[piece][i][:, j * width : (j + 1) * width],
                    lhsT=wa_w[:, a, 2 * P * t : 2 * P * (t + 1)].bitcast(FP4X4), lhsT_scale=wa_s[:, a, tile_cols(t)],
                    rhs=v_w[a, half][:, c0:c1].bitcast(FP8X4), rhs_scale=v_s[:, a, half * COLS + c0 : half * COLS + c1],
                    start=a == 0 and j == 0, stop=a == PASSES - 1 and j == shared - 1,
                )

        def tanh_piece(piece):
            half, c0, c1 = A_PIECES[piece]
            shared = COLS // (c1 - c0)
            for i, acc in enumerate(a_acc[piece]):
                wa_passes(piece, i, 1)
                nc.scalar.activation(
                    out=tanh_a[half][:, shared * i : shared * (i + 1), c0:c1],
                    in_=acc[:].rearrange("p (j c) -> p j c", j=shared), func=ACT.Tanh,
                )

        for piece in (0, 2, 1):
            for i in range(len(A_BANKS[piece])):
                wa_passes(piece, i, 0)
        for piece in (0, 1):
            tanh_piece(piece)

        wb_g = [sbuf("wb_g%d" % a, [P, PACK * H], BF16) for a in range(PASSES)]
        wb_w = [sbuf("wb_w%d" % a, [P, H], U32) for a in range(PASSES)]
        wb_s = [sbuf("wb_s%d" % a, [P, H], U8) for a in range(PASSES)]

        def round_wb(a, t0, t1, copy=nc.vector.tensor_copy, m0=0, m1=P):
            dealt = wb_g[a][:].rearrange("p (t m j) -> p m j t", t=PACK, j=PACK)
            rows = wb_raw[a][:].rearrange("p j (m t) -> p m j t", t=PACK)
            copy(out=dealt[:, m0:m1, :, t0:t1], in_=rows[:, m0:m1, :, t0:t1])

        def quantize_wb(a, t0, t1):
            cols = slice(P * t0, P * t1)
            nc.vector.quantize_mx(
                out=wb_w[a][:, cols].bitcast(FP8X4), scales=wb_s[a][:, cols],
                in_=wb_g[a][:, K_PASS * t0 : K_PASS * t1],
            )

        exp_b = [sbuf("exp_b%d" % half, [P, PACK, COLS], F32) for half in range(HALVES)]
        h_sb = [sbuf("h_sb%d" % half, [P, PACK, COLS], F32) for half in range(HALVES)]
        h_w = [sbuf("h_w%d" % half, [P, COLS], U32) for half in range(HALVES)]
        h_s = sbuf("h_s", [P, S], U8)
        h_rows = out_1.rearrange("(p t) j -> p t j", t=PACK)

        def interleave(copy, dst, src):
            copy(
                out=dst.rearrange("p (c i t) -> p c t i", i=4, t=PACK),
                in_=src.rearrange("p t (c i) -> p c t i", i=4),
            )

        wh_g = sbuf("wh_g", [P, PACK * N], BF16)
        wh_w = sbuf("wh_w", [P, N], U32)
        wh_s = sbuf("wh_s", [P, N], U8)

        def round_wh(copy, c0, c1):
            interleave(copy, wh_g[:, PACK * c0 : PACK * c1], wh_raw[:, :, c0:c1])

        def quantize_wh(c0, c1):
            nc.vector.quantize_mx(
                out=wh_w[:, c0:c1].bitcast(FP8X4), scales=wh_s[:, c0:c1], in_=wh_g[:, PACK * c0 : PACK * c1]
            )

        for step in (round_wb, quantize_wb):
            step(0, 0, 2)
            step(0, 2, PACK)
        round_wb(1, 2, PACK, nc.scalar.copy, m0=WB_SPLIT)
        tanh_piece(2)
        round_wb(1, 0, 2)
        round_wb(1, 2, PACK, m1=WB_SPLIT)
        quantize_wb(1, 0, 2)
        quantize_wb(1, 2, PACK)

        b_acc = {}

        def wb_pass(i, a):
            half, t = tiles[i]
            if a == 0:
                b_acc[i] = bank(i)
            words = wb_w[a][:, tile_cols(t)].bitcast(FP8X4)
            times_v(b_acc[i], words, wb_s[a][:, tile_cols(t)], a, half, a == 0, a == PASSES - 1)

        for i in range(EARLY_B):
            wb_pass(i, 0)
        for i, (half, t) in enumerate(tiles):
            for a in range(1 if i < EARLY_B else 0, PASSES):
                wb_pass(i, a)
            nc.scalar.activation(out=exp_b[half][:, t, :], in_=b_acc[i][:], func=ACT.Exp)

        wh_pieces = ((0, 2 * P), (2 * P, N))
        for c0, c1 in wh_pieces:
            round_wh(nc.vector.tensor_copy, c0, c1)
        for c0, c1 in wh_pieces:
            quantize_wh(c0, c1)

        h_g = [sbuf("h_g%d" % half, [P, PACK * COLS], BF16) for half in range(HALVES)]

        def wx_passes(acc, n, half, closes):
            for a in range(PASSES):
                words = wx_w[:, a, tile_cols(n)].bitcast(FP8X4)
                times_v(acc, words, wx_s[4 + 4 * a : P, tile_cols(n)], a, half, a == 0, closes and a == PASSES - 1)

        both_acc, e_acc, weighted = {}, {}, {}

        def e_passes(half, n):
            e_acc[half, n] = bank(E_BANKS[half][n])
            wx_passes(e_acc[half, n], n, half, True)

        for half in range(HALVES):
            for n in range(N_TILES):
                both_acc[half, n] = bank(BOTH_BANKS[half][n])
                wx_passes(both_acc[half, n], n, half, False)
        e_passes(0, 1)

        for half, t in tiles:
            nc.vector.scalar_tensor_tensor(
                out=h_sb[half][:, t, :], in0=tanh_a[half][:, t, :], scalar=gain_sb[:, t : t + 1],
                in1=exp_b[half][:, t, :], op0=ALU.mult, op1=ALU.mult,
            )
            if t % 2 == 1:
                nc.sync.dma_start(out=h_rows[:, t - 1 : t + 1, half_cols(half)], in_=h_sb[half][:, t - 1 : t + 1, :])

        for half in range(HALVES):
            pieces = ((nc.scalar.copy, 0, H_SPLIT), (nc.vector.tensor_copy, H_SPLIT, COLS))
            for copy, c0, c1 in pieces:
                interleave(copy, h_g[half][:, PACK * c0 : PACK * c1], h_sb[half][:, :, c0:c1])
            for copy, c0, c1 in pieces:
                nc.vector.quantize_mx(
                    out=h_w[half][:, c0:c1].bitcast(FP8X4), scales=h_s[:, half * COLS + c0 : half * COLS + c1],
                    in_=h_g[half][:, PACK * c0 : PACK * c1],
                )
            nc.sync.dma_start(
                out=out_2[0, :, half_cols(half), :].rearrange("p m t -> p (m t)").bitcast(I32),
                in_=h_w[half][:].bitcast(I32),
            )
        for half in range(HALVES):
            for n in range(N_TILES):
                nc.tensor.matmul_mx(
                    out=both_acc[half, n][:], lhsT=wh_w[:, tile_cols(n)].bitcast(FP8X4), lhsT_scale=wh_s[:, tile_cols(n)],
                    rhs=h_w[half][:].bitcast(FP8X4), rhs_scale=h_s[:, half_cols(half)],
                    start=False, stop=True,
                )
            if half == 0:
                e_passes(0, 2)
        for r in range(4):
            nc.sync.dma_start(out=out_3[0, r:SCALE_ROWS:4, :].bitcast(I32), in_=h_s[r:P:32, :].bitcast(I32))

        def weigh(half, n, engine, bracket, pieces=1):
            weighted[half, n] = sbuf("weighted%d%d" % (half, n), [P, COLS], F32)
            width = COLS // pieces
            for c0 in range(0, COLS, width):
                engine.tensor_tensor(
                    out=weighted[half, n][:, c0 : c0 + width], in0=bracket[:, c0 : c0 + width],
                    in1=conf_sb[:, n, half * COLS + c0 : half * COLS + c0 + width], op=ALU.mult,
                )

        def weigh_on_gpsimd(half, n):
            bracket = sbuf("bracket%d%d" % (half, n), [P, COLS], F32)
            nc.scalar.copy(out=bracket[:], in_=both_acc[half, n][:])
            weigh(half, n, nc.gpsimd, bracket)

        def finish(half, n, c0=0, c1=COLS):
            y = sbuf("y%d%d_%d" % (half, n, c0), [P, c1 - c0], F32)
            nc.vector.tensor_tensor(
                out=y[:], in0=weighted[half, n][:, c0:c1], in1=e_acc[half, n][:, c0:c1], op=ALU.subtract
            )
            nc.sync.dma_start(out=out_0[tile_cols(n), half * COLS + c0 : half * COLS + c1], in_=y[:])

        weigh_on_gpsimd(0, 0)
        e_passes(0, 0)
        for n in (1, 2):
            weigh(0, n, nc.vector, both_acc[0, n])
            finish(0, n)
        for n in (0, 1):
            weigh_on_gpsimd(1, n)
        finish(0, 0)
        for n in (0, 2, 1):
            e_passes(1, n)
        finish(1, 0)
        weigh(1, 2, nc.vector, both_acc[1, 2], pieces=2)
        for n, cuts in ((2, (0, 256, 512)), (1, (0, 256, 384, 512))):
            for c0, c1 in zip(cuts, cuts[1:]):
                finish(1, n, c0, c1)
